import numpy as np, ml_dtypes
CORES = [40,64,80,88,96,104,120,144]
N = 8
import mx_ref
BF = ml_dtypes.bfloat16
def gentries(a):
    return np.ascontiguousarray(a.reshape(8, 16, -1).transpose(0, 2, 1)).reshape(8, -1)
def gtable(e):
    e = np.asarray(e); return np.ascontiguousarray(e.reshape(8, -1, 16).transpose(0, 2, 1)).reshape(128, -1).astype(np.int32)
def gcols(t, e):
    v = np.concatenate([t.reshape(8, 16, -1, 4), np.zeros((8, 16, 1, 4), BF)], axis=2)
    return np.ascontiguousarray(np.stack([v[g][:, e[g]] for g in range(8)])).reshape(128, -1)
def tile(rs):
    return np.stack(rs, axis=2).reshape(128, -1).astype(BF)
def pick(q, e):
    c = np.concatenate([q[0].reshape(128, -1, 4), np.zeros((128, 1, 4), np.uint8)], axis=1); s = np.concatenate([q[1], np.ones((16, 1), np.uint8)], axis=1)
    return (np.ascontiguousarray(c[:, e].reshape(128, -1)), np.ascontiguousarray(s[:, e]))
def join(*qs):
    return (np.concatenate([q[0] for q in qs], axis=1), np.concatenate([q[1] for q in qs], axis=1))
def put(q, e, v):
    c, s = q[0].reshape(128, -1, 4).copy(), q[1].copy(); c[:, e] = v[0].reshape(128, -1, 4); s[:, e] = v[1]
    return (c.reshape(128, -1), s)
def pk(c, s):
    return (np.ascontiguousarray(c), mx_ref.live(s))
def emit(q):
    return q[0], q[1]
def packed(v, rng):
    q = [mx_ref.quantize(np.ascontiguousarray(v[r])) for r in range(N)]
    return np.stack([a for a, b in q]), np.stack([mx_ref.plane(b, rng) for a, b in q])
def values_of_codes():
    e, c = np.zeros((128, 128, 4), np.float32), np.zeros((128, 2, 4), np.uint8)
    e[np.arange(128), np.arange(128), 0] = 1
    c[:127, :, 0] = np.arange(256).reshape(2, 128).T[:127]
    return mx_ref.matmul(mx_ref.quantize(e.reshape(128, 512).astype(BF)), (c.reshape(128, 8), np.full((16, 2), 127, np.uint8))).T.reshape(-1).astype(np.float64)
CODE_VALUE, SCALE_VALUE = values_of_codes(), 2.0 ** (np.arange(256) - 127.0)
def decode(q):
    return (CODE_VALUE[q[0]].reshape(16, 8, -1, 4) * SCALE_VALUE[q[1]][:, None, :, None] + 0.0).reshape(128, -1).astype(np.float32)
def f(rng, *shape):
    return mx_ref.flush((rng.standard_normal(shape, dtype=np.float32) * np.exp2(rng.integers(-2, 3, shape[:-1] + (1,)))).astype(BF))
def wide(rng, *shape, cols=0):
    v = rng.standard_normal(shape, dtype=np.float32) * np.exp2(rng.integers(-12, 13, shape)).astype(np.float32)
    if cols: v *= np.repeat(np.exp2(rng.integers(-cols, cols + 1, shape[:-2] + (1, shape[-1] // 4))) * (rng.random(shape[:-2] + (1, shape[-1] // 4)) > 0.0625), 4, axis=-1).astype(np.float32)
    return mx_ref.flush(v.astype(BF))
C = 352
MASK = [2, 4, 1]
ALIKE = 1
def numbers_of(rng):
    return {"x": np.array(f(rng, N, 128, 4 * C)), "u": np.array(f(rng, N, 128, 512)), "v": np.array(f(rng, N, 128, 512))}
def stored(k):
    return {"se": np.stack([gtable(k[r].reshape(8, 2 * C)) for r in range(N)])}
def lists(rng):
    return stored(rng.permuted(np.tile(np.arange(C), (N, 8, 2, 1)), axis=3))
def layers(rng):
    return np.array(f(rng, N, 128, 2048)).reshape(N, 8, 16, 4, 8, 16, 4)
def weights(rng, w):
    c, s = packed(np.ascontiguousarray(w).reshape(N, 128, 2048), rng)
    return {"wc": c, "ws": s}
def setup_inputs(rng):
    return {**numbers_of(rng), **lists(rng), **weights(rng, layers(rng))}
def setup_inputs_ties(rng):
    d = numbers_of(rng)
    o = rng.permutation(N)
    k = rng.integers(-1, 2, (N, 8, 7, C)).astype(np.float32)
    k[o[1]] = 1
    x = d["x"].reshape(N, 8, 16, C, 4)
    x[:, :, :7, :, 0] = k.astype(BF)
    x[:, :, 8:] = 0
    a = np.exp2(rng.integers(-3, 4, (8, 1)).astype(np.float32))
    x[:, :, 8, :, 0] = (-3.0 * a).astype(BF)
    x[:, :, 10, :, 0] = (-0.0625 * a).astype(BF)
    x[:, :, 11, :, 0] = (0.28125 * a).astype(BF)
    c = np.ones(N, np.float32)
    c[o[0]] = 0
    c[o[2]] = -1
    u = d["u"].reshape(N, 128, 128, 4)
    for l in range(7):
        u[:, :, l::16] = 0
        for h in range(0, 128, 16): u[:, h + l, h + l, 0] = c.astype(BF)
    w = layers(rng)
    w[:, :, :, 0, :, :7] = 0
    w[:, :, :, :, :, 8:] = 0
    for g in range(8):
        w[:, g, 11, 0, g, 8, 0] = 112.0
        for b in range(4): w[:, g, 10, b, g, 9, 0] = -(1.125 + 0.25 * b) * 2.0 ** -5
    return {"x": x.reshape(N, 128, 4 * C), "u": u.reshape(N, 128, 512), "v": d["v"], **lists(rng), **weights(rng, w)}
def setup_inputs_near(rng):
    d = numbers_of(rng)
    k = np.where(((np.arange(N) & ALIKE) > 0) ^ (rng.random() < 0.5), 2.0 ** -30, 1.0)
    x = np.zeros((N, 8, 16, C, 4))
    s = rng.integers(-1, 2, (N, 8, 7, C)) * k[:, None, None, None]
    x[:, :, :7, :, 0] = 1.125 * s
    x[:, :, 8:15, :, 0] = -1.25 * s
    x[:, :, 15] = rng.choice([-1.0, 1.0], (N, 8, C, 4)) * (1.0 + 0.125 * rng.integers(0, 8, (N, 8, C, 4)) * (np.arange(4) > 1)) * 2.0 ** -30
    x[:, :, 15, :, 1] = 2.0 ** -30
    x[:, :, 7, :, 0] = 2.0 ** -30
    for r in range(N):
        at = [0, C - 1, int(rng.integers(C)), int(rng.integers(C))]
        for g, j in zip(rng.permutation(8)[:4], at): x[r, g, int(rng.integers(7)), j, 0] = 2.0 ** 30 * rng.choice([-1.0, 1.0])
    u = d["u"].reshape(N, 128, 128, 4)
    w = np.zeros((N, 8, 16, 4, 8, 16, 4), np.float32)
    for g in range(8):
        w[:, g, 15, 1, g, 7, 0] = 32.0
        w[:, g, 15, 1, g, 15, 1] = 32.0
        w[:, g, 15, 2:, g, 15, 2:] = rng.choice([-1.0, 1.0], (N, 2, 2)) * (8.0 + rng.integers(0, 8, (N, 2, 2)))
    for l in range(7):
        u[:, :, l::16] = 0
        for g in range(8):
            h = 16 * g
            u[:, h + l, h + l, 0] = (1.125 * k).astype(np.float32).astype(BF)
            u[:, h + 8 + l, h + l, 0] = k.astype(np.float32).astype(BF)
            w[:, g, 15, 0, g, l, 0] = rng.choice([-1.0, 1.0], N) * 2.0 ** -8
    return {"x": x.astype(np.float32).reshape(N, 128, 4 * C).astype(BF), "u": u.reshape(N, 128, 512), "v": d["v"], **lists(rng), **weights(rng, w.astype(BF))}
def setup_inputs_odd(rng):
    d = numbers_of(rng)
    x = (1.0 + (2 * rng.integers(0, 64, (N, 8, 16, C, 4)) + 1) * 2.0 ** -7) * np.exp2(-rng.integers(0, 7, (N, 8, 16, C, 4)).astype(np.float64)) * rng.choice([-1.0, 1.0], (N, 8, 16, C, 4))
    n = 2 * rng.integers(4, 8, (N, 8, 7, C)) + 1
    c = rng.choice([-1.0, 1.0], (N, 8, 7, C)) * 2.0 ** -8
    x[:, :, 0, :, 0] = 1.96875 * 2.0 ** 8 * rng.choice([-1.0, 1.0], (N, 8, 1))
    x[:, :, 1:8, :, 0] = c * n
    x[:, :, 8:15, :, 0] = -8.0 * c
    x[:, :, 8:15, :, 1] = -c * (n - 8 + rng.choice([-0.5, 0.5], (N, 8, 7, C)))
    u = d["u"].reshape(N, 128, 128, 4)
    for l in range(7):
        u[:, :, l::16] = 0
        for h in range(0, 128, 16):
            u[:, h + 1 + l, h + l, 0] = 1.0
            u[:, h + 8 + l, h + l, :2] = 1.0
    w = layers(rng)
    w[:, :, :, 0, :, :15] = 0
    w[:, :, :, 1, :, 8:15] = 0
    w[:, :, 0, :, :, :, 0] = 0
    return {"x": x.astype(np.float32).reshape(N, 128, 4 * C).astype(BF), "u": u.reshape(N, 128, 512), "v": d["v"], **lists(rng), **weights(rng, w)}
def setup_inputs_ends(rng):
    d = numbers_of(rng)
    o = rng.permutation(N) % 4
    j = np.arange(C)
    s = rng.choice([-1.0, 1.0], (N, 128, C, 4))
    s[o == 0] = -1
    s[o == 1] = (1.0 - j % 2 * 2.0)[:, None]
    x = s * (0.83 + 0.02 * rng.random((N, 128, C, 4))) * 2.0 ** 30
    x[o == 3] = -(1.0 + 0.125 * rng.integers(0, 8, (N, 128, C, 4))[o == 3]) * 2.0 ** -30
    size = np.where(o == 3, 2.0 ** -30, 2.0 ** 30)
    a = rng.permuted(np.tile(np.arange(8) % 2 * 2.0 - 1.0, (N, 7, 1)), axis=2).transpose(0, 2, 1) * size[:, None, None]
    for r in range(N): a[r, rng.permutation(8)[:2]] = 0
    u = d["u"].reshape(N, 128, 8, 16, 4)
    u[:, :, :, :7] = a.astype(np.float32).astype(BF)[:, None, :, :, None]
    v = rng.choice([-1.0, 1.0], (N, 128, 512)) * np.where(o % 2 == 0, 2.0 ** 30, 2.0 ** -30)[:, None, None]
    t = np.stack([j, (j + 2) % C, C - 1 - j, (j + 1) % C])
    k = rng.integers(0, 2, (N, 8, 2)) + 2 * (rng.permutation(8) < 4)[:, None]
    w = np.zeros((N, 128, 4, 128, 4), np.float32)
    i = np.arange(128)
    for b in range(4): w[:, i, b, i, b] = np.where(o == 3, 32.0, -1.0)[:, None]
    return {"x": x.astype(np.float32).reshape(N, 128, 4 * C).astype(BF), "u": u.reshape(N, 128, 512), "v": v.astype(np.float32).astype(BF), **stored(t[k]), **weights(rng, w.astype(BF))}
def setup_inputs_spread(rng):
    d = setup_inputs(rng)
    d["x"] = wide(rng, N, 128, 4 * C, cols=6)
    return d
def check_inputs(d):
    b = []
    for k in ("x", "u", "v"):
        a = np.abs(d[k].astype(np.float32))
        if not (np.isfinite(a).all() and ((a == 0) | (a >= 2.0 ** -30) & (a <= 2.0 ** 30)).all()): b.append("a value of " + k)
    none, least, most = [emit(mx_ref.quantize(np.full((128, 16), k, np.float32).astype(BF)))[1][0, 0] for k in (0.0, 2.0 ** -8, 2.0 ** 8)]
    for r in range(N):
        if not (np.sort(gentries(d["se"][r]).reshape(8, 2, C), axis=2) == np.arange(C)).all(): b.append("se: a list that is no permutation")
        if ((d["wc"][r] == 0x7F) | (d["wc"][r] == 0xFF)).any(): b.append("wc: a code that is no number")
        s = mx_ref.live(d["ws"][r])
        if ((s != none) & ((s < least) | (s > most))).any(): b.append("ws: a scale out of range")
    return b
def reference(x, u, v, se, wc, ws):
    qu = [mx_ref.quantize(u[r]) for r in range(N)]
    lay = [pk(wc[r], ws[r]) for r in range(N)]
    sec = [gentries(se[r]).reshape(8, 2, C) for r in range(N)]
    now = [x[r] for r in range(N)]
    g = np.arange(8)[:, None]
    for m in MASK:
        new, out = [], []
        for r in range(N):
            p = r ^ m
            bit = (mx_ref.matmul(qu[r], mx_ref.quantize(now[r])).reshape(8, 16, C)[:, :7] > 0).astype(np.int64)
            i = np.tile(np.arange(C), (8, 1))
            k = i
            for l in range(6):
                b = bit[g, l, i]
                i, k = sec[r][g, b, i], sec[p][g, 1 - b, k]
            end = bit[g, 6, k]
            turn = np.arange(C) ^ end ^ end[:, np.arange(C) ^ 1]
            new.append(np.stack([sec[p][g, 1 - b, turn[g, sec[r][:, b]]] for b in range(2)], axis=1))
            z = mx_ref.quantize(((gcols(now[r], i).astype(np.float32) + gcols(now[r], k).astype(np.float32)) * np.float32(0.5)).astype(BF))
            out.append(mx_ref.quantize(tile([mx_ref.matmul(pick(lay[r], np.arange(128 * b, 128 * b + 128)), z) * np.float32(0.03125) for b in range(4)])))
        now = [(now[r].astype(np.float32) + gcols(decode(out[r ^ m]).astype(BF), new[r][:, 0]).astype(np.float32)).astype(BF) for r in range(N)]
        sec = new
    y, so = np.zeros((N, 128, C), np.float32), np.zeros((N, 8, 2 * C), np.float32)
    oc, osc = np.zeros((N, 128, 4 * C), np.uint8), np.zeros((N, 16, C), np.uint8)
    for r in range(N):
        q = mx_ref.quantize(now[r])
        y[r] = mx_ref.matmul(mx_ref.quantize(v[r]), q)
        so[r] = sec[r].reshape(8, 2 * C)
        oc[r], osc[r] = emit(q)
    return {"y": y, "so": so, "oc": oc, "osc": osc}

@@ -1,0 +1,461 @@
+from concourse.bass import DstId, RemoteDMATransfer
+from concourse.mybir import dt, AluOpType as OP, ActivationFunctionType as AF
+
+C = 352
+MASK = [2, 4, 1]
+HALF = [(0, 192), (192, 160)]
+BF, F32, I32, U16, U8, E4 = "bfloat16", "float32", "int32", "uint16", "uint8", "float8_e4m3fn_x4"
+SCRATCH = {
+    "sei": ("sbuf", [128, 44], I32), "ub": ("sbuf", [128, 512], BF), "vb": ("sbuf", [128, 512], BF),
+    "wq": ("sbuf", [128, 512], E4), "wp": ("sbuf", [128, 512], U8),
+    "uq": ("sbuf", [128, 128], E4), "us": ("sbuf", [128, 128], U8), "vq": ("sbuf", [128, 128], E4), "vs": ("sbuf", [128, 128], U8),
+    "u6q": ("sbuf", [128, 128], E4), "u6s": ("sbuf", [128, 128], U8),
+    "pc": ("sbuf", [128, 8], I32), "ci": ("sbuf", [128, 8], I32), "cf": ("sbuf", [128, 8], F32), "cg": ("sbuf", [128, 8], F32),
+    "par": ("sbuf", [128, 384], F32), "mk1": ("sbuf", [128, 384], F32), "mk2": ("sbuf", [128, 384], F32),
+    "j16": ("sbuf", [128, C], F32), "w6": ("sbuf", [128, 704], F32), "m16": ("sbuf", [128, 704], BF), "r16": ("sbuf", [128, 704], BF),
+    "clf": ("sbuf", [128, 22], F32), "cl": ("sbuf", [128, 22], I32), "lpf": ("sbuf", [128, 44], F32), "lph": ("sbuf", [128, 44], U16),
+    "u6f": ("sbuf", [128, 8], F32), "u6l": ("sbuf", [128, 8], U16),
+    "one": ("sbuf", [128, 512], BF), "eb": ("sbuf", [128, 2048], BF), "eq": ("sbuf", [128, 512], E4), "es": ("sbuf", [128, 512], U8),
+    "xq": ("sbuf", [128, 384], E4), "xs": ("sbuf", [128, 384], U8), "xh": ("sbuf", [128, 1408], BF), "b6": ("sbuf", [128, C], BF),
+    "kk": ("sbuf", [128, 736], BF), "tt": ("sbuf", [128, 736], BF), "fm": ("sbuf", [128, 264], F32), "fb": ("sbuf", [128, 264], F32),
+    "fo": ("sbuf", [128, 264], F32), "fl": ("sbuf", [128, 132], U16), "sd": ("sbuf", [128, 22], F32),
+    "wv0": ("sbuf", [128, 704], F32), "wv1": ("sbuf", [128, 704], F32),
+    "wm": ("sbuf", [128, C], F32), "wsn": ("sbuf", [128, C], F32), "vi": ("sbuf", [128, 22], I32), "vk": ("sbuf", [128, 88], I32),
+    "il": ("sbuf", [128, 22], U16),
+    "wf": ("sbuf", [128, 704], BF), "pl": ("sbuf", [128, 44], BF), "ll": ("sbuf", [128, 88], U16), "pw": ("sbuf", [128, 704], BF),
+    "s2": ("sbuf", [128, 2048], BF), "km": ("sbuf", [128, C], BF), "ksn": ("sbuf", [128, C], BF),
+    "ki": ("sbuf", [128, 22], I32), "k1": ("sbuf", [128, 22], U16), "k2": ("sbuf", [128, 22], U16), "k3": ("sbuf", [128, 22], U16),
+    "k6": ("sbuf", [128, 22], U16),
+    "sn": ("sbuf", [128, 44], U16), "tf": ("sbuf", [128, 44], F32), "tg": ("sbuf", [128, 44], F32), "tl": ("sbuf", [128, 44], U16),
+    "en": ("sbuf", [128, C], BF), "dd": ("sbuf", [128, C], BF), "tm": ("sbuf", [128, 704], BF), "ts": ("sbuf", [128, 704], BF),
+    "tx": ("sbuf", [128, 22], U16), "tw": ("sbuf", [128, 704], F32),
+    "gi": ("sbuf", [128, 1408], BF), "z": ("sbuf", [128, 1408], BF), "zq": ("sbuf", [128, C], E4), "zs": ("sbuf", [128, C], U8),
+    "hb": ("sbuf", [128, 1408], BF), "dw": ("sbuf", [128, 1408], BF), "yb": ("sbuf", [128, C], F32),
+    "pa": ("psum", [128, 2048], F32), "pb": ("psum", [128, 2048], F32),
+}
+for _r in range(4):
+    SCRATCH["xp%d" % _r] = ("sbuf", [128, 1536], BF)
+for _r in range(3):
+    SCRATCH["sl%d" % _r] = ("sbuf", [128, 44], BF)
+    SCRATCH["lh%d" % _r] = ("sbuf", [128, 44], BF)
+    SCRATCH["ld%d" % _r] = ("dram", [128, 44], BF)
+    SCRATCH["hq%d" % _r] = ("sbuf", [128, C], E4)
+    SCRATCH["hs%d" % _r] = ("sbuf", [128, C], U8)
+    SCRATCH["fq%d" % _r] = ("sbuf", [128, 96], E4)
+    SCRATCH["fs%d" % _r] = ("sbuf", [128, 96], U8)
+    SCRATCH["dq%d" % _r] = ("sbuf", [128, C], E4)
+    SCRATCH["ds%d" % _r] = ("sbuf", [128, C], U8)
+SEMAPHORES = ["sv", "sa", "sp", "sg", "ls"] + ["d_" + n for n in ("se", "x", "x2", "u", "w", "wp", "v", "y", "oc", "so")]
+for _r in range(3):
+    SEMAPHORES += [n + str(_r) for n in ("hl", "hc", "hp", "la", "ca", "cb", "rp")]
+
+
+def route(topo, core, dst):
+    ok = [h for h in topo.cores_of(core) if h != core and topo.may_write(h, dst)]
+    near = [h for h in ok if topo.die(h) == topo.die(core)]
+    far = [h for h in ok if topo.die(h) != topo.die(core)]
+    return [near[0], far[0], near[1], far[1]]
+
+
+def chunk(i):
+    a, n = HALF[i // 2]
+    return a + n // 2 * (i % 2), n // 2
+
+
+def bits(e):
+    return sum(1 << i for i in e)
+
+
+def hand_on(g, core, T, topo):
+    mine = [c for c in T.cores if c in topo.cores_of(core)]
+    sent = 0
+    for r in range(3):
+        for c in mine:
+            dst = T.cores[T.rank_of(c) ^ MASK[r]]
+            hs = route(topo, c, dst)
+            if core not in hs:
+                continue
+            i = hs.index(core)
+            rid, pid = topo.addr(dst, core)
+            e = topo.engines(core, dst)
+            n_in = len(topo.engines(c, core)) // 2
+            if i == 0:
+                g.wait_ge(T.sem["hl%d" % r], n_in)
+                g.remote_dma(T["ld%d" % r][:, :], T["lh%d" % r][:, :], T.sem["la%d" % r], T.sem.ls, pid, rid, bits(e))
+                sent += len(e)
+            arr = T.sem[("ca%d" if i < 2 else "cb%d") % r]
+            a, n = chunk(i)
+            g.wait_ge(T.sem["hc%d" % r], n_in)
+            g.remote_dma(T["dq%d" % r][:, a:a + n].bitcast(dt.uint8), T["fq%d" % r][:, 0:n].bitcast(dt.uint8), arr, T.sem.ls, pid, rid, bits(e))
+            g.wait_ge(T.sem["hp%d" % r], n_in)
+            g.remote_dma(T["ds%d" % r][:, a:a + n], T["fs%d" % r][:, 0:n], arr, T.sem.ls, pid, rid, bits(e))
+            sent += 2 * len(e)
+    if sent:
+        g.wait_ge(T.sem.ls, sent)
+
+
+def rank_program(g, core, T, topo):
+    rank = T.rank_of(core)
+    if rank is None:
+        hand_on(g, core, T, topo)
+        return
+    eng = {"v": g.vector, "a": g.scalar, "p": g.tensor, "g": g, "s": g.sync}
+    sem_of = {"v": "sv", "a": "sa", "p": "sp", "g": "sg"}
+    total, seen = {}, {}
+    last, readers = {}, {}
+
+    def need(q, r, w):
+        d = {}
+        for k in r:
+            t = last.get(k)
+            if t is not None:
+                d[t[0]] = max(d.get(t[0], 0), t[1])
+        for k in w:
+            for t in readers.get(k, []) + ([last[k]] if k in last else []):
+                if t[2] != q or t[0][0:2] == "d_":
+                    d[t[0]] = max(d.get(t[0], 0), t[1])
+        for s in d:
+            if seen.get((q, s), 0) < d[s]:
+                eng[q].wait_ge(T.sem[s], d[s])
+                seen[(q, s)] = d[s]
+
+    def mark(t, r, w):
+        for k in r:
+            readers[k] = [x for x in readers.get(k, []) if x[0] != t[0]] + [t]
+        for k in w:
+            last[k] = t
+            readers[k] = []
+
+    def op(q, r, w, f, *args, **kw):
+        r, w = r.split(), w.split()
+        need(q, r, w)
+        s = sem_of[q]
+        f(*args, **kw).then_inc(T.sem[s], 1)
+        total[s] = total.get(s, 0) + 1
+        mark((s, total[s], q), r, w)
+
+    def dma(q, sem, r, w, out, in_):
+        r, w = r.split(), w.split()
+        need(q, r, w)
+        eng[q].dma_start(out, in_).then_inc(T.sem[sem], 16)
+        total[sem] = total.get(sem, 0) + 16
+        mark((sem, total[sem], q), r, w)
+
+    V, A, P = g.vector, g.scalar, g.tensor
+
+    def ts(r, w, out, in0, s1, s2, o0, o1=None):
+        if o1 is None:
+            op("v", r, w, V.tensor_scalar, out, in0, s1, s2, o0)
+        else:
+            op("v", r, w, V.tensor_scalar, out, in0, s1, s2, o0, o1)
+
+    def tten(r, w, out, a, b, o):
+        op("v", r, w, V.tensor_tensor, out, a, b, o)
+
+    def cp(r, w, out, in_):
+        op("v", r, w, V.tensor_copy, out, in_)
+
+    def scan(r, w, out, d0, d1):
+        op("v", r, w, V.tensor_tensor_scan, out, d0, d1, 0.0, OP.mult, OP.add)
+
+    def act(r, w, out, in_, func=AF.Copy, **kw):
+        op("a", r, w, A.activation, out, in_, func, **kw)
+
+    def mm(r, w, out, wq, wsc, xq, xsc):
+        op("p", r, w, P.matmul_mx, out, wq, wsc, xq, xsc, True, True)
+
+    def arrived(key, sem, n):
+        total[sem] = n
+        last[key] = (sem, n, "r")
+        readers[key] = []
+
+    dma("s", "d_se", "", "sei", T.sei[:, :], T.se[:, :])
+    dma("s", "d_x", "", "xp00", T.xp0[:, 64:768], T.x[:, 0:704])
+    dma("a", "d_u", "", "ub", T.ub[:, :], T.u[:, :])
+    dma("a", "d_x2", "", "xp01", T.xp0[:, 768:1472], T.x[:, 704:1408])
+
+    def iota(k, out, pattern, base, cm):
+        op("g", "", k, g.iota, out, pattern, base, cm, allow_small_or_imprecise_dtypes=True)
+
+    op("g", "", "pc", g.iota, T.pc[:, 0:1], [[0, 1]], 0, 1)
+    iota("u6f", T.u6f[:, :], [[16, 8]], 6, 0)
+    iota("par", T.par[:, :], [[0, 12], [1, 2], [0, 16]], 0, 0)
+    iota("j16", T.j16[:, :], [[0, 22], [1, 16]], 0, 0)
+    for r in range(4):
+        op("v", "", "pad%d" % r, V.memset, T["xp%d" % r][:, 0:64], 0.0)
+        op("v", "", "pad%d" % r, V.memset, T["xp%d" % r][:, 1472:1536], 0.0)
+    op("v", "", "one", V.memset, T.one[:, :], 1.0)
+    for e in range(4):
+        op("v", "", "s2g", V.memset, T.s2[:, 512 * e + C:512 * e + 512], 0.0)
+    op("v", "", "r16o", V.memset, T.r16[:, :], 1.0)
+    op("v", "r16o", "r16", V.memset, T.r16[:, 0:704:16], 0.0)
+    op("v", "", "fm", V.memset, T.fm[:, :], 0.0)
+    ci, cf, cg = T.ci, T.cf, T.cg
+    ts("pc", "ci", ci[:, 0:1], T.pc[:, 0:1], 15, None, OP.bitwise_and)
+    ts("pc", "ci", ci[:, 1:2], T.pc[:, 0:1], 4, 1, OP.logical_shift_right, OP.bitwise_and)
+    cp("u6f", "u6l", T.u6l[:, :], T.u6f[:, :])
+    cp("ci", "cf", cf[:, 0:2], ci[:, 0:2])
+    PR, PH = cf[:, 0:1], cf[:, 1:2]
+    ts("sei", "sl0", T.sl0[:, 0:22], T.sei[:, 22:44], -176.0, None, OP.add)
+    ts("sei", "sl0", T.sl0[:, 22:44], T.sei[:, 0:22], -176.0, None, OP.add)
+
+    sent = [0]
+
+    def partner(r):
+        return T.cores[rank ^ MASK[r]]
+
+    def send_list(r):
+        h = route(topo, core, partner(r))[0]
+        rid, pid = topo.addr(h, core)
+        e = topo.engines(core, h)
+        e = e[:len(e) // 2]
+        need("g", ["sl%d" % r], [])
+        g.remote_dma(T["lh%d" % r][:, :], T["sl%d" % r][:, :], T.sem["hl%d" % r], T.sem.ls, pid, rid, bits(e))
+        sent[0] += len(e)
+
+    def send_half(r, h):
+        hs = route(topo, core, partner(r))[2 * h:2 * h + 2]
+        for codes in (True, False):
+            tr = []
+            for i, k in enumerate(hs):
+                rid, pid = topo.addr(k, core)
+                e = topo.engines(core, k)
+                n = len(e) // 2
+                a, m = chunk(2 * h + i)
+                if codes:
+                    s, d = T["hq%d" % r][:, a:a + m].bitcast(dt.uint8), T["fq%d" % r][:, 0:m].bitcast(dt.uint8)
+                else:
+                    s, d = T["hs%d" % r][:, a:a + m], T["fs%d" % r][:, 0:m]
+                tr.append(RemoteDMATransfer(dst_ids=[DstId(rid=rid, pnc=pid)], dma_engine_mask=bits(e[n * i:n * i + n]),
+                                            remote_sem=T.sem[("hc%d" if codes else "hp%d") % r], src=s, dst=d))
+                sent[0] += n
+            need("g", ["hq%d%d" % (r, h)], [])
+            g.remote_dma_fused(tr, local_sem=T.sem.ls)
+
+    send_list(0)
+    iota("w6", T.w6[:, :], [[16384, 2], [1, C]], 0, 0)
+    iota("clf", T.clf[:, :], [[16, 22]], 0, 0)
+    iota("lpf", T.lpf[:, :], [[1, 44]], 0, 0)
+    for b in range(4):
+        op("g", "one", "eb", g.affine_select, T.eb[:, 512 * b:512 * b + 512], T.one[:, :], [[-1, 512]], OP.is_equal, 0.0, b, 4)
+    ts("par cf", "mk1", T.mk1[:, :], T.par[:, :], PH, 1e25, OP.is_equal, OP.mult)
+    ts("par cf", "mk2", T.mk2[:, :], T.par[:, :], PH, 1e25, OP.not_equal, OP.mult)
+    op("v", "ub", "uq", V.quantize_mx, T.uq[:, :], T.us[:, :], T.ub[:, :])
+    cp("uq u6l", "u6", T.u6q[:, :].bitcast(dt.uint32), T.uq[:, :].bitcast(dt.uint32).indirect(T.u6l[:, 0:8]))
+    act("uq u6l", "u6s", T.u6s[:, :], T.us[:, :].indirect(T.u6l[:, 0:8]))
+
+    def own_lists(r):
+        sl, k = T["sl%d" % r], "sl%d" % r
+        ts(k, "sn", T.sn[:, :], sl[:, :], 176.0, None, OP.add)
+        ts(k, "tf", T.tf[:, 0:22], sl[:, 0:22], 528.0, None, OP.add)
+        ts(k, "tf", T.tf[:, 22:44], sl[:, 22:44], 176.0, None, OP.add)
+        tten(k, "sd", T.sd[:, :], sl[:, 0:22], sl[:, 22:44], OP.subtract)
+        ts(k, "fb", T.fb[:, 1:44:2], sl[:, 22:44], 176.0, None, OP.add)
+        ts("sd", "fb", T.fb[:, 0:44:2], T.sd[:, :], 352.0, None, OP.add)
+
+    def repeat_lists():
+        act("fb", "fb", T.fb[:, 44:88], T.fb[:, 0:44])
+        act("fb", "fb", T.fb[:, 88:176], T.fb[:, 0:88])
+        act("fb", "fb", T.fb[:, 176:264], T.fb[:, 0:88])
+
+    def fetch(r):
+        arrived("ld%d" % r, "la%d" % r, len(topo.engines(route(topo, partner(r), core)[0], core)))
+        ld = T["ld%d" % r]
+        dma("s", "rp%d" % r, "ld%d" % r, "pl", T.pl[:, :], ld[:, :])
+        for i in range(16):
+            dma("s", "rp%d" % r, "ld%d" % r, "wf%d" % i, T.wf[i:128:16, :], ld[:, :])
+        for k in ["pl"] + ["wf%d" % i for i in range(16)]:
+            last[k] = ("rp%d" % r, total["rp%d" % r], "s")
+
+    WF = " ".join("wf%d" % i for i in range(16))
+
+    def choose():
+        for e in range(2):
+            ts("pl", "ll", T.ll[:, 44 * e:44 * e + 44], T.pl[:, :], 176.0 + 352.0 * e, None, OP.add)
+
+    def spread():
+        act(WF + " lph", "pw", T.pw[:, :], T.wf[:, :].indirect(T.lph[:, :]))
+
+    def table(e, q):
+        o, a = T.s2[:, 512 * e:512 * e + C], T.pw[:, :].indirect(T.ll[:, 22 * e:22 * e + 22])
+        if q == "a":
+            act("pw ll", "s2%d" % e, o, a)
+        else:
+            cp("pw ll", "s2%d" % e, o, a)
+
+    S2 = "s20 s21 s22 s23 s2g "
+
+    def bank(h, b):
+        n = HALF[h][1]
+        return ("pb%d" if h else "pa%d") % b, (T.pb if h else T.pa)[:, 512 * b:512 * b + n]
+
+    def plane(t, b):
+        return t[:, C * b:C * b + C]
+
+    def qx(r, h):
+        op("v", "xp%d0 xp%d1 pad%d" % (r, r, r), "xq%d" % h, V.quantize_mx, T.xq[:, 192 * h:192 * h + 192], T.xs[:, 192 * h:192 * h + 192],
+           T["xp%d" % r][:, 768 * h:768 * h + 768])
+
+    own_lists(0)
+    repeat_lists()
+    for r in range(3):
+        XP = T["xp%d" % r]
+        for h in range(2):
+            qx(r, h)
+            mm("uq xq%d" % h, "pb%d" % h, T.pb[:, 512 * h:512 * h + 192], T.uq[:, :], T.us[:, :], T.xq[:, 192 * h:192 * h + 192], T.xs[:, 192 * h:192 * h + 192])
+        mm("u6 u6s xq0 xq1", "pb2", T.pb[:, 1024:1024 + C], T.u6q[:, :], T.u6s[:, :], T.xq[:, 16:368], T.xs[:, 16:368])
+        for b in range(4):
+            act("xp%d0 xp%d1" % (r, r), "xh%d" % b, plane(T.xh, b), XP[:, 64 + b:1472:4], scale=0.5)
+        act("pb2", "b6", T.b6[:, :], T.pb[:, 1024:1024 + C], AF.Sign, bias=-2.0 ** -93)
+        for h in range(2):
+            tten("pb%d mk2" % h, "kk", T.kk[:, 352 + 192 * h:544 + 192 * h], T.pb[:, 512 * h:512 * h + 192], T.mk2[:, 192 * h:192 * h + 192], OP.is_gt)
+            a = 16 - 16 * h
+            tten("pb%d mk1" % h, "kk", T.kk[:, 176 * h:176 * h + 176], T.pb[:, 512 * h + a:512 * h + a + 176], T.mk1[:, 192 * h + a:192 * h + a + 176], OP.is_gt)
+        op("v", "kk", "tt", V.transpose, T.tt[:, :], T.kk[:, :])
+        for l in range(6):
+            tten("tt", "fm", T.fm[:, 44 * l + 1:44 * l + 44:2], T.tt[:, l:352:16], T.tt[:, 368 + l:720:16], OP.add)
+        scan("fm fb", "fo", T.fo[:, :], T.fm[:, :], T.fb[:, :])
+        cp("fo", "fl", T.fl[:, :], T.fo[:, 1:264:2])
+        if r == 0:
+            fetch(0)
+            dma("s", "d_w", "", "wq", T.wq[:, :].bitcast(dt.uint8), T.wc[:, :])
+            dma("s", "d_wp", "", "wp", T.wp[:, :], T.ws[:, :])
+            dma("s", "d_v", "", "vb", T.vb[:, :], T.v[:, :])
+        else:
+            choose()
+            spread()
+        W, key = T.w6, "w6"
+        for l in range(5, 0, -1):
+            N_, nk = (T.wv0, "wv0") if l % 2 else (T.wv1, "wv1")
+            off = T.fl[:, 22 * l:22 * l + 22]
+            rk = key if key == "w6" else key + "a " + key + "b"
+            cp(rk + " fl", nk + "a", N_[:, 0:352], W[:, :].indirect(off))
+            act(rk + " fl", nk + "b", N_[:, 352:704], W[:, :].indirect(off), AF.Identity, bias=float(512 << (l - 1)))
+            W, key = N_, nk
+            if r == 0 and l == 5:
+                ts("j16 cf", "m16", T.m16[:, 0:C], T.j16[:, :], PR, None, OP.is_equal)
+            if r == 0 and l == 4:
+                ts("clf cf", "cl", T.cl[:, :], T.clf[:, :], PR, None, OP.add)
+                ts("cf", "cg", cg[:, 0:1], PR, 44.0, None, OP.mult)
+                ts("lpf cg", "lph", T.lph[:, :], T.lpf[:, :], cg[:, 0:1], None, OP.add)
+        if r == 0:
+            choose()
+            spread()
+        for e in range(3):
+            table(e, "a")
+        tten(key + "a " + key + "b fl m16", "wm", T.wm[:, :], W[:, :].indirect(T.fl[:, 0:22]), T.m16[:, 0:352], OP.mult)
+        scan("wm r16", "wsn", T.wsn[:, :], T.r16[:, 0:352], T.wm[:, :])
+        cp("wsn", "vi", T.vi[:, :], T.wsn[:, 15:352:16])
+        ts("vi", "vk0", T.vk[:, 0:22], T.vi[:, :], 0x600, None, OP.bitwise_and)
+        ts("vi", "vk3", T.vk[:, 66:88], T.vi[:, :], 511, None, OP.bitwise_and)
+        tten("vk0 cl", "ki", T.ki[:, :], T.vk[:, 0:22], T.cl[:, :], OP.add)
+        cp("vk3", "il", T.il[:, :], T.vk[:, 66:88])
+        cp("ki", "k1", T.k1[:, :], T.ki[:, :])
+        ts("vi", "vk1", T.vk[:, 22:44], T.vi[:, :], 2, 0x600, OP.logical_shift_right, OP.bitwise_and)
+        ts("vi", "vk2", T.vk[:, 44:66], T.vi[:, :], 4, 0x600, OP.logical_shift_right, OP.bitwise_and)
+        table(3, "v")
+        if r == 0:
+            cp("m16", "m16", T.m16[:, 352:704], T.m16[:, 0:352])
+            op("v", "eb", "eq", V.quantize_mx, T.eq[:, :], T.es[:, :], T.eb[:, :])
+        for h in range(2):
+            a, n = HALF[h]
+            for b in range(4):
+                act("xh%d il" % b, "gi%d%d" % (h, b), T.gi[:, 4 * a + b:4 * a + 4 * n:4], plane(T.xh, b).indirect(T.il[:, a // 16:(a + n) // 16]))
+        for j in (1, 2, 3):
+            tten(S2 + "k%d m16" % j, "km", T.km[:, :], T.s2[:, :].indirect(T["k%d" % j][:, :]), T.m16[:, 0:352], OP.mult)
+            scan("km r16", "ksn", T.ksn[:, :], T.r16[:, 0:352], T.km[:, :])
+            if j < 3:
+                tten("ksn vk%d" % j, "ki", T.ki[:, :], T.ksn[:, 15:352:16], T.vk[:, 22 * j:22 * j + 22], OP.add)
+                ts("ki", "k%d" % (j + 1), T["k%d" % (j + 1)][:, :], T.ki[:, :], 176.0, None, OP.add)
+            else:
+                ts("ksn", "k6", T.k6[:, :], T.ksn[:, 15:352:16], 176.0, None, OP.add)
+
+        def mosaic(h):
+            a, n = HALF[h]
+            for b in range(4):
+                v = slice(4 * a + b, 4 * a + 4 * n, 4)
+                tten("xh%d k6 gi%d%d" % (b, h, b), "z%d" % h, T.z[:, v], plane(T.xh, b).indirect(T.k6[:, a // 16:(a + n) // 16]), T.gi[:, v], OP.add)
+            op("v", "z%d" % h, "zq%d" % h, V.quantize_mx, T.zq[:, a:a + n], T.zs[:, a:a + n], T.z[:, 4 * a:4 * a + 4 * n])
+            for b in range(4):
+                k, o = bank(h, b)
+                mm("wq wp zq%d" % h, k, o, T.wq[:, 128 * b:128 * b + 128], T.wp[:, 128 * b:128 * b + 128], T.zq[:, a:a + n], T.zs[:, a:a + n])
+
+        def hcast(h, b, q):
+            a, n = HALF[h]
+            k, i = bank(h, b)
+            o = T.hb[:, 4 * a + b:4 * a + 4 * n:4]
+            if q == "a":
+                act(k, "hb%d%d" % (h, b), o, i, scale=0.03125)
+            else:
+                ts(k, "hb%d%d" % (h, b), o, i, 0.03125, None, OP.mult)
+
+        def qh(h):
+            a, n = HALF[h]
+            op("v", " ".join("hb%d%d" % (h, b) for b in range(4)), "hq%d%d" % (r, h), V.quantize_mx, T["hq%d" % r][:, a:a + n],
+               T["hs%d" % r][:, a:a + n], T.hb[:, 4 * a:4 * a + 4 * n])
+            send_half(r, h)
+
+        mosaic(0)
+        for b in range(4):
+            hcast(0, b, "a")
+        act("b6 k6", "en", T.en[:, :], T.b6[:, :].indirect(T.k6[:, :]))
+        mosaic(1)
+        qh(0)
+        hcast(1, 0, "a")
+        hcast(1, 1, "v")
+        hcast(1, 2, "a")
+        hcast(1, 3, "v")
+        qh(1)
+        tten("en", "dd", T.dd[:, 0:352:2], T.en[:, 0:352:2], T.en[:, 1:352:2], OP.not_equal)
+        ts("dd", "dd", T.dd[:, 1:352:2], T.dd[:, 0:352:2], -1.0, None, OP.mult)
+        tten("dd sn m16", "tm", T.tm[:, :], T.dd[:, :].indirect(T.sn[:, :]), T.m16[:, :], OP.mult)
+        scan("tm r16", "ts", T.ts[:, :], T.r16[:, :], T.tm[:, :])
+        tten("ts tf", "tg", T.tg[:, :], T.ts[:, 15:704:16], T.tf[:, :], OP.add)
+        cp("tg", "tl", T.tl[:, :], T.tg[:, :])
+        lo = 0 if r < 2 else 352
+        tten("pw tl m16", "tm", T.tm[:, lo:704], T.pw[:, :].indirect(T.tl[:, lo // 16:44]), T.m16[:, lo:704], OP.mult)
+        scan("tm r16", "ts", T.ts[:, lo:704], T.r16[:, lo:704], T.tm[:, lo:704])
+        if r < 2:
+            cp("ts", "sl%d" % (r + 1), T["sl%d" % (r + 1)][:, :], T.ts[:, 15:704:16])
+            send_list(r + 1)
+            fetch(r + 1)
+        ts("ts", "tx", T.tx[:, :], T.ts[:, 367:704:16], 176.0, None, OP.add)
+        if r < 2:
+            own_lists(r + 1)
+        else:
+            op("v", "vb", "vq", V.quantize_mx, T.vq[:, :], T.vs[:, :], T.vb[:, :])
+        hp = route(topo, partner(r), core)
+        for h in range(2):
+            a, n = HALF[h]
+            arrived("dq%d%d" % (r, h), ("ca%d" if h == 0 else "cb%d") % r, sum(2 * len(topo.engines(k, core)) for k in hp[2 * h:2 * h + 2]))
+            for b in range(4):
+                k, ps = bank(h, b)
+                mm("eq dq%d%d" % (r, h), k, ps, T.eq[:, 128 * b:128 * b + 128], T.es[:, 128 * b:128 * b + 128],
+                   T["dq%d" % r][:, a:a + n], T["ds%d" % r][:, a:a + n])
+            for b in range(4):
+                k, ps = bank(h, b)
+                o = T.dw[:, C * b + a:C * b + a + n]
+                if h == 0 or b % 2 == 0:
+                    act(k, "dw%d%d" % (h, b), o, ps)
+                else:
+                    cp(k, "dw%d%d" % (h, b), o, ps)
+        if r < 2:
+            repeat_lists()
+        for b in range(4):
+            v = slice(64 + b, 1472, 4)
+            tten("tx xp%d0 xp%d1 dw0%d dw1%d" % (r, r, b, b), "xp%d0" % (r + 1), T["xp%d" % (r + 1)][:, v], plane(T.dw, b).indirect(T.tx[:, :]), XP[:, v], OP.add)
+
+    act("pw tl", "tw", T.tw[:, :], T.pw[:, :].indirect(T.tl[:, :]), AF.Identity, bias=176.0)
+    dma("s", "d_so", "tw", "so", T.so[:, 0:352], T.tw[0:128:16, 352:704])
+    dma("s", "d_so", "tw", "so2", T.so[:, 352:704], T.tw[0:128:16, 0:352])
+    qx(3, 0)
+    qx(3, 1)
+    dma("s", "d_oc", "xq0 xq1", "oc", T.oc[:, :], T.xq[:, 16:368].bitcast(dt.uint8))
+    for k in range(4):
+        dma("s", "d_oc", "xq0 xq1", "osc%d" % k, T.osc[4 * k:4 * k + 4, :], T.xs[32 * k:32 * k + 4, 16:368])
+    mm("vq xq0 xq1", "pa0", T.pa[:, 0:C], T.vq[:, :], T.vs[:, :], T.xq[:, 16:368], T.xs[:, 16:368])
+    cp("pa0", "yb", T.yb[:, :], T.pa[:, 0:C])
+    dma("a", "d_y", "yb", "y", T.y[:, :], T.yb[:, :])
+    total["ls"] = sent[0]
+    for s in total:
+        g.wait_ge(T.sem[s], total[s])

@@ -3,51 +3,59 @@ from concourse.mybir import dt, AluOpType as OP, ActivationFunctionType as AF
 
 C = 352
 MASK = [2, 4, 1]
-HALF = [(0, 192), (192, 160)]
+PART = [(0, 224), (224, 128)]
+XH = [(0, 192), (192, 160)]
+KM, BIG = 16384.0, 1048576.0
 BF, F32, I32, U16, U8, E4 = "bfloat16", "float32", "int32", "uint16", "uint8", "float8_e4m3fn_x4"
 SCRATCH = {
     "sei": ("sbuf", [128, 44], I32), "ub": ("sbuf", [128, 512], BF), "vb": ("sbuf", [128, 512], BF),
     "wq": ("sbuf", [128, 512], E4), "wp": ("sbuf", [128, 512], U8),
     "uq": ("sbuf", [128, 128], E4), "us": ("sbuf", [128, 128], U8), "vq": ("sbuf", [128, 128], E4), "vs": ("sbuf", [128, 128], U8),
-    "u6q": ("sbuf", [128, 128], E4), "u6s": ("sbuf", [128, 128], U8),
+    "urq": ("sbuf", [128, 256], E4), "urs": ("sbuf", [128, 256], U8),
     "pc": ("sbuf", [128, 8], I32), "ci": ("sbuf", [128, 8], I32), "cf": ("sbuf", [128, 8], F32), "cg": ("sbuf", [128, 8], F32),
-    "par": ("sbuf", [128, 384], F32), "mk1": ("sbuf", [128, 384], F32), "mk2": ("sbuf", [128, 384], F32),
-    "j16": ("sbuf", [128, C], F32), "w6": ("sbuf", [128, 704], F32), "m16": ("sbuf", [128, 704], BF), "r16": ("sbuf", [128, 704], BF),
-    "clf": ("sbuf", [128, 22], F32), "cl": ("sbuf", [128, 22], I32), "lpf": ("sbuf", [128, 44], F32), "lph": ("sbuf", [128, 44], U16),
-    "u6f": ("sbuf", [128, 8], F32), "u6l": ("sbuf", [128, 8], U16),
+    "j16": ("sbuf", [128, C], F32), "jj": ("sbuf", [128, C], F32), "cw": ("sbuf", [128, 704], F32), "cb": ("sbuf", [128, C], BF),
+    "m16": ("sbuf", [128, C], BF), "r16": ("sbuf", [128, C], BF), "mx": ("sbuf", [128, C], BF), "m8": ("sbuf", [128, 176], BF),
+    "cq": ("sbuf", [128, 24], F32), "cl": ("sbuf", [128, 24], F32), "ga": ("sbuf", [128, 10], I32), "gb": ("sbuf", [128, 10], F32),
+    "ge": ("sbuf", [128, 10], F32), "gl": ("sbuf", [128, 10], U16),
+    "urf": ("sbuf", [128, 16], F32), "url": ("sbuf", [128, 16], U16),
     "one": ("sbuf", [128, 512], BF), "eb": ("sbuf", [128, 2048], BF), "eq": ("sbuf", [128, 512], E4), "es": ("sbuf", [128, 512], U8),
-    "xq": ("sbuf", [128, 384], E4), "xs": ("sbuf", [128, 384], U8), "xh": ("sbuf", [128, 1408], BF), "b6": ("sbuf", [128, C], BF),
-    "kk": ("sbuf", [128, 736], BF), "tt": ("sbuf", [128, 736], BF), "fm": ("sbuf", [128, 264], F32), "fb": ("sbuf", [128, 264], F32),
-    "fo": ("sbuf", [128, 264], F32), "fl": ("sbuf", [128, 132], U16), "sd": ("sbuf", [128, 22], F32),
-    "wv0": ("sbuf", [128, 704], F32), "wv1": ("sbuf", [128, 704], F32),
-    "wm": ("sbuf", [128, C], F32), "wsn": ("sbuf", [128, C], F32), "vi": ("sbuf", [128, 22], I32), "vk": ("sbuf", [128, 88], I32),
-    "il": ("sbuf", [128, 22], U16),
-    "wf": ("sbuf", [128, 704], BF), "pl": ("sbuf", [128, 44], BF), "ll": ("sbuf", [128, 88], U16), "pw": ("sbuf", [128, 704], BF),
-    "s2": ("sbuf", [128, 2048], BF), "km": ("sbuf", [128, C], BF), "ksn": ("sbuf", [128, C], BF),
-    "ki": ("sbuf", [128, 22], I32), "k1": ("sbuf", [128, 22], U16), "k2": ("sbuf", [128, 22], U16), "k3": ("sbuf", [128, 22], U16),
-    "k6": ("sbuf", [128, 22], U16),
-    "sn": ("sbuf", [128, 44], U16), "tf": ("sbuf", [128, 44], F32), "tg": ("sbuf", [128, 44], F32), "tl": ("sbuf", [128, 44], U16),
-    "en": ("sbuf", [128, C], BF), "dd": ("sbuf", [128, C], BF), "tm": ("sbuf", [128, 704], BF), "ts": ("sbuf", [128, 704], BF),
-    "tx": ("sbuf", [128, 22], U16), "tw": ("sbuf", [128, 704], F32),
+    "xq": ("sbuf", [128, 384], E4), "xs": ("sbuf", [128, 384], U8), "xh": ("sbuf", [128, 1408], BF),
+    "b1": ("sbuf", [128, C], BF), "b6": ("sbuf", [128, C], BF),
+    "tt": ("sbuf", [128, 736], F32), "fm": ("sbuf", [128, 320], F32), "fb": ("sbuf", [128, 308], F32),
+    "fo": ("sbuf", [128, 308], F32), "fl": ("sbuf", [128, 132], U16), "sf": ("sbuf", [128, 44], F32),
+    "la": ("sbuf", [128, C], F32), "lb": ("sbuf", [128, C], F32), "lm": ("sbuf", [128, C], F32), "ln": ("sbuf", [128, C], F32),
+    "ha": ("sbuf", [128, 704], F32), "hc": ("sbuf", [128, 704], F32), "hd": ("sbuf", [128, C], F32), "hm": ("sbuf", [128, C], F32),
+    "hn": ("sbuf", [128, C], F32),
+    "i3": ("sbuf", [128, 22], U16), "i6": ("sbuf", [128, 22], U16), "vi": ("sbuf", [128, 22], I32), "vj": ("sbuf", [128, 22], I32),
+    "va": ("sbuf", [128, 88], I32),
+    "pw": ("sbuf", [128, 704], BF), "s2": ("sbuf", [128, 1408], BF), "km": ("sbuf", [128, C], BF), "ksn": ("sbuf", [128, C], BF),
+    "ki": ("sbuf", [128, 22], F32), "kb": ("sbuf", [128, 22], F32),
+    "k0": ("sbuf", [128, 22], U16), "k2": ("sbuf", [128, 22], U16), "k4": ("sbuf", [128, 22], U16), "k6": ("sbuf", [128, 22], U16),
+    "en": ("sbuf", [128, C], BF), "dd": ("sbuf", [128, 176], BF), "dn": ("sbuf", [128, 176], BF), "tf": ("sbuf", [128, 22], F32),
+    "tg": ("sbuf", [128, 22], F32), "tl": ("sbuf", [128, 22], U16), "uw": ("sbuf", [128, 704], BF), "t1": ("sbuf", [128, C], BF),
+    "tw": ("sbuf", [128, 704], F32),
     "gi": ("sbuf", [128, 1408], BF), "z": ("sbuf", [128, 1408], BF), "zq": ("sbuf", [128, C], E4), "zs": ("sbuf", [128, C], U8),
     "hb": ("sbuf", [128, 1408], BF), "dw": ("sbuf", [128, 1408], BF), "yb": ("sbuf", [128, C], F32),
     "pa": ("psum", [128, 2048], F32), "pb": ("psum", [128, 2048], F32),
 }
 for _r in range(4):
     SCRATCH["xp%d" % _r] = ("sbuf", [128, 1536], BF)
+    SCRATCH["sn%d" % _r] = ("sbuf", [128, 48], U16)
 for _r in range(3):
-    SCRATCH["sl%d" % _r] = ("sbuf", [128, 44], BF)
-    SCRATCH["lh%d" % _r] = ("sbuf", [128, 44], BF)
-    SCRATCH["ld%d" % _r] = ("dram", [128, 44], BF)
+    SCRATCH["lh%d" % _r] = ("sbuf", [128, 44], U16)
+    SCRATCH["pl%d" % _r] = ("sbuf", [128, 44], U16)
     SCRATCH["hq%d" % _r] = ("sbuf", [128, C], E4)
     SCRATCH["hs%d" % _r] = ("sbuf", [128, C], U8)
-    SCRATCH["fq%d" % _r] = ("sbuf", [128, 96], E4)
-    SCRATCH["fs%d" % _r] = ("sbuf", [128, 96], U8)
+    SCRATCH["fq%d" % _r] = ("sbuf", [128, 112], E4)
+    SCRATCH["fs%d" % _r] = ("sbuf", [128, 224], U8)
     SCRATCH["dq%d" % _r] = ("sbuf", [128, C], E4)
     SCRATCH["ds%d" % _r] = ("sbuf", [128, C], U8)
 SEMAPHORES = ["sv", "sa", "sp", "sg", "ls"] + ["d_" + n for n in ("se", "x", "x2", "u", "w", "wp", "v", "y", "oc", "so")]
 for _r in range(3):
-    SEMAPHORES += [n + str(_r) for n in ("hl", "hc", "hp", "la", "ca", "cb", "rp")]
+    SEMAPHORES += [n + str(_r) for n in ("hl", "hc", "hp", "la", "ca", "cb")]
+CODES = [(0, 1), (2, 3)]
+SCALES = [2, 0]
+LISTS = 3
 
 
 def route(topo, core, dst):
@@ -57,9 +65,9 @@ def route(topo, core, dst):
     return [near[0], far[0], near[1], far[1]]
 
 
-def chunk(i):
-    a, n = HALF[i // 2]
-    return a + n // 2 * (i % 2), n // 2
+def chunk(h, i):
+    a, n = PART[h]
+    return a + n // 2 * i, n // 2
 
 
 def bits(e):
@@ -78,18 +86,23 @@ def hand_on(g, core, T, topo):
             i = hs.index(core)
             rid, pid = topo.addr(dst, core)
             e = topo.engines(core, dst)
-            n_in = len(topo.engines(c, core)) // 2
-            if i == 0:
+            n_in = len(topo.engines(c, core))
+            if i == LISTS:
                 g.wait_ge(T.sem["hl%d" % r], n_in)
-                g.remote_dma(T["ld%d" % r][:, :], T["lh%d" % r][:, :], T.sem["la%d" % r], T.sem.ls, pid, rid, bits(e))
+                g.remote_dma(T["pl%d" % r][:, :], T["lh%d" % r][:, :], T.sem["la%d" % r], T.sem.ls, pid, rid, bits(e))
                 sent += len(e)
-            arr = T.sem[("ca%d" if i < 2 else "cb%d") % r]
-            a, n = chunk(i)
-            g.wait_ge(T.sem["hc%d" % r], n_in)
-            g.remote_dma(T["dq%d" % r][:, a:a + n].bitcast(dt.uint8), T["fq%d" % r][:, 0:n].bitcast(dt.uint8), arr, T.sem.ls, pid, rid, bits(e))
-            g.wait_ge(T.sem["hp%d" % r], n_in)
-            g.remote_dma(T["ds%d" % r][:, a:a + n], T["fs%d" % r][:, 0:n], arr, T.sem.ls, pid, rid, bits(e))
-            sent += 2 * len(e)
+            for h in range(2):
+                arr = T.sem[("ca%d", "cb%d")[h] % r]
+                if i in CODES[h]:
+                    a, n = chunk(h, CODES[h].index(i))
+                    g.wait_ge(T.sem["hc%d" % r], n_in // 2)
+                    g.remote_dma(T["dq%d" % r][:, a:a + n].bitcast(dt.uint8), T["fq%d" % r][:, 0:n].bitcast(dt.uint8), arr, T.sem.ls, pid, rid, bits(e))
+                    sent += len(e)
+                if i == SCALES[h]:
+                    a, n = PART[h]
+                    g.wait_ge(T.sem["hp%d" % r], n_in)
+                    g.remote_dma(T["ds%d" % r][:, a:a + n], T["fs%d" % r][:, 0:n], arr, T.sem.ls, pid, rid, bits(e))
+                    sent += len(e)
     if sent:
         g.wait_ge(T.sem.ls, sent)
 
@@ -128,6 +141,12 @@ def rank_program(g, core, T, topo):
 
     def op(q, r, w, f, *args, **kw):
         r, w = r.split(), w.split()
+        banks = [k for k in r if k[0:2] in ("pa", "pb")]
+        for k in banks:
+            for t in readers.get(k, []):
+                if t[2] != q and seen.get((q, t[0]), 0) < t[1]:
+                    eng[q].wait_ge(T.sem[t[0]], t[1])
+                    seen[(q, t[0])] = t[1]
         need(q, r, w)
         s = sem_of[q]
         f(*args, **kw).then_inc(T.sem[s], 1)
@@ -158,6 +177,9 @@ def rank_program(g, core, T, topo):
     def scan(r, w, out, d0, d1):
         op("v", r, w, V.tensor_tensor_scan, out, d0, d1, 0.0, OP.mult, OP.add)
 
+    def hold(r, w, out, d0, d1):
+        op("v", r, w, V.tensor_tensor_scan, out, d0, d1, 0.0, OP.add, OP.max)
+
     def act(r, w, out, in_, func=AF.Copy, **kw):
         op("a", r, w, A.activation, out, in_, func, **kw)
 
@@ -169,35 +191,48 @@ def rank_program(g, core, T, topo):
         last[key] = (sem, n, "r")
         readers[key] = []
 
-    dma("s", "d_se", "", "sei", T.sei[:, :], T.se[:, :])
-    dma("s", "d_x", "", "xp00", T.xp0[:, 64:768], T.x[:, 0:704])
-    dma("a", "d_u", "", "ub", T.ub[:, :], T.u[:, :])
-    dma("a", "d_x2", "", "xp01", T.xp0[:, 768:1472], T.x[:, 704:1408])
-
     def iota(k, out, pattern, base, cm):
         op("g", "", k, g.iota, out, pattern, base, cm, allow_small_or_imprecise_dtypes=True)
 
+    dma("s", "d_se", "", "sei", T.sei[:, :], T.se[:, :])
+    dma("a", "d_u", "", "ub", T.ub[:, :], T.u[:, :])
+    dma("s", "d_x", "", "xp00", T.xp0[:, 64:832], T.x[:, 0:768])
+    dma("a", "d_x2", "", "xp01", T.xp0[:, 832:1472], T.x[:, 768:1408])
     op("g", "", "pc", g.iota, T.pc[:, 0:1], [[0, 1]], 0, 1)
-    iota("u6f", T.u6f[:, :], [[16, 8]], 6, 0)
-    iota("par", T.par[:, :], [[0, 12], [1, 2], [0, 16]], 0, 0)
+    iota("urf", T.urf[:, :], [[5, 2], [16, 8]], 1, 0)
+    iota("cq", T.cq[:, :], [[16, 24]], 0, 0)
     iota("j16", T.j16[:, :], [[0, 22], [1, 16]], 0, 0)
-    for r in range(4):
+    iota("jj", T.jj[:, :], [[1, C]], 0, 0)
+    for r in range(3):
         op("v", "", "pad%d" % r, V.memset, T["xp%d" % r][:, 0:64], 0.0)
         op("v", "", "pad%d" % r, V.memset, T["xp%d" % r][:, 1472:1536], 0.0)
-    op("v", "", "one", V.memset, T.one[:, :], 1.0)
-    for e in range(4):
-        op("v", "", "s2g", V.memset, T.s2[:, 512 * e + C:512 * e + 512], 0.0)
-    op("v", "", "r16o", V.memset, T.r16[:, :], 1.0)
-    op("v", "r16o", "r16", V.memset, T.r16[:, 0:704:16], 0.0)
-    op("v", "", "fm", V.memset, T.fm[:, :], 0.0)
     ci, cf, cg = T.ci, T.cf, T.cg
     ts("pc", "ci", ci[:, 0:1], T.pc[:, 0:1], 15, None, OP.bitwise_and)
     ts("pc", "ci", ci[:, 1:2], T.pc[:, 0:1], 4, 1, OP.logical_shift_right, OP.bitwise_and)
-    cp("u6f", "u6l", T.u6l[:, :], T.u6f[:, :])
-    cp("ci", "cf", cf[:, 0:2], ci[:, 0:2])
-    PR, PH = cf[:, 0:1], cf[:, 1:2]
-    ts("sei", "sl0", T.sl0[:, 0:22], T.sei[:, 22:44], -176.0, None, OP.add)
-    ts("sei", "sl0", T.sl0[:, 22:44], T.sei[:, 0:22], -176.0, None, OP.add)
+    ts("pc", "ci", ci[:, 2:3], T.pc[:, 0:1], 1, None, OP.bitwise_and)
+    ts("pc", "ci", ci[:, 3:4], T.pc[:, 0:1], 14, None, OP.bitwise_and)
+    op("v", "", "fm", V.memset, T.fm[:, 0:320:2], 0.0)
+    op("v", "", "r16o", V.memset, T.r16[:, :], 1.0)
+    cp("ci", "cf", cf[:, 0:4], ci[:, 0:4])
+    cp("urf", "url", T.url[:, :], T.urf[:, :])
+    op("v", "r16o", "r16", V.memset, T.r16[:, 0:C:16], 0.0)
+    PR, PH, PP, PE = (cf[:, i:i + 1] for i in range(4))
+    ts("cf", "cg0", cg[:, 0:1], PH, PP, 368.0, OP.not_equal, OP.mult)
+    ts("cq cf", "cl", T.cl[:, :], T.cq[:, :], PR, None, OP.add)
+    ts("cf", "cg1", cg[:, 1:2], PR, KM / 32, -15 * KM / 32, OP.mult, OP.add)
+    ts("cf", "cg2", cg[:, 2:3], PR, KM, 176 - 15 * KM, OP.mult, OP.add)
+    ts("cl", "ga", T.ga[:, :], T.cl[:, 0:10], 1.0 / 22, -0.477, OP.mult, OP.add)
+    ts("cf", "cg3", cg[:, 3:4], PE, -2.0, 28.0, OP.mult, OP.add)
+    ts("cl cg0", "ge", T.ge[:, :], T.cl[:, 0:10], 16.0, cg[:, 0:1], OP.mult, OP.add)
+    ts("ga", "gb", T.gb[:, :], T.ga[:, :], -351.0, -1.0, OP.mult, OP.add)
+    ts("cf", "cg4", cg[:, 4:5], PP, -2.0, 1.0, OP.mult, OP.add)
+    ts("ga", "ga0", T.cq[:, 0:10], T.ga[:, :], 0.0, None, OP.is_equal)
+    tten("gb ge", "ge", T.ge[:, :], T.ge[:, :], T.gb[:, :], OP.add)
+    ts("cl", "fbc", T.fb[:, 1:44:2], T.cl[:, 0:22], 4.0, None, OP.mult)
+    tten("ge ga0", "ge", T.ge[:, :], T.ge[:, :], T.cq[:, 0:10], OP.add)
+    op("v", "", "fbc", V.memset, T.fb[:, 0:44:2], 2.0)
+    cp("ge", "gl", T.gl[:, :], T.ge[:, :])
+    cp("sei", "sn0", T.sn0[:, 0:44], T.sei[:, :])
 
     sent = [0]
 
@@ -205,183 +240,197 @@ def rank_program(g, core, T, topo):
         return T.cores[rank ^ MASK[r]]
 
     def send_list(r):
-        h = route(topo, core, partner(r))[0]
+        h = route(topo, core, partner(r))[LISTS]
         rid, pid = topo.addr(h, core)
         e = topo.engines(core, h)
-        e = e[:len(e) // 2]
-        need("g", ["sl%d" % r], [])
-        g.remote_dma(T["lh%d" % r][:, :], T["sl%d" % r][:, :], T.sem["hl%d" % r], T.sem.ls, pid, rid, bits(e))
+        need("g", ["sn%d" % r], [])
+        g.remote_dma(T["lh%d" % r][:, :], T["sn%d" % r][:, 0:44], T.sem["hl%d" % r], T.sem.ls, pid, rid, bits(e))
+        sent[0] += len(e)
+        arrived("pl%d" % r, "la%d" % r, len(topo.engines(route(topo, partner(r), core)[LISTS], core)))
+
+    def send_part(r, h):
+        hs = route(topo, core, partner(r))
+        tr = []
+        for i, k in enumerate(CODES[h]):
+            rid, pid = topo.addr(hs[k], core)
+            e = topo.engines(core, hs[k])
+            n = len(e) // 2
+            a, m = chunk(h, i)
+            tr.append(RemoteDMATransfer(dst_ids=[DstId(rid=rid, pnc=pid)], dma_engine_mask=bits(e[n * i:n * i + n]), remote_sem=T.sem["hc%d" % r],
+                                        src=T["hq%d" % r][:, a:a + m].bitcast(dt.uint8), dst=T["fq%d" % r][:, 0:m].bitcast(dt.uint8)))
+            sent[0] += n
+        need("g", ["hq%d%d" % (r, h)], [])
+        g.remote_dma_fused(tr, local_sem=T.sem.ls)
+        rid, pid = topo.addr(hs[SCALES[h]], core)
+        e = topo.engines(core, hs[SCALES[h]])
+        a, m = PART[h]
+        g.remote_dma(T["fs%d" % r][:, 0:m], T["hs%d" % r][:, a:a + m], T.sem["hp%d" % r], T.sem.ls, pid, rid, bits(e))
         sent[0] += len(e)
 
-    def send_half(r, h):
-        hs = route(topo, core, partner(r))[2 * h:2 * h + 2]
-        for codes in (True, False):
-            tr = []
-            for i, k in enumerate(hs):
-                rid, pid = topo.addr(k, core)
-                e = topo.engines(core, k)
-                n = len(e) // 2
-                a, m = chunk(2 * h + i)
-                if codes:
-                    s, d = T["hq%d" % r][:, a:a + m].bitcast(dt.uint8), T["fq%d" % r][:, 0:m].bitcast(dt.uint8)
-                else:
-                    s, d = T["hs%d" % r][:, a:a + m], T["fs%d" % r][:, 0:m]
-                tr.append(RemoteDMATransfer(dst_ids=[DstId(rid=rid, pnc=pid)], dma_engine_mask=bits(e[n * i:n * i + n]),
-                                            remote_sem=T.sem[("hc%d" if codes else "hp%d") % r], src=s, dst=d))
-                sent[0] += n
-            need("g", ["hq%d%d" % (r, h)], [])
-            g.remote_dma_fused(tr, local_sem=T.sem.ls)
-
     send_list(0)
-    iota("w6", T.w6[:, :], [[16384, 2], [1, C]], 0, 0)
-    iota("clf", T.clf[:, :], [[16, 22]], 0, 0)
-    iota("lpf", T.lpf[:, :], [[1, 44]], 0, 0)
-    for b in range(4):
-        op("g", "one", "eb", g.affine_select, T.eb[:, 512 * b:512 * b + 512], T.one[:, :], [[-1, 512]], OP.is_equal, 0.0, b, 4)
-    ts("par cf", "mk1", T.mk1[:, :], T.par[:, :], PH, 1e25, OP.is_equal, OP.mult)
-    ts("par cf", "mk2", T.mk2[:, :], T.par[:, :], PH, 1e25, OP.not_equal, OP.mult)
     op("v", "ub", "uq", V.quantize_mx, T.uq[:, :], T.us[:, :], T.ub[:, :])
-    cp("uq u6l", "u6", T.u6q[:, :].bitcast(dt.uint32), T.uq[:, :].bitcast(dt.uint32).indirect(T.u6l[:, 0:8]))
-    act("uq u6l", "u6s", T.u6s[:, :], T.us[:, :].indirect(T.u6l[:, 0:8]))
 
     def own_lists(r):
-        sl, k = T["sl%d" % r], "sl%d" % r
-        ts(k, "sn", T.sn[:, :], sl[:, :], 176.0, None, OP.add)
-        ts(k, "tf", T.tf[:, 0:22], sl[:, 0:22], 528.0, None, OP.add)
-        ts(k, "tf", T.tf[:, 22:44], sl[:, 22:44], 176.0, None, OP.add)
-        tten(k, "sd", T.sd[:, :], sl[:, 0:22], sl[:, 22:44], OP.subtract)
-        ts(k, "fb", T.fb[:, 1:44:2], sl[:, 22:44], 176.0, None, OP.add)
-        ts("sd", "fb", T.fb[:, 0:44:2], T.sd[:, :], 352.0, None, OP.add)
+        k = "sn%d" % r
+        cp(k, "sf", T.sf[:, :], T[k][:, 0:44])
+        tten("sf", "fb", T.fb[:, 44:88:2], T.sf[:, 22:44], T.sf[:, 0:22], OP.subtract)
 
     def repeat_lists():
-        act("fb", "fb", T.fb[:, 44:88], T.fb[:, 0:44])
-        act("fb", "fb", T.fb[:, 88:176], T.fb[:, 0:88])
-        act("fb", "fb", T.fb[:, 176:264], T.fb[:, 0:88])
+        act("sf", "fb1", T.fb[:, 45:88:2], T.sf[:, 0:22])
+        act("sf", "fb1", T.fb[:, 133:176:2], T.sf[:, 0:22])
+        act("fb", "fb1", T.fb[:, 132:176:2], T.fb[:, 44:88:2], AF.Identity, bias=352.0)
+        act("fb fb1", "fb2", T.fb[:, 88:132], T.fb[:, 44:88])
+        act("fb1", "fb2", T.fb[:, 176:220], T.fb[:, 132:176])
+        act("fb1 fb2", "fb3", T.fb[:, 220:308], T.fb[:, 132:220])
 
-    def fetch(r):
-        arrived("ld%d" % r, "la%d" % r, len(topo.engines(route(topo, partner(r), core)[0], core)))
-        ld = T["ld%d" % r]
-        dma("s", "rp%d" % r, "ld%d" % r, "pl", T.pl[:, :], ld[:, :])
-        for i in range(16):
-            dma("s", "rp%d" % r, "ld%d" % r, "wf%d" % i, T.wf[i:128:16, :], ld[:, :])
-        for k in ["pl"] + ["wf%d" % i for i in range(16)]:
-            last[k] = ("rp%d" % r, total["rp%d" % r], "s")
-
-    WF = " ".join("wf%d" % i for i in range(16))
-
-    def choose():
-        for e in range(2):
-            ts("pl", "ll", T.ll[:, 44 * e:44 * e + 44], T.pl[:, :], 176.0 + 352.0 * e, None, OP.add)
-
-    def spread():
-        act(WF + " lph", "pw", T.pw[:, :], T.wf[:, :].indirect(T.lph[:, :]))
-
-    def table(e, q):
-        o, a = T.s2[:, 512 * e:512 * e + C], T.pw[:, :].indirect(T.ll[:, 22 * e:22 * e + 22])
+    def table(r, e, q):
+        a, b = e >> 1, e & 1
+        o, i = T.s2[:, e:1408:4], T.pw[:, C * (1 - b):C * (2 - b)].indirect(T["pl%d" % r][:, 22 * (1 - a):22 * (2 - a)])
         if q == "a":
-            act("pw ll", "s2%d" % e, o, a)
+            act("pw pl%d" % r, "s2%d" % e, o, i, scale=4.0)
         else:
-            cp("pw ll", "s2%d" % e, o, a)
+            ts("pw pl%d" % r, "s2%d" % e, o, i, 4.0, None, OP.mult)
 
-    S2 = "s20 s21 s22 s23 s2g "
+    def window(r):
+        act("cb pl%d" % r, "pw", T.pw[:, :], T.cb[:, :].indirect(T["pl%d" % r][:, :]))
+
+    S2 = "s20 s21 s22 s23 "
 
     def bank(h, b):
-        n = HALF[h][1]
+        n = PART[h][1]
         return ("pb%d" if h else "pa%d") % b, (T.pb if h else T.pa)[:, 512 * b:512 * b + n]
 
     def plane(t, b):
         return t[:, C * b:C * b + C]
 
     def qx(r, h):
-        op("v", "xp%d0 xp%d1 pad%d" % (r, r, r), "xq%d" % h, V.quantize_mx, T.xq[:, 192 * h:192 * h + 192], T.xs[:, 192 * h:192 * h + 192],
-           T["xp%d" % r][:, 768 * h:768 * h + 768])
+        a, n = ((0, 208), (208, 176))[h] if r < 3 else ((16, 192), (208, 160))[h]
+        op("v", "xp%d%d pad%d" % (r, h, r), "xq%d" % h, V.quantize_mx, T.xq[:, a:a + n], T.xs[:, a:a + n], T["xp%d" % r][:, 4 * a:4 * a + 4 * n])
 
+    def scores(h):
+        a, n = ((0, 208), (192, 192))[h]
+        mm("uq xq0" + " xq1" * h, "pb%d" % h, T.pb[:, 512 * h:512 * h + n], T.uq[:, :], T.us[:, :], T.xq[:, a:a + n], T.xs[:, a:a + n])
+
+    def turn(h):
+        a, n = ((0, 192), (192, 160))[h]
+        op("v", "pb%d" % h, "tt", V.transpose, T.tt[:, a:a + n], T.pb[:, 512 * h + 16:512 * h + 16 + n])
+        op("v", "pb%d" % h, "tt", V.transpose, T.tt[:, C + 192 * h:C + 192 * h + 192], T.pb[:, 512 * h:512 * h + 192])
+
+    def halve(r, h):
+        a, n = XH[h]
+        for b in range(4):
+            act("xp%d%d" % (r, h), "xh%d%d" % (h, b), T.xh[:, C * b + a:C * b + a + n], T["xp%d" % r][:, 64 + 4 * a + b:64 + 4 * a + 4 * n:4], scale=0.5)
+
+    def F(l):
+        return T.fl[:, 22 * l:22 * l + 22]
+
+    act("jj", "cw", T.cw[:, 0:C], T.jj[:, :], scale=32.0)
+    act("jj", "cw", T.cw[:, C:704], T.jj[:, :], AF.Identity, scale=32.0, bias=4.0)
+    act("jj", "cb", T.cb[:, :], T.jj[:, :], AF.Identity, bias=-176.0)
     own_lists(0)
     repeat_lists()
+    qx(0, 0)
+    scores(0)
+    cp("uq url", "ur", T.urq[:, :].bitcast(dt.uint32), T.uq[:, :].bitcast(dt.uint32).indirect(T.url[:, :]))
+    act("uq url", "urs", T.urs[:, :], T.us[:, :].indirect(T.url[:, :]))
+    qx(0, 1)
+    dma("s", "d_w", "xp00 xp01 ub", "wq", T.wq[:, :].bitcast(dt.uint8), T.wc[:, :])
+    dma("s", "d_wp", "", "wp", T.wp[:, :], T.ws[:, :])
+    dma("s", "d_v", "", "vb", T.vb[:, :], T.v[:, :])
+    op("g", "", "one", g.iota, T.one[:, :], [[0, 512]], 1, 0, allow_small_or_imprecise_dtypes=True)
+    for b in range(4):
+        op("g", "one", "eb", g.affine_select, T.eb[:, 512 * b:512 * b + 512], T.one[:, :], [[-1, 512]], OP.is_equal, 0.0, b, 4)
+
     for r in range(3):
         XP = T["xp%d" % r]
-        for h in range(2):
-            qx(r, h)
-            mm("uq xq%d" % h, "pb%d" % h, T.pb[:, 512 * h:512 * h + 192], T.uq[:, :], T.us[:, :], T.xq[:, 192 * h:192 * h + 192], T.xs[:, 192 * h:192 * h + 192])
-        mm("u6 u6s xq0 xq1", "pb2", T.pb[:, 1024:1024 + C], T.u6q[:, :], T.u6s[:, :], T.xq[:, 16:368], T.xs[:, 16:368])
-        for b in range(4):
-            act("xp%d0 xp%d1" % (r, r), "xh%d" % b, plane(T.xh, b), XP[:, 64 + b:1472:4], scale=0.5)
-        act("pb2", "b6", T.b6[:, :], T.pb[:, 1024:1024 + C], AF.Sign, bias=-2.0 ** -93)
-        for h in range(2):
-            tten("pb%d mk2" % h, "kk", T.kk[:, 352 + 192 * h:544 + 192 * h], T.pb[:, 512 * h:512 * h + 192], T.mk2[:, 192 * h:192 * h + 192], OP.is_gt)
-            a = 16 - 16 * h
-            tten("pb%d mk1" % h, "kk", T.kk[:, 176 * h:176 * h + 176], T.pb[:, 512 * h + a:512 * h + a + 176], T.mk1[:, 192 * h + a:192 * h + a + 176], OP.is_gt)
-        op("v", "kk", "tt", V.transpose, T.tt[:, :], T.kk[:, :])
-        for l in range(6):
-            tten("tt", "fm", T.fm[:, 44 * l + 1:44 * l + 44:2], T.tt[:, l:352:16], T.tt[:, 368 + l:720:16], OP.add)
-        scan("fm fb", "fo", T.fo[:, :], T.fm[:, :], T.fb[:, :])
-        cp("fo", "fl", T.fl[:, :], T.fo[:, 1:264:2])
+        scores(1)
+        for i in range(2):
+            mm("ur urs xq0 xq1", "pb%d" % (2 + i), T.pb[:, 1024 + 512 * i:1024 + 512 * i + C], T.urq[:, 128 * i:128 * i + 128], T.urs[:, 128 * i:128 * i + 128],
+               T.xq[:, 16:368], T.xs[:, 16:368])
+        turn(0)
+        turn(1)
+        ts("tt gl", "fm", T.fm[:, 1:320:2], T.tt[:, :].indirect(T.gl[:, :]), 0.0, None, OP.is_gt)
+        scan("fm fbc fb fb1 fb2 fb3", "fo", T.fo[:, :], T.fm[:, 0:308], T.fb[:, :])
+        cp("fo", "fl", T.fl[:, :], T.fo[:, 45:308:2])
+        act("pb2", "b1", T.b1[:, :], T.pb[:, 1024:1024 + C], AF.Sign, bias=-2.0 ** -93)
         if r == 0:
-            fetch(0)
-            dma("s", "d_w", "", "wq", T.wq[:, :].bitcast(dt.uint8), T.wc[:, :])
-            dma("s", "d_wp", "", "wp", T.wp[:, :], T.ws[:, :])
-            dma("s", "d_v", "", "vb", T.vb[:, :], T.v[:, :])
+            halve(0, 0)
         else:
-            choose()
-            spread()
-        W, key = T.w6, "w6"
-        for l in range(5, 0, -1):
-            N_, nk = (T.wv0, "wv0") if l % 2 else (T.wv1, "wv1")
-            off = T.fl[:, 22 * l:22 * l + 22]
-            rk = key if key == "w6" else key + "a " + key + "b"
-            cp(rk + " fl", nk + "a", N_[:, 0:352], W[:, :].indirect(off))
-            act(rk + " fl", nk + "b", N_[:, 352:704], W[:, :].indirect(off), AF.Identity, bias=float(512 << (l - 1)))
-            W, key = N_, nk
-            if r == 0 and l == 5:
-                ts("j16 cf", "m16", T.m16[:, 0:C], T.j16[:, :], PR, None, OP.is_equal)
-            if r == 0 and l == 4:
-                ts("clf cf", "cl", T.cl[:, :], T.clf[:, :], PR, None, OP.add)
-                ts("cf", "cg", cg[:, 0:1], PR, 44.0, None, OP.mult)
-                ts("lpf cg", "lph", T.lph[:, :], T.lpf[:, :], cg[:, 0:1], None, OP.add)
+            table(r, 2, "a")
+        act("cw fl", "ha", T.ha[:, 0:C], T.cw[:, :].indirect(F(5)))
+        ts("cw fl", "la", T.la[:, :], T.cw[:, :].indirect(F(2)), 1.0, None, OP.add)
+        act("ha", "ha2", T.ha[:, C:704], T.ha[:, 0:C], AF.Identity, bias=8.0)
+        tten("la fl b1", "lb", T.lb[:, :], T.la[:, :].indirect(F(1)), T.b1[:, :], OP.add)
+        act("ha ha2 fl", "hc", T.hc[:, 0:C], T.ha[:, :].indirect(F(4)))
         if r == 0:
-            choose()
-            spread()
-        for e in range(3):
-            table(e, "a")
-        tten(key + "a " + key + "b fl m16", "wm", T.wm[:, :], W[:, :].indirect(T.fl[:, 0:22]), T.m16[:, 0:352], OP.mult)
-        scan("wm r16", "wsn", T.wsn[:, :], T.r16[:, 0:352], T.wm[:, :])
-        cp("wsn", "vi", T.vi[:, :], T.wsn[:, 15:352:16])
-        ts("vi", "vk0", T.vk[:, 0:22], T.vi[:, :], 0x600, None, OP.bitwise_and)
-        ts("vi", "vk3", T.vk[:, 66:88], T.vi[:, :], 511, None, OP.bitwise_and)
-        tten("vk0 cl", "ki", T.ki[:, :], T.vk[:, 0:22], T.cl[:, :], OP.add)
-        cp("vk3", "il", T.il[:, :], T.vk[:, 66:88])
-        cp("ki", "k1", T.k1[:, :], T.ki[:, :])
-        ts("vi", "vk1", T.vk[:, 22:44], T.vi[:, :], 2, 0x600, OP.logical_shift_right, OP.bitwise_and)
-        ts("vi", "vk2", T.vk[:, 44:66], T.vi[:, :], 4, 0x600, OP.logical_shift_right, OP.bitwise_and)
-        table(3, "v")
+            ts("j16 cf", "m16", T.m16[:, :], T.j16[:, :], PR, None, OP.is_equal)
+        tten("lb fl m16", "lm", T.lm[:, :], T.lb[:, :].indirect(F(0)), T.m16[:, :], OP.mult)
+        act("hc", "hc2", T.hc[:, C:704], T.hc[:, 0:C], AF.Identity, bias=1.0)
+        scan("lm r16", "ln", T.ln[:, :], T.r16[:, :], T.lm[:, :])
+        act("hc hc2 fl", "hd", T.hd[:, :], T.hc[:, :].indirect(F(3)))
+        ts("ln", "i3", T.i3[:, :], T.ln[:, 15:C:16], 1.0 / 32, None, OP.mult)
+        cp("ln", "vi", T.vi[:, :], T.ln[:, 15:C:16])
+        act("hd i3", "hm", T.hm[:, :], T.hd[:, :].indirect(T.i3[:, :]))
         if r == 0:
-            cp("m16", "m16", T.m16[:, 352:704], T.m16[:, 0:352])
+            ts("m16", "mx", T.mx[:, :], T.m16[:, :], -BIG - KM, KM, OP.mult, OP.add)
+            window(0)
+        ts("vi", "va0", T.va[:, 0:22], T.vi[:, :], 1, 1, OP.logical_shift_right, OP.bitwise_and)
+        ts("vi", "va1", T.va[:, 22:44], T.vi[:, :], 1, 2, OP.logical_shift_right, OP.bitwise_and)
+        tten("va0 fo", "ki", T.ki[:, :], T.va[:, 0:22], T.fo[:, 1:44:2], OP.add)
+        cp("ki", "k0", T.k0[:, :], T.ki[:, :])
+
+        def second(j):
+            tten(S2 + "k%d m16" % j, "km", T.km[:, :], T.s2[:, :].indirect(T["k%d" % j][:, :]), T.m16[:, :], OP.mult)
+            scan("km r16", "ksn", T.ksn[:, :], T.r16[:, :], T.km[:, :])
+
+        def onward(j):
+            k, e = ("kb", T.kb[:, :]) if j == 0 else ("va3", T.va[:, 66:88])
+            tten("ksn " + k, "ki", T.ki[:, :], T.ksn[:, 15:C:16], e, OP.add)
+            ts("ki", "k%d" % (j + 2), T["k%d" % (j + 2)][:, :], T.ki[:, :], 704.0, None, OP.add)
+
+        if r > 0:
+            table(r, 3, "v")
+            second(0)
+        else:
+            table(r, 0, "a")
+            table(r, 1, "a")
+        halve(r, 1)
+        hold("hm mx", "hn", T.hn[:, :], T.mx[:, :], T.hm[:, :])
+        ts("hn cg1", "i6", T.i6[:, :], T.hn[:, 15:C:16], 1.0 / 32, cg[:, 1:2], OP.mult, OP.add)
+        cp("hn", "vj", T.vj[:, :], T.hn[:, 15:C:16])
+        if r == 0:
+            ts("j16 cf", "m8", T.m8[:, :], T.j16[:, 0:C:2], PE, None, OP.is_equal)
             op("v", "eb", "eq", V.quantize_mx, T.eq[:, :], T.es[:, :], T.eb[:, :])
+            ts("m8", "m8", T.m8[:, :], T.m8[:, :], -132.0, 4.0, OP.mult, OP.add)
+            table(r, 3, "v")
+        ts("vj", "va2", T.va[:, 44:66], T.vj[:, :], 1, None, OP.bitwise_and)
+        ts("vj", "va3", T.va[:, 66:88], T.vj[:, :], 2, 3, OP.logical_shift_right, OP.bitwise_and)
+        tten("va1 va2", "kb", T.kb[:, :], T.va[:, 22:44], T.va[:, 44:66], OP.add)
+        if r == 0:
+            table(r, 2, "v")
+            second(0)
         for h in range(2):
-            a, n = HALF[h]
+            a, n = PART[h]
             for b in range(4):
-                act("xh%d il" % b, "gi%d%d" % (h, b), T.gi[:, 4 * a + b:4 * a + 4 * n:4], plane(T.xh, b).indirect(T.il[:, a // 16:(a + n) // 16]))
-        for j in (1, 2, 3):
-            tten(S2 + "k%d m16" % j, "km", T.km[:, :], T.s2[:, :].indirect(T["k%d" % j][:, :]), T.m16[:, 0:352], OP.mult)
-            scan("km r16", "ksn", T.ksn[:, :], T.r16[:, 0:352], T.km[:, :])
-            if j < 3:
-                tten("ksn vk%d" % j, "ki", T.ki[:, :], T.ksn[:, 15:352:16], T.vk[:, 22 * j:22 * j + 22], OP.add)
-                ts("ki", "k%d" % (j + 1), T["k%d" % (j + 1)][:, :], T.ki[:, :], 176.0, None, OP.add)
-            else:
-                ts("ksn", "k6", T.k6[:, :], T.ksn[:, 15:352:16], 176.0, None, OP.add)
+                act("xh0%d xh1%d i6" % (b, b), "gi%d%d" % (h, b), T.gi[:, 4 * a + b:4 * a + 4 * n:4], plane(T.xh, b).indirect(T.i6[:, a // 16:(a + n) // 16]))
+        act("pb3", "b6", T.b6[:, :], T.pb[:, 1536:1536 + C], AF.Sign, bias=-2.0 ** -93)
+        for j in (0, 2):
+            onward(j)
+            second(j + 2)
+        ts("ksn", "k6", T.k6[:, :], T.ksn[:, 15:C:16], 0.25, 176.0, OP.mult, OP.add)
 
         def mosaic(h):
-            a, n = HALF[h]
+            a, n = PART[h]
             for b in range(4):
                 v = slice(4 * a + b, 4 * a + 4 * n, 4)
-                tten("xh%d k6 gi%d%d" % (b, h, b), "z%d" % h, T.z[:, v], plane(T.xh, b).indirect(T.k6[:, a // 16:(a + n) // 16]), T.gi[:, v], OP.add)
+                tten("xh0%d xh1%d k6 gi%d%d" % (b, b, h, b), "z%d" % h, T.z[:, v], plane(T.xh, b).indirect(T.k6[:, a // 16:(a + n) // 16]), T.gi[:, v], OP.add)
             op("v", "z%d" % h, "zq%d" % h, V.quantize_mx, T.zq[:, a:a + n], T.zs[:, a:a + n], T.z[:, 4 * a:4 * a + 4 * n])
             for b in range(4):
                 k, o = bank(h, b)
                 mm("wq wp zq%d" % h, k, o, T.wq[:, 128 * b:128 * b + 128], T.wp[:, 128 * b:128 * b + 128], T.zq[:, a:a + n], T.zs[:, a:a + n])
 
         def hcast(h, b, q):
-            a, n = HALF[h]
+            a, n = PART[h]
             k, i = bank(h, b)
             o = T.hb[:, 4 * a + b:4 * a + 4 * n:4]
             if q == "a":
@@ -390,15 +439,15 @@ def rank_program(g, core, T, topo):
                 ts(k, "hb%d%d" % (h, b), o, i, 0.03125, None, OP.mult)
 
         def qh(h):
-            a, n = HALF[h]
+            a, n = PART[h]
             op("v", " ".join("hb%d%d" % (h, b) for b in range(4)), "hq%d%d" % (r, h), V.quantize_mx, T["hq%d" % r][:, a:a + n],
                T["hs%d" % r][:, a:a + n], T.hb[:, 4 * a:4 * a + 4 * n])
-            send_half(r, h)
+            send_part(r, h)
 
         mosaic(0)
+        act("b6 k6", "en", T.en[:, :], T.b6[:, :].indirect(T.k6[:, :]))
         for b in range(4):
             hcast(0, b, "a")
-        act("b6 k6", "en", T.en[:, :], T.b6[:, :].indirect(T.k6[:, :]))
         mosaic(1)
         qh(0)
         hcast(1, 0, "a")
@@ -406,28 +455,30 @@ def rank_program(g, core, T, topo):
         hcast(1, 2, "a")
         hcast(1, 3, "v")
         qh(1)
-        tten("en", "dd", T.dd[:, 0:352:2], T.en[:, 0:352:2], T.en[:, 1:352:2], OP.not_equal)
-        ts("dd", "dd", T.dd[:, 1:352:2], T.dd[:, 0:352:2], -1.0, None, OP.mult)
-        tten("dd sn m16", "tm", T.tm[:, :], T.dd[:, :].indirect(T.sn[:, :]), T.m16[:, :], OP.mult)
-        scan("tm r16", "ts", T.ts[:, :], T.r16[:, :], T.tm[:, :])
-        tten("ts tf", "tg", T.tg[:, :], T.ts[:, 15:704:16], T.tf[:, :], OP.add)
+        sn, ns = T["sn%d" % r], T["sn%d" % (r + 1)]
+        tten("en", "dd", T.dd[:, :], T.en[:, 0:C:2], T.en[:, 1:C:2], OP.mult)
+        hold("dd m8", "dn", T.dn[:, :], T.m8[:, :], T.dd[:, :])
+        ts("dn cg3 cg4", "tf", T.tf[:, :], T.dn[:, 7:176:8], cg[:, 3:4], cg[:, 4:5], OP.is_lt, OP.mult)
+        tten("tf cl", "tg", T.tg[:, :], T.tf[:, :], T.cl[:, 0:22], OP.add)
         cp("tg", "tl", T.tl[:, :], T.tg[:, :])
-        lo = 0 if r < 2 else 352
-        tten("pw tl m16", "tm", T.tm[:, lo:704], T.pw[:, :].indirect(T.tl[:, lo // 16:44]), T.m16[:, lo:704], OP.mult)
-        scan("tm r16", "ts", T.ts[:, lo:704], T.r16[:, lo:704], T.tm[:, lo:704])
+        cp("pw tl", "uw0", T.uw[:, 0:C], T.pw[:, C:704].indirect(T.tl[:, :]))
+        act("pw tl", "uw1", T.uw[:, C:704], T.pw[:, 0:C].indirect(T.tl[:, :]))
+        tten("uw0 sn%d m16" % r, "km", T.km[:, :], T.uw[:, 0:C].indirect(sn[:, 0:22]), T.m16[:, :], OP.mult)
         if r < 2:
-            cp("ts", "sl%d" % (r + 1), T["sl%d" % (r + 1)][:, :], T.ts[:, 15:704:16])
+            act("uw1 sn%d" % r, "t1", T.t1[:, :], T.uw[:, C:704].indirect(sn[:, 22:44]))
+        scan("km r16", "ksn", T.ksn[:, :], T.r16[:, :], T.km[:, :])
+        ts("ksn", "tx%d" % r, ns[:, 0:22], T.ksn[:, 15:C:16], 176.0, None, OP.add)
+        if r < 2:
+            hold("t1 mx", "hn", T.hn[:, :], T.mx[:, :], T.t1[:, :])
+            ts("hn cg2 tx%d" % r, "sn%d" % (r + 1), ns[:, 22:44], T.hn[:, 15:C:16], cg[:, 2:3], None, OP.add)
             send_list(r + 1)
-            fetch(r + 1)
-        ts("ts", "tx", T.tx[:, :], T.ts[:, 367:704:16], 176.0, None, OP.add)
-        if r < 2:
             own_lists(r + 1)
         else:
             op("v", "vb", "vq", V.quantize_mx, T.vq[:, :], T.vs[:, :], T.vb[:, :])
         hp = route(topo, partner(r), core)
         for h in range(2):
-            a, n = HALF[h]
-            arrived("dq%d%d" % (r, h), ("ca%d" if h == 0 else "cb%d") % r, sum(2 * len(topo.engines(k, core)) for k in hp[2 * h:2 * h + 2]))
+            a, n = PART[h]
+            arrived("dq%d%d" % (r, h), ("ca%d", "cb%d")[h] % r, sum(len(topo.engines(hp[k], core)) for k in CODES[h] + (SCALES[h],)))
             for b in range(4):
                 k, ps = bank(h, b)
                 mm("eq dq%d%d" % (r, h), k, ps, T.eq[:, 128 * b:128 * b + 128], T.es[:, 128 * b:128 * b + 128],
@@ -435,27 +486,38 @@ def rank_program(g, core, T, topo):
             for b in range(4):
                 k, ps = bank(h, b)
                 o = T.dw[:, C * b + a:C * b + a + n]
-                if h == 0 or b % 2 == 0:
+                if h == 0 or b > 0:
                     act(k, "dw%d%d" % (h, b), o, ps)
                 else:
                     cp(k, "dw%d%d" % (h, b), o, ps)
         if r < 2:
             repeat_lists()
-        for b in range(4):
-            v = slice(64 + b, 1472, 4)
-            tten("tx xp%d0 xp%d1 dw0%d dw1%d" % (r, r, b, b), "xp%d0" % (r + 1), T["xp%d" % (r + 1)][:, v], plane(T.dw, b).indirect(T.tx[:, :]), XP[:, v], OP.add)
-
-    act("pw tl", "tw", T.tw[:, :], T.pw[:, :].indirect(T.tl[:, :]), AF.Identity, bias=176.0)
-    dma("s", "d_so", "tw", "so", T.so[:, 0:352], T.tw[0:128:16, 352:704])
-    dma("s", "d_so", "tw", "so2", T.so[:, 352:704], T.tw[0:128:16, 0:352])
-    qx(3, 0)
-    qx(3, 1)
-    dma("s", "d_oc", "xq0 xq1", "oc", T.oc[:, :], T.xq[:, 16:368].bitcast(dt.uint8))
+            window(r + 1)
+        else:
+            for b in range(2):
+                act("uw%d sn2" % b, "tw", T.tw[:, C * b:C * b + C], T.uw[:, C * b:C * b + C].indirect(sn[:, 22 * b:22 * b + 22]), AF.Identity, bias=176.0)
+            dma("s", "d_so", "tw", "so", T.so[:, :], T.tw[0:128:16, :])
+        for h in range(2):
+            a, n = XH[h]
+            for b in range(4):
+                v = slice(64 + 4 * a + b, 64 + 4 * a + 4 * n, 4)
+                tten("tx%d xp%d%d dw0%d dw1%d" % (r, r, h, b, b), "xp%d%d" % (r + 1, h), T["xp%d" % (r + 1)][:, v],
+                     plane(T.dw, b).indirect(ns[:, a // 16:(a + n) // 16]), XP[:, v], OP.add)
+            qx(r + 1, h)
+            if r < 2:
+                if h == 0:
+                    scores(0)
+                    halve(r + 1, 0)
+                    table(r + 1, 0, "a")
+                    table(r + 1, 1, "a")
+            else:
+                q = slice(16 + a, 16 + a + n)
+                mm("vq xq%d" % h, "pa%d" % h, T.pa[:, 512 * h:512 * h + n], T.vq[:, :], T.vs[:, :], T.xq[:, q], T.xs[:, q])
+                dma("s", "d_oc", "xq%d" % h, "oc%d" % h, T.oc[:, 4 * a:4 * a + 4 * n], T.xq[:, q].bitcast(dt.uint8))
+                act("pa%d" % h, "yb%d" % h, T.yb[:, a:a + n], T.pa[:, 512 * h:512 * h + n])
+                dma("a", "d_y", "yb%d" % h, "y%d" % h, T.y[:, a:a + n], T.yb[:, a:a + n])
     for k in range(4):
         dma("s", "d_oc", "xq0 xq1", "osc%d" % k, T.osc[4 * k:4 * k + 4, :], T.xs[32 * k:32 * k + 4, 16:368])
-    mm("vq xq0 xq1", "pa0", T.pa[:, 0:C], T.vq[:, :], T.vs[:, :], T.xq[:, 16:368], T.xs[:, 16:368])
-    cp("pa0", "yb", T.yb[:, :], T.pa[:, 0:C])
-    dma("a", "d_y", "yb", "y", T.y[:, :], T.yb[:, :])
     total["ls"] = sent[0]
     for s in total:
         g.wait_ge(T.sem[s], total[s])

@@ -3,33 +3,33 @@ from concourse.mybir import dt, AluOpType as OP, ActivationFunctionType as AF
 
 C = 352
 MASK = [2, 4, 1]
-PART = [(0, 224), (224, 128)]
+PART = [(0, 192), (192, 160)]
 XH = [(0, 192), (192, 160)]
 KM, BIG = 16384.0, 1048576.0
+ROWS = [1, 6]
 BF, F32, I32, U16, U8, E4 = "bfloat16", "float32", "int32", "uint16", "uint8", "float8_e4m3fn_x4"
 SCRATCH = {
     "sei": ("sbuf", [128, 44], I32), "ub": ("sbuf", [128, 512], BF), "vb": ("sbuf", [128, 512], BF),
     "wq": ("sbuf", [128, 512], E4), "wp": ("sbuf", [128, 512], U8),
     "uq": ("sbuf", [128, 128], E4), "us": ("sbuf", [128, 128], U8), "vq": ("sbuf", [128, 128], E4), "vs": ("sbuf", [128, 128], U8),
-    "urq": ("sbuf", [128, 256], E4), "urs": ("sbuf", [128, 256], U8),
+    "urq": ("sbuf", [128, 384], E4), "urs": ("sbuf", [128, 384], U8),
     "pc": ("sbuf", [128, 8], I32), "ci": ("sbuf", [128, 8], I32), "cf": ("sbuf", [128, 8], F32), "cg": ("sbuf", [128, 8], F32),
+    "cn": ("sbuf", [128, 4], F32),
     "j16": ("sbuf", [128, C], F32), "jj": ("sbuf", [128, C], F32), "cw": ("sbuf", [128, 704], F32), "cb": ("sbuf", [128, C], BF),
     "m16": ("sbuf", [128, C], BF), "r16": ("sbuf", [128, C], BF), "mx": ("sbuf", [128, C], BF), "m8": ("sbuf", [128, 176], BF),
     "cq": ("sbuf", [128, 24], F32), "cl": ("sbuf", [128, 24], F32), "ga": ("sbuf", [128, 10], I32), "gb": ("sbuf", [128, 10], F32),
-    "ge": ("sbuf", [128, 10], F32), "gl": ("sbuf", [128, 10], U16),
-    "urf": ("sbuf", [128, 16], F32), "url": ("sbuf", [128, 16], U16),
+    "ge": ("sbuf", [128, 10], F32), "gl": ("sbuf", [128, 10], U16), "url": ("sbuf", [128, 24], U16),
     "one": ("sbuf", [128, 512], BF), "eb": ("sbuf", [128, 2048], BF), "eq": ("sbuf", [128, 512], E4), "es": ("sbuf", [128, 512], U8),
     "xq": ("sbuf", [128, 384], E4), "xs": ("sbuf", [128, 384], U8), "xh": ("sbuf", [128, 1408], BF),
-    "b1": ("sbuf", [128, C], BF), "b6": ("sbuf", [128, C], BF),
+    "b1": ("sbuf", [128, C], BF), "b3": ("sbuf", [128, C], BF), "b6": ("sbuf", [128, C], BF),
     "tt": ("sbuf", [128, 736], F32), "fm": ("sbuf", [128, 320], F32), "fb": ("sbuf", [128, 308], F32),
     "fo": ("sbuf", [128, 308], F32), "fl": ("sbuf", [128, 132], U16), "sf": ("sbuf", [128, 44], F32),
     "la": ("sbuf", [128, C], F32), "lb": ("sbuf", [128, C], F32), "lm": ("sbuf", [128, C], F32), "ln": ("sbuf", [128, C], F32),
-    "ha": ("sbuf", [128, 704], F32), "hc": ("sbuf", [128, 704], F32), "hd": ("sbuf", [128, C], F32), "hm": ("sbuf", [128, C], F32),
-    "hn": ("sbuf", [128, C], F32),
+    "ha": ("sbuf", [128, 704], F32), "hc": ("sbuf", [128, 704], F32), "hd": ("sbuf", [128, C], F32),
     "i3": ("sbuf", [128, 22], U16), "i6": ("sbuf", [128, 22], U16), "vi": ("sbuf", [128, 22], I32), "vj": ("sbuf", [128, 22], I32),
     "va": ("sbuf", [128, 88], I32),
     "pw": ("sbuf", [128, 704], BF), "s2": ("sbuf", [128, 1408], BF), "km": ("sbuf", [128, C], BF), "ksn": ("sbuf", [128, C], BF),
-    "ki": ("sbuf", [128, 22], F32), "kb": ("sbuf", [128, 22], F32),
+    "ku": ("sbuf", [128, C], BF), "kh": ("sbuf", [128, C], F32), "ki": ("sbuf", [128, 22], F32), "kb": ("sbuf", [128, 22], F32),
     "k0": ("sbuf", [128, 22], U16), "k2": ("sbuf", [128, 22], U16), "k4": ("sbuf", [128, 22], U16), "k6": ("sbuf", [128, 22], U16),
     "en": ("sbuf", [128, C], BF), "dd": ("sbuf", [128, 176], BF), "dn": ("sbuf", [128, 176], BF), "tf": ("sbuf", [128, 22], F32),
     "tg": ("sbuf", [128, 22], F32), "tl": ("sbuf", [128, 22], U16), "uw": ("sbuf", [128, 704], BF), "t1": ("sbuf", [128, C], BF),
@@ -56,6 +56,17 @@ for _r in range(3):
 CODES = [(0, 1), (2, 3)]
 SCALES = [2, 0]
 LISTS = 3
+
+BITS = "s1 m1 m6 ts0 tr1 ts1 fm fo fl t2.a b1 t3.a "
+BITS0 = "m1 tr1 ts1 fm fo fl b1 kc "
+PATH = "ha la ha2 lb hc lm hc2 ln hd vi i3 hm.a va0 va1 ki "
+PATH1 = "k0 g0 hn xh0.a xh1.a xh2.a xh3.a h0 vj kb va2 i6 va3 "
+PATH0 = "k0 pw0.v pw1.a hn r16 vj i6 va2 va3 t0.a t1.v t2.a t3.v xh0.a xh1.a r6 m6 g0 xh2.v h0 xh3.v kb m8 "
+SECOND = "gi0 gi1 gi2 gi3 b6 k2 g2 k4 g4 k6 en "
+LAYER = "z0 z10 q0 c00.a c01.a c02.a z11 z12 z13 dd q1 dn c03.v tf h0q tg c10.a c11.v tl c12.a c13.v h1q "
+TURNS = "u0.v u1.a n0 n1 ns0 ns1 "
+NEWX = "e0 fb0 fb1 d00.v d01.a d02.v d03.a e1 d10.v d11.a d12.a d13.a "
+NEXT = "pw0.a pw1.a fb2 x0 x10 qx0 s0 t0.a t1.a x11 x12 x13 qx1 tr0"
 
 
 def route(topo, core, dst):
@@ -141,12 +152,6 @@ def rank_program(g, core, T, topo):
 
     def op(q, r, w, f, *args, **kw):
         r, w = r.split(), w.split()
-        banks = [k for k in r if k[0:2] in ("pa", "pb")]
-        for k in banks:
-            for t in readers.get(k, []):
-                if t[2] != q and seen.get((q, t[0]), 0) < t[1]:
-                    eng[q].wait_ge(T.sem[t[0]], t[1])
-                    seen[(q, t[0])] = t[1]
         need(q, r, w)
         s = sem_of[q]
         f(*args, **kw).then_inc(T.sem[s], 1)
@@ -183,6 +188,14 @@ def rank_program(g, core, T, topo):
     def act(r, w, out, in_, func=AF.Copy, **kw):
         op("a", r, w, A.activation, out, in_, func, **kw)
 
+    def times(q, r, w, out, in_, c=None):
+        if q == "a":
+            act(r, w, out, in_, **({} if c is None else {"scale": c}))
+        elif c is None:
+            cp(r, w, out, in_)
+        else:
+            ts(r, w, out, in_, c, None, OP.mult)
+
     def mm(r, w, out, wq, wsc, xq, xsc):
         op("p", r, w, P.matmul_mx, out, wq, wsc, xq, xsc, True, True)
 
@@ -199,40 +212,43 @@ def rank_program(g, core, T, topo):
     dma("s", "d_x", "", "xp00", T.xp0[:, 64:832], T.x[:, 0:768])
     dma("a", "d_x2", "", "xp01", T.xp0[:, 832:1472], T.x[:, 768:1408])
     op("g", "", "pc", g.iota, T.pc[:, 0:1], [[0, 1]], 0, 1)
-    iota("urf", T.urf[:, :], [[5, 2], [16, 8]], 1, 0)
     iota("cq", T.cq[:, :], [[16, 24]], 0, 0)
     iota("j16", T.j16[:, :], [[0, 22], [1, 16]], 0, 0)
-    iota("jj", T.jj[:, :], [[1, C]], 0, 0)
-    for r in range(3):
-        op("v", "", "pad%d" % r, V.memset, T["xp%d" % r][:, 0:64], 0.0)
-        op("v", "", "pad%d" % r, V.memset, T["xp%d" % r][:, 1472:1536], 0.0)
+    iota("fbc", T.fb[:, 0:44:2], [[0, 22]], 2, 0)
+    op("v", "", "pad0", V.memset, T.xp0[:, 0:64], 0.0)
+    op("v", "", "pad0", V.memset, T.xp0[:, 1472:1536], 0.0)
     ci, cf, cg = T.ci, T.cf, T.cg
     ts("pc", "ci", ci[:, 0:1], T.pc[:, 0:1], 15, None, OP.bitwise_and)
     ts("pc", "ci", ci[:, 1:2], T.pc[:, 0:1], 4, 1, OP.logical_shift_right, OP.bitwise_and)
     ts("pc", "ci", ci[:, 2:3], T.pc[:, 0:1], 1, None, OP.bitwise_and)
     ts("pc", "ci", ci[:, 3:4], T.pc[:, 0:1], 14, None, OP.bitwise_and)
-    op("v", "", "fm", V.memset, T.fm[:, 0:320:2], 0.0)
-    op("v", "", "r16o", V.memset, T.r16[:, :], 1.0)
+    for i, l in enumerate(ROWS):
+        ts("cq", "url", T.url[:, 8 * i:8 * i + 8], T.cq[:, 0:8], float(l), None, OP.add)
     cp("ci", "cf", cf[:, 0:4], ci[:, 0:4])
-    cp("urf", "url", T.url[:, :], T.urf[:, :])
-    op("v", "r16o", "r16", V.memset, T.r16[:, 0:C:16], 0.0)
+    op("v", "", "fm", V.memset, T.fm[:, 0:320:2], 0.0)
     PR, PH, PP, PE = (cf[:, i:i + 1] for i in range(4))
-    ts("cf", "cg0", cg[:, 0:1], PH, PP, 368.0, OP.not_equal, OP.mult)
     ts("cq cf", "cl", T.cl[:, :], T.cq[:, :], PR, None, OP.add)
-    ts("cf", "cg1", cg[:, 1:2], PR, KM / 32, -15 * KM / 32, OP.mult, OP.add)
-    ts("cf", "cg2", cg[:, 2:3], PR, KM, 176 - 15 * KM, OP.mult, OP.add)
+    ts("cf", "cg0", cg[:, 0:1], PH, PP, 368.0, OP.not_equal, OP.mult)
+    ts("cf", "cn", T.cn[:, :], cf[:, 0:4], -1.0, None, OP.mult)
+    for i, (p, a, b) in enumerate(((PR, KM, 176 - 15 * KM), (PE, -2.0, 28.0), (PP, -2.0, 1.0), (PR, KM / 32, -15 * KM / 32))):
+        act("cf", "cg%d" % (i + 2), cg[:, i + 2:i + 3], p, AF.Identity, scale=a, bias=b)
+    act("cl", "fbd", T.fb[:, 1:44:2], T.cl[:, 0:22], scale=4.0)
+    act("j16 cn", "ln", T.ln[:, :], T.j16[:, :], AF.Abs, bias=T.cn[:, 0:1])
+    act("j16 cn", "lm", T.lm[:, 0:176], T.j16[:, 0:C:2], AF.Abs, bias=T.cn[:, 3:4])
+    act("ln", "m16", T.m16[:, :], T.ln[:, :], AF.Relu, scale=-1.0, bias=1.0)
     ts("cl", "ga", T.ga[:, :], T.cl[:, 0:10], 1.0 / 22, -0.477, OP.mult, OP.add)
-    ts("cf", "cg3", cg[:, 3:4], PE, -2.0, 28.0, OP.mult, OP.add)
     ts("cl cg0", "ge", T.ge[:, :], T.cl[:, 0:10], 16.0, cg[:, 0:1], OP.mult, OP.add)
-    ts("ga", "gb", T.gb[:, :], T.ga[:, :], -351.0, -1.0, OP.mult, OP.add)
-    ts("cf", "cg4", cg[:, 4:5], PP, -2.0, 1.0, OP.mult, OP.add)
-    ts("ga", "ga0", T.cq[:, 0:10], T.ga[:, :], 0.0, None, OP.is_equal)
-    tten("gb ge", "ge", T.ge[:, :], T.ge[:, :], T.gb[:, :], OP.add)
-    ts("cl", "fbc", T.fb[:, 1:44:2], T.cl[:, 0:22], 4.0, None, OP.mult)
-    tten("ge ga0", "ge", T.ge[:, :], T.ge[:, :], T.cq[:, 0:10], OP.add)
-    op("v", "", "fbc", V.memset, T.fb[:, 0:44:2], 2.0)
-    cp("ge", "gl", T.gl[:, :], T.ge[:, :])
     cp("sei", "sn0", T.sn0[:, 0:44], T.sei[:, :])
+
+    def score_list():
+        ts("ga", "gb", T.gb[:, :], T.ga[:, :], -351.0, -1.0, OP.mult, OP.add)
+        ts("ga", "ga0", T.cq[:, 10:20], T.ga[:, :], 0.0, None, OP.is_equal)
+        own_lists(0)
+        tten("gb ge", "ge", T.ge[:, :], T.ge[:, :], T.gb[:, :], OP.add)
+        run(0, "tr0")
+        tten("ge ga0", "ge", T.ge[:, :], T.ge[:, :], T.cq[:, 10:20], OP.add)
+        run(0, "ts0")
+        cp("ge", "gl", T.gl[:, :], T.ge[:, :])
 
     sent = [0]
 
@@ -266,35 +282,24 @@ def rank_program(g, core, T, topo):
         a, m = PART[h]
         g.remote_dma(T["fs%d" % r][:, 0:m], T["hs%d" % r][:, a:a + m], T.sem["hp%d" % r], T.sem.ls, pid, rid, bits(e))
         sent[0] += len(e)
-
-    send_list(0)
-    op("v", "ub", "uq", V.quantize_mx, T.uq[:, :], T.us[:, :], T.ub[:, :])
+        hp = route(topo, partner(r), core)
+        arrived("dq%d%d" % (r, h), ("ca%d", "cb%d")[h] % r, sum(len(topo.engines(hp[k], core)) for k in CODES[h] + (SCALES[h],)))
 
     def own_lists(r):
         k = "sn%d" % r
         cp(k, "sf", T.sf[:, :], T[k][:, 0:44])
         tten("sf", "fb", T.fb[:, 44:88:2], T.sf[:, 22:44], T.sf[:, 0:22], OP.subtract)
 
-    def repeat_lists():
-        act("sf", "fb1", T.fb[:, 45:88:2], T.sf[:, 0:22])
-        act("sf", "fb1", T.fb[:, 133:176:2], T.sf[:, 0:22])
-        act("fb", "fb1", T.fb[:, 132:176:2], T.fb[:, 44:88:2], AF.Identity, bias=352.0)
-        act("fb fb1", "fb2", T.fb[:, 88:132], T.fb[:, 44:88])
-        act("fb1", "fb2", T.fb[:, 176:220], T.fb[:, 132:176])
-        act("fb1 fb2", "fb3", T.fb[:, 220:308], T.fb[:, 132:220])
-
-    def table(r, e, q):
-        a, b = e >> 1, e & 1
-        o, i = T.s2[:, e:1408:4], T.pw[:, C * (1 - b):C * (2 - b)].indirect(T["pl%d" % r][:, 22 * (1 - a):22 * (2 - a)])
-        if q == "a":
-            act("pw pl%d" % r, "s2%d" % e, o, i, scale=4.0)
+    def repeat_lists(i):
+        if i == 0:
+            act("sf", "fb1", T.fb[:, 45:88:2], T.sf[:, 0:22])
+            act("sf", "fb1", T.fb[:, 133:176:2], T.sf[:, 0:22])
+            act("fb", "fb1", T.fb[:, 132:176:2], T.fb[:, 44:88:2], AF.Identity, bias=352.0)
+        elif i == 1:
+            act("fb fb1", "fb2", T.fb[:, 88:132], T.fb[:, 44:88])
+            act("fb1", "fb2", T.fb[:, 176:220], T.fb[:, 132:176])
         else:
-            ts("pw pl%d" % r, "s2%d" % e, o, i, 4.0, None, OP.mult)
-
-    def window(r):
-        act("cb pl%d" % r, "pw", T.pw[:, :], T.cb[:, :].indirect(T["pl%d" % r][:, :]))
-
-    S2 = "s20 s21 s22 s23 "
+            act("fb1 fb2", "fb3", T.fb[:, 220:308], T.fb[:, 132:220])
 
     def bank(h, b):
         n = PART[h][1]
@@ -311,211 +316,224 @@ def rank_program(g, core, T, topo):
         a, n = ((0, 208), (192, 192))[h]
         mm("uq xq0" + " xq1" * h, "pb%d" % h, T.pb[:, 512 * h:512 * h + n], T.uq[:, :], T.us[:, :], T.xq[:, a:a + n], T.xs[:, a:a + n])
 
-    def turn(h):
-        a, n = ((0, 192), (192, 160))[h]
-        op("v", "pb%d" % h, "tt", V.transpose, T.tt[:, a:a + n], T.pb[:, 512 * h + 16:512 * h + 16 + n])
-        op("v", "pb%d" % h, "tt", V.transpose, T.tt[:, C + 192 * h:C + 192 * h + 192], T.pb[:, 512 * h:512 * h + 192])
-
-    def halve(r, h):
-        a, n = XH[h]
-        for b in range(4):
-            act("xp%d%d" % (r, h), "xh%d%d" % (h, b), T.xh[:, C * b + a:C * b + a + n], T["xp%d" % r][:, 64 + 4 * a + b:64 + 4 * a + 4 * n:4], scale=0.5)
-
     def F(l):
         return T.fl[:, 22 * l:22 * l + 22]
 
+    def rows_bank(i):
+        return "pb%d" % (2 + i), T.pb[:, 1024 + 512 * i:1024 + 512 * i + C]
+
+    S2 = "s20 s21 s22 s23 "
+
+    def step(r, name):
+        n, q = (name.split(".") + [None])[0:2]
+        x = [int(ch) for ch in n if ch.isdigit()]
+        sn, ns, XP = T["sn%d" % r], T["sn%d" % min(r + 1, 3)], T["xp%d" % r]
+        L = slice(15, C, 16)
+        if n in ("s0", "s1"):
+            scores(x[0])
+        elif n in ("m1", "m6"):
+            i = ROWS.index(x[0])
+            k, o = rows_bank(i)
+            mm("ur%d urs%d xq0 xq1" % (i, i), k, o, T.urq[:, 128 * i:128 * i + 128], T.urs[:, 128 * i:128 * i + 128], T.xq[:, 16:368], T.xs[:, 16:368])
+        elif n in ("b1", "b6"):
+            k, o = rows_bank(ROWS.index(x[0]))
+            act(k, n, T[n][:, :], o, AF.Sign, bias=-2.0 ** -93)
+        elif n in ("tr0", "tr1"):
+            h = x[0]
+            a, m = ((0, 192), (192, 160))[h]
+            op("v", "pb%d" % h, "tt", V.transpose, T.tt[:, a:a + m], T.pb[:, 512 * h + 16:512 * h + 16 + m])
+        elif n in ("ts0", "ts1"):
+            h = x[0]
+            op("v", "pb%d" % h, "tt", V.transpose, T.tt[:, C + 192 * h:C + 192 * h + 192], T.pb[:, 512 * h:512 * h + 192])
+        elif n == "fm":
+            ts("tt gl", "fm", T.fm[:, 1:320:2], T.tt[:, :].indirect(T.gl[:, :]), 0.0, None, OP.is_gt)
+        elif n == "fo":
+            scan("fm fbc fbd fb fb1 fb2 fb3", "fo", T.fo[:, :], T.fm[:, 0:308], T.fb[:, :])
+        elif n == "fl":
+            cp("fo", "fl", T.fl[:, :], T.fo[:, 45:308:2])
+        elif n[0:2] == "xh":
+            times(q, "xp%d0 xp%d1" % (r, r), n, plane(T.xh, x[0]), XP[:, 64 + x[0]:1472:4], 0.5)
+        elif n == "la":
+            ts("cw fl", "la", T.la[:, :], T.cw[:, :].indirect(F(2)), 1.0, None, OP.add)
+        elif n == "lb":
+            tten("la fl b1", "lb", T.lb[:, :], T.la[:, :].indirect(F(1)), T.b1[:, :], OP.add)
+        elif n == "lm":
+            cp("lb fl", "lm", T.lm[:, :], T.lb[:, :].indirect(F(0)))
+        elif n in ("ln", "hn"):
+            hold("lm mx", "ln", T.ln[:, :], T.mx[:, :], T.lm[:, :])
+        elif n in ("i3", "i6"):
+            ts("ln cg5", n, T[n][:, :], T.ln[:, L], 1.0 / 32, cg[:, 5:6], OP.mult, OP.add)
+        elif n in ("vi", "vj"):
+            cp("ln", n, T[n][:, :], T.ln[:, L])
+        elif n == "ha":
+            act("cw fl", "ha", T.ha[:, 0:C], T.cw[:, :].indirect(F(5)))
+        elif n == "ha2":
+            act("ha", "ha2", T.ha[:, C:704], T.ha[:, 0:C], AF.Identity, bias=8.0)
+        elif n == "hc":
+            act("ha ha2 fl", "hc", T.hc[:, 0:C], T.ha[:, :].indirect(F(4)))
+        elif n == "hc2":
+            act("hc", "hc2", T.hc[:, C:704], T.hc[:, 0:C], AF.Identity, bias=2.0)
+        elif n == "hd":
+            act("hc hc2 fl", "hd", T.hd[:, :], T.hc[:, :].indirect(F(3)))
+        elif n == "hm":
+            times(q, "hd i3", "lm", T.lm[:, :], T.hd[:, :].indirect(T.i3[:, :]))
+        elif n[0:2] == "va":
+            k, sh, m = (("vi", 1, 1), ("vi", 1, 2), ("vj", 1, 1), ("vj", 2, 3))[x[0]]
+            ts(k, n, T.va[:, 22 * x[0]:22 * x[0] + 22], T[k][:, :], sh, m, OP.logical_shift_right, OP.bitwise_and)
+        elif n[0:2] == "pw":
+            times(q, "cb pl%d" % r, n, plane(T.pw, x[0]), T.cb[:, :].indirect(T["pl%d" % r][:, 22 * x[0]:22 * x[0] + 22]))
+        elif n in ("t0", "t1", "t2", "t3"):
+            a, b = x[0] >> 1, x[0] & 1
+            times(q, "pw%d pl%d" % (1 - b, r), "s2%d" % x[0], T.s2[:, x[0]:1408:4], plane(T.pw, 1 - b).indirect(T["pl%d" % r][:, 22 * (1 - a):22 * (2 - a)]), 4.0)
+        elif n == "ki":
+            tten("va0 fo", "ki", T.ki[:, :], T.va[:, 0:22], T.fo[:, 1:44:2], OP.add)
+        elif n == "k0":
+            cp("ki", "k0", T.k0[:, :], T.ki[:, :])
+        elif n in ("g0", "g2", "g4"):
+            tten(S2 + "k%d m16" % x[0], "km", T.km[:, :], T.s2[:, :].indirect(T["k%d" % x[0]][:, :]), T.m16[:, :], OP.mult)
+            if x[0]:
+                scan("km r16", "ksn", T.ksn[:, :], T.r16[:, :], T.km[:, :])
+        elif n == "h0":
+            scan("km r16", "ksn", T.ksn[:, :], T.r16[:, :], T.km[:, :])
+        elif n == "kb":
+            tten("ksn va1", "kb", T.kb[:, :], T.ksn[:, L], T.va[:, 22:44], OP.add)
+        elif n == "k2":
+            tten("kb va2", "ki", T.ki[:, :], T.kb[:, :], T.va[:, 44:66], OP.add)
+            ts("ki", "k2", T.k2[:, :], T.ki[:, :], 704.0, None, OP.add)
+        elif n == "k4":
+            tten("ksn va3", "ki", T.ki[:, :], T.ksn[:, L], T.va[:, 66:88], OP.add)
+            ts("ki", "k4", T.k4[:, :], T.ki[:, :], 704.0, None, OP.add)
+        elif n == "k6":
+            ts("ksn", "k6", T.k6[:, :], T.ksn[:, L], 0.25, 176.0, OP.mult, OP.add)
+        elif n[0:2] == "gi":
+            act("xh%d i6" % x[0], n, T.gi[:, x[0]:1408:4], plane(T.xh, x[0]).indirect(T.i6[:, :]))
+        elif n[0] == "z":
+            a, m = PART[x[0]]
+            for b in x[1:] or range(4):
+                v = slice(4 * a + b, 4 * a + 4 * m, 4)
+                tten("xh%d k6 gi%d" % (b, b), "z%d" % x[0], T.z[:, v], plane(T.xh, b).indirect(T.k6[:, a // 16:(a + m) // 16]), T.gi[:, v], OP.add)
+        elif n in ("q0", "q1"):
+            a, m = PART[x[0]]
+            op("v", "z%d" % x[0], "zq%d" % x[0], V.quantize_mx, T.zq[:, a:a + m], T.zs[:, a:a + m], T.z[:, 4 * a:4 * a + 4 * m])
+            for b in range(4):
+                k, o = bank(x[0], b)
+                mm("wq wp zq%d" % x[0], k, o, T.wq[:, 128 * b:128 * b + 128], T.wp[:, 128 * b:128 * b + 128], T.zq[:, a:a + m], T.zs[:, a:a + m])
+        elif n[0] == "c":
+            a, m = PART[x[0]]
+            k, i = bank(x[0], x[1])
+            times(q, k, "hb%d%d" % (x[0], x[1]), T.hb[:, 4 * a + x[1]:4 * a + 4 * m:4], i, 0.03125)
+        elif n in ("h0q", "h1q"):
+            a, m = PART[x[0]]
+            op("v", " ".join("hb%d%d" % (x[0], b) for b in range(4)), "hq%d%d" % (r, x[0]), V.quantize_mx, T["hq%d" % r][:, a:a + m],
+               T["hs%d" % r][:, a:a + m], T.hb[:, 4 * a:4 * a + 4 * m])
+            send_part(r, x[0])
+        elif n == "en":
+            act("b6 k6", "en", T.en[:, :], T.b6[:, :].indirect(T.k6[:, :]))
+        elif n == "dd":
+            tten("en", "dd", T.dd[:, :], T.en[:, 0:C:2], T.en[:, 1:C:2], OP.mult)
+        elif n == "dn":
+            hold("dd m8", "dn", T.dn[:, :], T.m8[:, :], T.dd[:, :])
+        elif n == "tf":
+            ts("dn cg3 cg4", "tf", T.tf[:, :], T.dn[:, 7:176:8], cg[:, 3:4], cg[:, 4:5], OP.is_lt, OP.mult)
+        elif n == "tg":
+            tten("tf cl", "tg", T.tg[:, :], T.tf[:, :], T.cl[:, 0:22], OP.add)
+        elif n == "tl":
+            cp("tg", "tl", T.tl[:, :], T.tg[:, :])
+        elif n in ("u0", "u1"):
+            times(q, "pw%d tl" % (1 - x[0]), "uw%d" % x[0], plane(T.uw, x[0]), plane(T.pw, 1 - x[0]).indirect(T.tl[:, :]))
+        elif n == "n0":
+            tten("uw0 sn%d m16" % r, "km", T.km[:, :], T.uw[:, 0:C].indirect(sn[:, 0:22]), T.m16[:, :], OP.mult)
+        elif n == "n1" and r < 2:
+            act("uw1 sn%d" % r, "t1", T.t1[:, :], T.uw[:, C:704].indirect(sn[:, 22:44]))
+        elif n == "ns0":
+            scan("km r16", "ksn", T.ksn[:, :], T.r16[:, :], T.km[:, :])
+            ts("ksn", "tx", ns[:, 0:22], T.ksn[:, L], 176.0, None, OP.add)
+        elif n == "ns1" and r < 2:
+            hold("t1 mx", "kh", T.kh[:, :], T.mx[:, :], T.t1[:, :])
+            ts("kh cg2 tx", "sn%d" % (r + 1), ns[:, 22:44], T.kh[:, L], cg[:, 2:3], None, OP.add)
+            send_list(r + 1)
+            own_lists(r + 1)
+        elif n[0] == "e" and x:
+            a, m = PART[x[0]]
+            for b in x[1:] or range(4):
+                k, ps = bank(x[0], b)
+                mm("eq dq%d%d" % (r, x[0]), k, ps, T.eq[:, 128 * b:128 * b + 128], T.es[:, 128 * b:128 * b + 128],
+                   T["dq%d" % r][:, a:a + m], T["ds%d" % r][:, a:a + m])
+        elif n[0] == "d" and len(x) == 2:
+            a, m = PART[x[0]]
+            k, ps = bank(x[0], x[1])
+            times(q, k, "dw%d%d" % (x[0], x[1]), T.dw[:, C * x[1] + a:C * x[1] + a + m], ps)
+        elif n[0] == "x":
+            a, m = XH[x[0]]
+            for b in x[1:] or range(4):
+                v = slice(64 + 4 * a + b, 64 + 4 * a + 4 * m, 4)
+                tten("tx xp%d%d dw0%d dw1%d" % (r - 1, x[0], b, b), "xp%d%d" % (r, x[0]), XP[:, v],
+                     plane(T.dw, b).indirect(sn[:, a // 16:(a + m) // 16]), T["xp%d" % (r - 1)][:, v], OP.add)
+        elif n[0:2] == "qx":
+            qx(r, x[0])
+        elif n[0:2] == "fb":
+            repeat_lists(x[0])
+        elif n == "r6":
+            pick_rows(1, 128, 128)
+        elif n == "mx":
+            act("m16", "mx", T.mx[:, :], T.m16[:, :], AF.Identity, scale=-BIG - KM, bias=KM)
+        elif n == "kc":
+            act("jj", "cb", T.cb[:, :], T.jj[:, :], AF.Identity, bias=-176.0)
+        elif n == "m8":
+            act("dd", "m8", T.m8[:, :], T.dd[:, :], AF.Identity, scale=-132.0, bias=4.0)
+        elif n == "r16":
+            op("v", "r16o", "r16", V.memset, T.r16[:, 0:C:16], 0.0)
+        elif n == "eq":
+            op("v", "eb", "eq", V.quantize_mx, T.eq[:, :], T.es[:, :], T.eb[:, :])
+
+    def run(r, names):
+        for name in names.split():
+            step(r, name)
+
+    def pick_rows(i, a, n):
+        cp("uq url", "ur%d" % i, T.urq[:, a:a + n].bitcast(dt.uint32), T.uq[:, :].bitcast(dt.uint32).indirect(T.url[:, a // 16:(a + n) // 16]))
+        act("uq url", "urs%d" % i, T.urs[:, a:a + n], T.us[:, :].indirect(T.url[:, a // 16:(a + n) // 16]))
+
+    send_list(0)
+    op("v", "ub", "uq", V.quantize_mx, T.uq[:, :], T.us[:, :], T.ub[:, :])
+    iota("jj", T.jj[:, :], [[1, C]], 0, 0)
+    run(0, "qx0 s0")
+    pick_rows(0, 0, 128)
+    run(0, "qx1 s1")
+    score_list()
+    act("lm", "dd", T.dd[:, :], T.lm[:, 0:176], AF.Relu, scale=-1.0, bias=1.0)
+    run(0, "fb0 mx fb1 fb2")
     act("jj", "cw", T.cw[:, 0:C], T.jj[:, :], scale=32.0)
     act("jj", "cw", T.cw[:, C:704], T.jj[:, :], AF.Identity, scale=32.0, bias=4.0)
-    act("jj", "cb", T.cb[:, :], T.jj[:, :], AF.Identity, bias=-176.0)
-    own_lists(0)
-    repeat_lists()
-    qx(0, 0)
-    scores(0)
-    cp("uq url", "ur", T.urq[:, :].bitcast(dt.uint32), T.uq[:, :].bitcast(dt.uint32).indirect(T.url[:, :]))
-    act("uq url", "urs", T.urs[:, :], T.us[:, :].indirect(T.url[:, :]))
-    qx(0, 1)
     dma("s", "d_w", "xp00 xp01 ub", "wq", T.wq[:, :].bitcast(dt.uint8), T.wc[:, :])
     dma("s", "d_wp", "", "wp", T.wp[:, :], T.ws[:, :])
     dma("s", "d_v", "", "vb", T.vb[:, :], T.v[:, :])
-    op("g", "", "one", g.iota, T.one[:, :], [[0, 512]], 1, 0, allow_small_or_imprecise_dtypes=True)
+    iota("r16o", T.r16[:, :], [[0, C]], 1, 0)
+    for r in (1, 2):
+        iota("pad%d" % r, T["xp%d" % r][:, 0:64], [[0, 64]], 0, 0)
+        iota("pad%d" % r, T["xp%d" % r][:, 1472:1536], [[0, 64]], 0, 0)
+    iota("one", T.one[:, :], [[0, 512]], 1, 0)
     for b in range(4):
         op("g", "one", "eb", g.affine_select, T.eb[:, 512 * b:512 * b + 512], T.one[:, :], [[-1, 512]], OP.is_equal, 0.0, b, 4)
 
     for r in range(3):
-        XP = T["xp%d" % r]
-        scores(1)
-        for i in range(2):
-            mm("ur urs xq0 xq1", "pb%d" % (2 + i), T.pb[:, 1024 + 512 * i:1024 + 512 * i + C], T.urq[:, 128 * i:128 * i + 128], T.urs[:, 128 * i:128 * i + 128],
-               T.xq[:, 16:368], T.xs[:, 16:368])
-        turn(0)
-        turn(1)
-        ts("tt gl", "fm", T.fm[:, 1:320:2], T.tt[:, :].indirect(T.gl[:, :]), 0.0, None, OP.is_gt)
-        scan("fm fbc fb fb1 fb2 fb3", "fo", T.fo[:, :], T.fm[:, 0:308], T.fb[:, :])
-        cp("fo", "fl", T.fl[:, :], T.fo[:, 45:308:2])
-        act("pb2", "b1", T.b1[:, :], T.pb[:, 1024:1024 + C], AF.Sign, bias=-2.0 ** -93)
-        if r == 0:
-            halve(0, 0)
-        else:
-            table(r, 2, "a")
-        act("cw fl", "ha", T.ha[:, 0:C], T.cw[:, :].indirect(F(5)))
-        ts("cw fl", "la", T.la[:, :], T.cw[:, :].indirect(F(2)), 1.0, None, OP.add)
-        act("ha", "ha2", T.ha[:, C:704], T.ha[:, 0:C], AF.Identity, bias=8.0)
-        tten("la fl b1", "lb", T.lb[:, :], T.la[:, :].indirect(F(1)), T.b1[:, :], OP.add)
-        act("ha ha2 fl", "hc", T.hc[:, 0:C], T.ha[:, :].indirect(F(4)))
-        if r == 0:
-            ts("j16 cf", "m16", T.m16[:, :], T.j16[:, :], PR, None, OP.is_equal)
-        tten("lb fl m16", "lm", T.lm[:, :], T.lb[:, :].indirect(F(0)), T.m16[:, :], OP.mult)
-        act("hc", "hc2", T.hc[:, C:704], T.hc[:, 0:C], AF.Identity, bias=1.0)
-        scan("lm r16", "ln", T.ln[:, :], T.r16[:, :], T.lm[:, :])
-        act("hc hc2 fl", "hd", T.hd[:, :], T.hc[:, :].indirect(F(3)))
-        ts("ln", "i3", T.i3[:, :], T.ln[:, 15:C:16], 1.0 / 32, None, OP.mult)
-        cp("ln", "vi", T.vi[:, :], T.ln[:, 15:C:16])
-        act("hd i3", "hm", T.hm[:, :], T.hd[:, :].indirect(T.i3[:, :]))
-        if r == 0:
-            ts("m16", "mx", T.mx[:, :], T.m16[:, :], -BIG - KM, KM, OP.mult, OP.add)
-            window(0)
-        ts("vi", "va0", T.va[:, 0:22], T.vi[:, :], 1, 1, OP.logical_shift_right, OP.bitwise_and)
-        ts("vi", "va1", T.va[:, 22:44], T.vi[:, :], 1, 2, OP.logical_shift_right, OP.bitwise_and)
-        tten("va0 fo", "ki", T.ki[:, :], T.va[:, 0:22], T.fo[:, 1:44:2], OP.add)
-        cp("ki", "k0", T.k0[:, :], T.ki[:, :])
-
-        def second(j):
-            tten(S2 + "k%d m16" % j, "km", T.km[:, :], T.s2[:, :].indirect(T["k%d" % j][:, :]), T.m16[:, :], OP.mult)
-            scan("km r16", "ksn", T.ksn[:, :], T.r16[:, :], T.km[:, :])
-
-        def onward(j):
-            k, e = ("kb", T.kb[:, :]) if j == 0 else ("va3", T.va[:, 66:88])
-            tten("ksn " + k, "ki", T.ki[:, :], T.ksn[:, 15:C:16], e, OP.add)
-            ts("ki", "k%d" % (j + 2), T["k%d" % (j + 2)][:, :], T.ki[:, :], 704.0, None, OP.add)
-
-        if r > 0:
-            table(r, 3, "v")
-            second(0)
-        else:
-            table(r, 0, "a")
-            table(r, 1, "a")
-        halve(r, 1)
-        hold("hm mx", "hn", T.hn[:, :], T.mx[:, :], T.hm[:, :])
-        ts("hn cg1", "i6", T.i6[:, :], T.hn[:, 15:C:16], 1.0 / 32, cg[:, 1:2], OP.mult, OP.add)
-        cp("hn", "vj", T.vj[:, :], T.hn[:, 15:C:16])
-        if r == 0:
-            ts("j16 cf", "m8", T.m8[:, :], T.j16[:, 0:C:2], PE, None, OP.is_equal)
-            op("v", "eb", "eq", V.quantize_mx, T.eq[:, :], T.es[:, :], T.eb[:, :])
-            ts("m8", "m8", T.m8[:, :], T.m8[:, :], -132.0, 4.0, OP.mult, OP.add)
-            table(r, 3, "v")
-        ts("vj", "va2", T.va[:, 44:66], T.vj[:, :], 1, None, OP.bitwise_and)
-        ts("vj", "va3", T.va[:, 66:88], T.vj[:, :], 2, 3, OP.logical_shift_right, OP.bitwise_and)
-        tten("va1 va2", "kb", T.kb[:, :], T.va[:, 22:44], T.va[:, 44:66], OP.add)
-        if r == 0:
-            table(r, 2, "v")
-            second(0)
-        for h in range(2):
-            a, n = PART[h]
-            for b in range(4):
-                act("xh0%d xh1%d i6" % (b, b), "gi%d%d" % (h, b), T.gi[:, 4 * a + b:4 * a + 4 * n:4], plane(T.xh, b).indirect(T.i6[:, a // 16:(a + n) // 16]))
-        act("pb3", "b6", T.b6[:, :], T.pb[:, 1536:1536 + C], AF.Sign, bias=-2.0 ** -93)
-        for j in (0, 2):
-            onward(j)
-            second(j + 2)
-        ts("ksn", "k6", T.k6[:, :], T.ksn[:, 15:C:16], 0.25, 176.0, OP.mult, OP.add)
-
-        def mosaic(h):
-            a, n = PART[h]
-            for b in range(4):
-                v = slice(4 * a + b, 4 * a + 4 * n, 4)
-                tten("xh0%d xh1%d k6 gi%d%d" % (b, b, h, b), "z%d" % h, T.z[:, v], plane(T.xh, b).indirect(T.k6[:, a // 16:(a + n) // 16]), T.gi[:, v], OP.add)
-            op("v", "z%d" % h, "zq%d" % h, V.quantize_mx, T.zq[:, a:a + n], T.zs[:, a:a + n], T.z[:, 4 * a:4 * a + 4 * n])
-            for b in range(4):
-                k, o = bank(h, b)
-                mm("wq wp zq%d" % h, k, o, T.wq[:, 128 * b:128 * b + 128], T.wp[:, 128 * b:128 * b + 128], T.zq[:, a:a + n], T.zs[:, a:a + n])
-
-        def hcast(h, b, q):
-            a, n = PART[h]
-            k, i = bank(h, b)
-            o = T.hb[:, 4 * a + b:4 * a + 4 * n:4]
-            if q == "a":
-                act(k, "hb%d%d" % (h, b), o, i, scale=0.03125)
-            else:
-                ts(k, "hb%d%d" % (h, b), o, i, 0.03125, None, OP.mult)
-
-        def qh(h):
-            a, n = PART[h]
-            op("v", " ".join("hb%d%d" % (h, b) for b in range(4)), "hq%d%d" % (r, h), V.quantize_mx, T["hq%d" % r][:, a:a + n],
-               T["hs%d" % r][:, a:a + n], T.hb[:, 4 * a:4 * a + 4 * n])
-            send_part(r, h)
-
-        mosaic(0)
-        act("b6 k6", "en", T.en[:, :], T.b6[:, :].indirect(T.k6[:, :]))
-        for b in range(4):
-            hcast(0, b, "a")
-        mosaic(1)
-        qh(0)
-        hcast(1, 0, "a")
-        hcast(1, 1, "v")
-        hcast(1, 2, "a")
-        hcast(1, 3, "v")
-        qh(1)
-        sn, ns = T["sn%d" % r], T["sn%d" % (r + 1)]
-        tten("en", "dd", T.dd[:, :], T.en[:, 0:C:2], T.en[:, 1:C:2], OP.mult)
-        hold("dd m8", "dn", T.dn[:, :], T.m8[:, :], T.dd[:, :])
-        ts("dn cg3 cg4", "tf", T.tf[:, :], T.dn[:, 7:176:8], cg[:, 3:4], cg[:, 4:5], OP.is_lt, OP.mult)
-        tten("tf cl", "tg", T.tg[:, :], T.tf[:, :], T.cl[:, 0:22], OP.add)
-        cp("tg", "tl", T.tl[:, :], T.tg[:, :])
-        cp("pw tl", "uw0", T.uw[:, 0:C], T.pw[:, C:704].indirect(T.tl[:, :]))
-        act("pw tl", "uw1", T.uw[:, C:704], T.pw[:, 0:C].indirect(T.tl[:, :]))
-        tten("uw0 sn%d m16" % r, "km", T.km[:, :], T.uw[:, 0:C].indirect(sn[:, 0:22]), T.m16[:, :], OP.mult)
-        if r < 2:
-            act("uw1 sn%d" % r, "t1", T.t1[:, :], T.uw[:, C:704].indirect(sn[:, 22:44]))
-        scan("km r16", "ksn", T.ksn[:, :], T.r16[:, :], T.km[:, :])
-        ts("ksn", "tx%d" % r, ns[:, 0:22], T.ksn[:, 15:C:16], 176.0, None, OP.add)
-        if r < 2:
-            hold("t1 mx", "hn", T.hn[:, :], T.mx[:, :], T.t1[:, :])
-            ts("hn cg2 tx%d" % r, "sn%d" % (r + 1), ns[:, 22:44], T.hn[:, 15:C:16], cg[:, 2:3], None, OP.add)
-            send_list(r + 1)
-            own_lists(r + 1)
-        else:
+        run(r, (BITS if r else BITS0) + PATH + (PATH1 if r else PATH0) + SECOND + LAYER + "eq " * (r == 0) + TURNS)
+        if r == 2:
             op("v", "vb", "vq", V.quantize_mx, T.vq[:, :], T.vs[:, :], T.vb[:, :])
-        hp = route(topo, partner(r), core)
-        for h in range(2):
-            a, n = PART[h]
-            arrived("dq%d%d" % (r, h), ("ca%d", "cb%d")[h] % r, sum(len(topo.engines(hp[k], core)) for k in CODES[h] + (SCALES[h],)))
-            for b in range(4):
-                k, ps = bank(h, b)
-                mm("eq dq%d%d" % (r, h), k, ps, T.eq[:, 128 * b:128 * b + 128], T.es[:, 128 * b:128 * b + 128],
-                   T["dq%d" % r][:, a:a + n], T["ds%d" % r][:, a:a + n])
-            for b in range(4):
-                k, ps = bank(h, b)
-                o = T.dw[:, C * b + a:C * b + a + n]
-                if h == 0 or b > 0:
-                    act(k, "dw%d%d" % (h, b), o, ps)
-                else:
-                    cp(k, "dw%d%d" % (h, b), o, ps)
+        run(r, NEWX if r < 2 else NEWX.replace("fb0 ", "").replace("fb1 ", ""))
         if r < 2:
-            repeat_lists()
-            window(r + 1)
-        else:
-            for b in range(2):
-                act("uw%d sn2" % b, "tw", T.tw[:, C * b:C * b + C], T.uw[:, C * b:C * b + C].indirect(sn[:, 22 * b:22 * b + 22]), AF.Identity, bias=176.0)
-            dma("s", "d_so", "tw", "so", T.so[:, :], T.tw[0:128:16, :])
-        for h in range(2):
-            a, n = XH[h]
-            for b in range(4):
-                v = slice(64 + 4 * a + b, 64 + 4 * a + 4 * n, 4)
-                tten("tx%d xp%d%d dw0%d dw1%d" % (r, r, h, b, b), "xp%d%d" % (r + 1, h), T["xp%d" % (r + 1)][:, v],
-                     plane(T.dw, b).indirect(ns[:, a // 16:(a + n) // 16]), XP[:, v], OP.add)
-            qx(r + 1, h)
-            if r < 2:
-                if h == 0:
-                    scores(0)
-                    halve(r + 1, 0)
-                    table(r + 1, 0, "a")
-                    table(r + 1, 1, "a")
-            else:
-                q = slice(16 + a, 16 + a + n)
-                mm("vq xq%d" % h, "pa%d" % h, T.pa[:, 512 * h:512 * h + n], T.vq[:, :], T.vs[:, :], T.xq[:, q], T.xs[:, q])
-                dma("s", "d_oc", "xq%d" % h, "oc%d" % h, T.oc[:, 4 * a:4 * a + 4 * n], T.xq[:, q].bitcast(dt.uint8))
-                act("pa%d" % h, "yb%d" % h, T.yb[:, a:a + n], T.pa[:, 512 * h:512 * h + n])
-                dma("a", "d_y", "yb%d" % h, "y%d" % h, T.y[:, a:a + n], T.yb[:, a:a + n])
+            run(r + 1, NEXT)
+    for b in range(2):
+        act("uw%d sn2" % b, "tw", plane(T.tw, b), plane(T.uw, b).indirect(T.sn2[:, 22 * b:22 * b + 22]), AF.Identity, bias=176.0)
+    dma("s", "d_so", "tw", "so", T.so[:, :], T.tw[0:128:16, :])
+    for h in range(2):
+        run(3, "x%d qx%d" % (h, h))
+        a, n = XH[h]
+        q = slice(16 + a, 16 + a + n)
+        mm("vq xq%d" % h, "pa%d" % h, T.pa[:, 512 * h:512 * h + n], T.vq[:, :], T.vs[:, :], T.xq[:, q], T.xs[:, q])
+        dma("s", "d_oc", "xq%d" % h, "oc%d" % h, T.oc[:, 4 * a:4 * a + 4 * n], T.xq[:, q].bitcast(dt.uint8))
+        times("av"[h], "pa%d" % h, "yb%d" % h, T.yb[:, a:a + n], T.pa[:, 512 * h:512 * h + n])
+        dma("a", "d_y", "yb%d" % h, "y%d" % h, T.y[:, a:a + n], T.yb[:, a:a + n])
     for k in range(4):
         dma("s", "d_oc", "xq0 xq1", "osc%d" % k, T.osc[4 * k:4 * k + 4, :], T.xs[32 * k:32 * k + 4, 16:368])
     total["ls"] = sent[0]

@@ -4,8 +4,8 @@ from concourse.mybir import dt, AluOpType as OP, ActivationFunctionType as AF
 C = 352
 MASK = [2, 4, 1]
 PART = [(0, 192), (192, 160)]
-XH = [(0, 192), (192, 160)]
-KM, BIG = 16384.0, 1048576.0
+XH = [(0, 224), (224, 128)]
+KM, BIG = 32768.0, 2097152.0
 ROWS = [1, 6]
 BF, F32, I32, U16, U8, E4 = "bfloat16", "float32", "int32", "uint16", "uint8", "float8_e4m3fn_x4"
 SCRATCH = {
@@ -15,7 +15,7 @@ SCRATCH = {
     "urq": ("sbuf", [128, 384], E4), "urs": ("sbuf", [128, 384], U8),
     "pc": ("sbuf", [128, 8], I32), "ci": ("sbuf", [128, 8], I32), "cf": ("sbuf", [128, 8], F32), "cg": ("sbuf", [128, 8], F32),
     "cn": ("sbuf", [128, 4], F32),
-    "j16": ("sbuf", [128, C], F32), "jj": ("sbuf", [128, C], F32), "cw": ("sbuf", [128, 704], F32), "cb": ("sbuf", [128, C], BF),
+    "j16": ("sbuf", [128, C], F32), "cw": ("sbuf", [128, 704], F32), "cb": ("sbuf", [128, C], BF),
     "m16": ("sbuf", [128, C], BF), "r16": ("sbuf", [128, C], BF), "mx": ("sbuf", [128, C], BF), "m8": ("sbuf", [128, 176], BF),
     "cq": ("sbuf", [128, 24], F32), "cl": ("sbuf", [128, 24], F32), "ga": ("sbuf", [128, 10], I32), "gb": ("sbuf", [128, 10], F32),
     "ge": ("sbuf", [128, 10], F32), "gl": ("sbuf", [128, 10], U16), "url": ("sbuf", [128, 24], U16),
@@ -27,7 +27,7 @@ SCRATCH = {
     "la": ("sbuf", [128, C], F32), "lb": ("sbuf", [128, C], F32), "lm": ("sbuf", [128, C], F32), "ln": ("sbuf", [128, C], F32),
     "ha": ("sbuf", [128, 704], F32), "hc": ("sbuf", [128, 704], F32), "hd": ("sbuf", [128, C], F32),
     "i3": ("sbuf", [128, 22], U16), "i6": ("sbuf", [128, 22], U16), "vi": ("sbuf", [128, 22], I32), "vj": ("sbuf", [128, 22], I32),
-    "va": ("sbuf", [128, 88], I32),
+    "va": ("sbuf", [128, 88], I32), "y3": ("sbuf", [128, 22], F32),
     "pw": ("sbuf", [128, 704], BF), "s2": ("sbuf", [128, 1408], BF), "km": ("sbuf", [128, C], BF), "ksn": ("sbuf", [128, C], BF),
     "ku": ("sbuf", [128, C], BF), "kh": ("sbuf", [128, C], F32), "ki": ("sbuf", [128, 22], F32), "kb": ("sbuf", [128, 22], F32),
     "k0": ("sbuf", [128, 22], U16), "k2": ("sbuf", [128, 22], U16), "k4": ("sbuf", [128, 22], U16), "k6": ("sbuf", [128, 22], U16),
@@ -57,16 +57,17 @@ CODES = [(0, 1), (2, 3)]
 SCALES = [2, 0]
 LISTS = 3
 
-BITS = "s1 m1 m6 ts0 tr1 ts1 fm fo fl t2.a b1 t3.a "
-BITS0 = "m1 tr1 ts1 fm fo fl b1 kc "
-PATH = "ha la ha2 lb hc lm hc2 ln hd vi i3 hm.a va0 va1 ki "
-PATH1 = "k0 g0 hn xh0.a xh1.a xh2.a xh3.a h0 vj kb va2 i6 va3 "
-PATH0 = "k0 pw0.v pw1.a hn r16 vj i6 va2 va3 t0.a t1.v t2.a t3.v xh0.a xh1.a r6 m6 g0 xh2.v h0 xh3.v kb m8 "
-SECOND = "gi0 gi1 gi2 gi3 b6 k2 g2 k4 g4 k6 en "
-LAYER = "z0 z10 q0 c00.a c01.a c02.a z11 z12 z13 dd q1 dn c03.v tf h0q tg c10.a c11.v tl c12.a c13.v h1q "
-TURNS = "u0.v u1.a n0 n1 ns0 ns1 "
-NEWX = "e0 fb0 fb1 d00.v d01.a d02.v d03.a e1 d10.v d11.a d12.a d13.a "
-NEXT = "pw0.a pw1.a fb2 x0 x10 qx0 s0 t0.a t1.a x11 x12 x13 qx1 tr0"
+BITS = "s1 m1 m6 ts0 tr1 ts1 fm xh0.v fo xh1.v fl t2.a b1 t3.a "
+BITS0 = "m1 tr0 ts0 tr1 ts1 fm xh0.v fo xh1.v fl b1 kc "
+PATH = "ha la ha2 lb hc lm hc2 ln hd "
+PATH1 = "vi i3 hm xh2.a xh3.a b6 va0 va1 p0 k0 g0 hn h vj y3 kb va2 p2 i6 k2 va3 "
+PATH0 = "i3 vi pw0.v hm va0 pw1.v va1 p0 t1.v k0 t0.a t2.a hn t3.v vj y3 g0 va2 h i6 va3 r6 m6 xh2.a xh3.a kb w0 b6 p2 w1 k2 "
+SECOND = "g2B.a g2A gi0 gi1 w2 hA w3 p4A hB.a k4A p4B.a g4A k4B.a gi2 gi3 m8 hA g4B k6A hB z00 k6B en "
+LAYER = "z01 z02 z03 z10 q0 c00.a c01.a c02.a z11 z12 z13 q1 c03.v dd h0q dn c10.a c11.v tf c12.a c13.v tg h1q tl "
+LAYER2 = "z01 z02 z03 z10 q0 c00.a c01.a c02.a z11 z12 z13 q1 c03.v h0q c10.a dd c11.v c12.a c13.v h1q dn vq tf tg tl "
+TURNS = "u0.v u1.a n0 n1 h nh ns0 ns1 "
+NEXT = "sf sd e00 e01 e02 e10 e11 e03 e12 e13 fb0.a d00.v d01.a d02.v fb1.a d10.v d11.a d12.a d03.a d13.a pw0.a pw1.a fb2.a x0 x10 qx0 s0 t0.a t1.a x11 x12 x13 qx1 tr0 "
+LAST = "e00 e01 e02 e10 e11 e03 e12 e13 d00.v d01.a d02.a d10.v d11.v d12.a d03.a d13.a "
 
 
 def route(topo, core, dst):
@@ -209,8 +210,8 @@ def rank_program(g, core, T, topo):
 
     dma("s", "d_se", "", "sei", T.sei[:, :], T.se[:, :])
     dma("a", "d_u", "", "ub", T.ub[:, :], T.u[:, :])
-    dma("s", "d_x", "", "xp00", T.xp0[:, 64:832], T.x[:, 0:768])
-    dma("a", "d_x2", "", "xp01", T.xp0[:, 832:1472], T.x[:, 768:1408])
+    dma("s", "d_x", "", "xp00", T.xp0[:, 64:64 + 4 * XH[1][0]], T.x[:, 0:4 * XH[1][0]])
+    dma("a", "d_x2", "", "xp01", T.xp0[:, 64 + 4 * XH[1][0]:1472], T.x[:, 4 * XH[1][0]:1408])
     op("g", "", "pc", g.iota, T.pc[:, 0:1], [[0, 1]], 0, 1)
     iota("cq", T.cq[:, :], [[16, 24]], 0, 0)
     iota("j16", T.j16[:, :], [[0, 22], [1, 16]], 0, 0)
@@ -230,25 +231,19 @@ def rank_program(g, core, T, topo):
     ts("cq cf", "cl", T.cl[:, :], T.cq[:, :], PR, None, OP.add)
     ts("cf", "cg0", cg[:, 0:1], PH, PP, 368.0, OP.not_equal, OP.mult)
     ts("cf", "cn", T.cn[:, :], cf[:, 0:4], -1.0, None, OP.mult)
-    for i, (p, a, b) in enumerate(((PR, KM, 176 - 15 * KM), (PE, -2.0, 28.0), (PP, -2.0, 1.0), (PR, KM / 32, -15 * KM / 32))):
-        act("cf", "cg%d" % (i + 2), cg[:, i + 2:i + 3], p, AF.Identity, scale=a, bias=b)
+    columns = ((PR, -KM, 15.5 * KM), (PR, KM, 176 - 15 * KM), (PE, -2.0, 28.0), (PP, -2.0, 1.0), (PR, KM / 32, -15 * KM / 32),
+               (PR, KM, 704 - 15 * KM), (PR, KM / 4, 176 - 15 * KM / 4))
+    for i in (0, 4, 5, 6):
+        act("cf", "cg%d" % (i + 1), cg[:, i + 1:i + 2], columns[i][0], AF.Identity, scale=columns[i][1], bias=columns[i][2])
+    act("j16 cn", "lnA lnB", T.ln[:, :], T.j16[:, :], AF.Abs, bias=T.cn[:, 0:1])
     act("cl", "fbd", T.fb[:, 1:44:2], T.cl[:, 0:22], scale=4.0)
-    act("j16 cn", "ln", T.ln[:, :], T.j16[:, :], AF.Abs, bias=T.cn[:, 0:1])
-    act("j16 cn", "lm", T.lm[:, 0:176], T.j16[:, 0:C:2], AF.Abs, bias=T.cn[:, 3:4])
-    act("ln", "m16", T.m16[:, :], T.ln[:, :], AF.Relu, scale=-1.0, bias=1.0)
+    act("lnA lnB", "m16", T.m16[:, :], T.ln[:, :], AF.Relu, scale=-1.0, bias=1.0)
     ts("cl", "ga", T.ga[:, :], T.cl[:, 0:10], 1.0 / 22, -0.477, OP.mult, OP.add)
     ts("cl cg0", "ge", T.ge[:, :], T.cl[:, 0:10], 16.0, cg[:, 0:1], OP.mult, OP.add)
+    ts("ga", "gb", T.gb[:, :], T.ga[:, :], -351.0, -1.0, OP.mult, OP.add)
+    ts("ga", "ga0", T.cq[:, 10:20], T.ga[:, :], 0.0, None, OP.is_equal)
     cp("sei", "sn0", T.sn0[:, 0:44], T.sei[:, :])
-
-    def score_list():
-        ts("ga", "gb", T.gb[:, :], T.ga[:, :], -351.0, -1.0, OP.mult, OP.add)
-        ts("ga", "ga0", T.cq[:, 10:20], T.ga[:, :], 0.0, None, OP.is_equal)
-        own_lists(0)
-        tten("gb ge", "ge", T.ge[:, :], T.ge[:, :], T.gb[:, :], OP.add)
-        run(0, "tr0")
-        tten("ge ga0", "ge", T.ge[:, :], T.ge[:, :], T.cq[:, 10:20], OP.add)
-        run(0, "ts0")
-        cp("ge", "gl", T.gl[:, :], T.ge[:, :])
+    tten("gb ge", "ge", T.ge[:, :], T.ge[:, :], T.gb[:, :], OP.add)
 
     sent = [0]
 
@@ -259,7 +254,7 @@ def rank_program(g, core, T, topo):
         h = route(topo, core, partner(r))[LISTS]
         rid, pid = topo.addr(h, core)
         e = topo.engines(core, h)
-        need("g", ["sn%d" % r], [])
+        need("g", ["tx", "sn%d" % r], [])
         g.remote_dma(T["lh%d" % r][:, :], T["sn%d" % r][:, 0:44], T.sem["hl%d" % r], T.sem.ls, pid, rid, bits(e))
         sent[0] += len(e)
         arrived("pl%d" % r, "la%d" % r, len(topo.engines(route(topo, partner(r), core)[LISTS], core)))
@@ -285,21 +280,19 @@ def rank_program(g, core, T, topo):
         hp = route(topo, partner(r), core)
         arrived("dq%d%d" % (r, h), ("ca%d", "cb%d")[h] % r, sum(len(topo.engines(hp[k], core)) for k in CODES[h] + (SCALES[h],)))
 
-    def own_lists(r):
-        k = "sn%d" % r
-        cp(k, "sf", T.sf[:, :], T[k][:, 0:44])
-        tten("sf", "fb", T.fb[:, 44:88:2], T.sf[:, 22:44], T.sf[:, 0:22], OP.subtract)
-
-    def repeat_lists(i):
+    def repeat_lists(i, q):
         if i == 0:
-            act("sf", "fb1", T.fb[:, 45:88:2], T.sf[:, 0:22])
-            act("sf", "fb1", T.fb[:, 133:176:2], T.sf[:, 0:22])
-            act("fb", "fb1", T.fb[:, 132:176:2], T.fb[:, 44:88:2], AF.Identity, bias=352.0)
+            times(q, "sf", "fb1", T.fb[:, 45:88:2], T.sf[:, 0:22])
+            times(q, "sf", "fb1", T.fb[:, 133:176:2], T.sf[:, 0:22])
+            if q == "a":
+                act("fb", "fb1", T.fb[:, 132:176:2], T.fb[:, 44:88:2], AF.Identity, bias=352.0)
+            else:
+                ts("fb", "fb1", T.fb[:, 132:176:2], T.fb[:, 44:88:2], 352.0, None, OP.add)
         elif i == 1:
-            act("fb fb1", "fb2", T.fb[:, 88:132], T.fb[:, 44:88])
-            act("fb1", "fb2", T.fb[:, 176:220], T.fb[:, 132:176])
+            times(q, "fb fb1", "fb2", T.fb[:, 88:132], T.fb[:, 44:88])
+            times(q, "fb1", "fb2", T.fb[:, 176:220], T.fb[:, 132:176])
         else:
-            act("fb1 fb2", "fb3", T.fb[:, 220:308], T.fb[:, 132:220])
+            times(q, "fb1 fb2", "fb3", T.fb[:, 220:308], T.fb[:, 132:220])
 
     def bank(h, b):
         n = PART[h][1]
@@ -309,11 +302,13 @@ def rank_program(g, core, T, topo):
         return t[:, C * b:C * b + C]
 
     def qx(r, h):
-        a, n = ((0, 208), (208, 176))[h] if r < 3 else ((16, 192), (208, 160))[h]
+        a, n = 16 + XH[h][0], XH[h][1]
+        if r < 3:
+            a, n = a - 16 * (1 - h), n + 16
         op("v", "xp%d%d pad%d" % (r, h, r), "xq%d" % h, V.quantize_mx, T.xq[:, a:a + n], T.xs[:, a:a + n], T["xp%d" % r][:, 4 * a:4 * a + 4 * n])
 
     def scores(h):
-        a, n = ((0, 208), (192, 192))[h]
+        a, n = XH[h][0], XH[h][1] + 16 + 16 * h
         mm("uq xq0" + " xq1" * h, "pb%d" % h, T.pb[:, 512 * h:512 * h + n], T.uq[:, :], T.us[:, :], T.xq[:, a:a + n], T.xs[:, a:a + n])
 
     def F(l):
@@ -326,9 +321,19 @@ def rank_program(g, core, T, topo):
 
     def step(r, name):
         n, q = (name.split(".") + [None])[0:2]
+        parts = n[-1] if n[-1] in "AB" else "AB"
+        n = n.rstrip("AB")
         x = [int(ch) for ch in n if ch.isdigit()]
         sn, ns, XP = T["sn%d" % r], T["sn%d" % min(r + 1, 3)], T["xp%d" % r]
-        L = slice(15, C, 16)
+        lo, hi = (0 if "A" in parts else PART[1][0] // 16), (C // 16 if "B" in parts else PART[1][0] // 16)
+        Q, W, L = slice(lo, hi), slice(16 * lo, 16 * hi), slice(16 * lo + 15, 16 * hi, 16)
+
+        def K(k):
+            return "".join(k + p + " " for p in parts)
+
+        def VA(i):
+            return T.va[:, 22 * i + lo:22 * i + hi]
+
         if n in ("s0", "s1"):
             scores(x[0])
         elif n in ("m1", "m6"):
@@ -340,11 +345,12 @@ def rank_program(g, core, T, topo):
             act(k, n, T[n][:, :], o, AF.Sign, bias=-2.0 ** -93)
         elif n in ("tr0", "tr1"):
             h = x[0]
-            a, m = ((0, 192), (192, 160))[h]
+            a, m = XH[h]
             op("v", "pb%d" % h, "tt", V.transpose, T.tt[:, a:a + m], T.pb[:, 512 * h + 16:512 * h + 16 + m])
         elif n in ("ts0", "ts1"):
             h = x[0]
-            op("v", "pb%d" % h, "tt", V.transpose, T.tt[:, C + 192 * h:C + 192 * h + 192], T.pb[:, 512 * h:512 * h + 192])
+            a, m = XH[h][0], XH[h][1] + 32 * h
+            op("v", "pb%d" % h, "tt", V.transpose, T.tt[:, C + a:C + a + m], T.pb[:, 512 * h:512 * h + m])
         elif n == "fm":
             ts("tt gl", "fm", T.fm[:, 1:320:2], T.tt[:, :].indirect(T.gl[:, :]), 0.0, None, OP.is_gt)
         elif n == "fo":
@@ -358,13 +364,17 @@ def rank_program(g, core, T, topo):
         elif n == "lb":
             tten("la fl b1", "lb", T.lb[:, :], T.la[:, :].indirect(F(1)), T.b1[:, :], OP.add)
         elif n == "lm":
-            cp("lb fl", "lm", T.lm[:, :], T.lb[:, :].indirect(F(0)))
+            cp("lb fl", K("lm"), T.lm[:, W], T.lb[:, :].indirect(T.fl[:, Q]))
         elif n in ("ln", "hn"):
-            hold("lm mx", "ln", T.ln[:, :], T.mx[:, :], T.lm[:, :])
-        elif n in ("i3", "i6"):
-            ts("ln cg5", n, T[n][:, :], T.ln[:, L], 1.0 / 32, cg[:, 5:6], OP.mult, OP.add)
+            hold(K("lm") + "mx", K("ln"), T.ln[:, W], T.mx[:, W], T.lm[:, W])
+        elif n == "i3":
+            ts(K("ln") + "cg5", K(n), T.i3[:, Q], T.ln[:, L], 1.0 / 32, cg[:, 5:6], OP.mult, OP.add)
         elif n in ("vi", "vj"):
-            cp("ln", n, T[n][:, :], T.ln[:, L])
+            cp(K("ln"), K(n), T[n][:, Q], T.ln[:, L])
+        elif n == "y3":
+            ts(K("ln") + "cg1", K(n), T.y3[:, Q], T.ln[:, L], cg[:, 1:2], None, OP.is_ge)
+        elif n == "i6":
+            cp(K("va2"), K(n), T.i6[:, Q], VA(2))
         elif n == "ha":
             act("cw fl", "ha", T.ha[:, 0:C], T.cw[:, :].indirect(F(5)))
         elif n == "ha2":
@@ -372,46 +382,48 @@ def rank_program(g, core, T, topo):
         elif n == "hc":
             act("ha ha2 fl", "hc", T.hc[:, 0:C], T.ha[:, :].indirect(F(4)))
         elif n == "hc2":
-            act("hc", "hc2", T.hc[:, C:704], T.hc[:, 0:C], AF.Identity, bias=2.0)
+            act("hc", "hc2", T.hc[:, C:704], T.hc[:, 0:C], AF.Identity, bias=KM / 2)
         elif n == "hd":
             act("hc hc2 fl", "hd", T.hd[:, :], T.hc[:, :].indirect(F(3)))
         elif n == "hm":
-            times(q, "hd i3", "lm", T.lm[:, :], T.hd[:, :].indirect(T.i3[:, :]))
+            act("hd " + K("i3"), K("lm"), T.lm[:, W], T.hd[:, :].indirect(T.i3[:, Q]))
         elif n[0:2] == "va":
-            k, sh, m = (("vi", 1, 1), ("vi", 1, 2), ("vj", 1, 1), ("vj", 2, 3))[x[0]]
-            ts(k, n, T.va[:, 22 * x[0]:22 * x[0] + 22], T[k][:, :], sh, m, OP.logical_shift_right, OP.bitwise_and)
+            k, sh, m = (("vi", 1, 1), ("vi", 1, 2), ("vj", 5, 511), ("vj", 2, 3))[x[0]]
+            ts(K(k), K(n), VA(x[0]), T[k][:, Q], sh, m, OP.logical_shift_right, OP.bitwise_and)
         elif n[0:2] == "pw":
             times(q, "cb pl%d" % r, n, plane(T.pw, x[0]), T.cb[:, :].indirect(T["pl%d" % r][:, 22 * x[0]:22 * x[0] + 22]))
         elif n in ("t0", "t1", "t2", "t3"):
             a, b = x[0] >> 1, x[0] & 1
             times(q, "pw%d pl%d" % (1 - b, r), "s2%d" % x[0], T.s2[:, x[0]:1408:4], plane(T.pw, 1 - b).indirect(T["pl%d" % r][:, 22 * (1 - a):22 * (2 - a)]), 4.0)
-        elif n == "ki":
-            tten("va0 fo", "ki", T.ki[:, :], T.va[:, 0:22], T.fo[:, 1:44:2], OP.add)
-        elif n == "k0":
-            cp("ki", "k0", T.k0[:, :], T.ki[:, :])
+        elif n == "p0":
+            tten(K("va0") + "fo", K("ki"), T.ki[:, Q], VA(0), T.fo[:, 2 * lo + 1:2 * hi:2], OP.add)
+        elif n == "p2":
+            tten(K("kb") + K("y3"), K("ki"), T.ki[:, Q], T.kb[:, Q], T.y3[:, Q], OP.add)
+        elif n == "p4":
+            k = "kh" if q else "ksn"
+            tten(K(k) + K("va3"), K("ki"), T.ki[:, Q], T[k][:, L], VA(3), OP.add)
+        elif n in ("k0", "k2", "k4"):
+            ts(K("ki") + "cg6", K(n), T[n][:, Q], T.ki[:, Q], cg[:, 6:7] if q else 704.0 * (x[0] > 0), None, OP.add)
+        elif n in ("g0", "g2", "g4") and q:
+            act(S2 + K("k%d" % x[0]), K("km"), T.km[:, W], T.s2[:, :].indirect(T["k%d" % x[0]][:, Q]))
         elif n in ("g0", "g2", "g4"):
-            tten(S2 + "k%d m16" % x[0], "km", T.km[:, :], T.s2[:, :].indirect(T["k%d" % x[0]][:, :]), T.m16[:, :], OP.mult)
-            if x[0]:
-                scan("km r16", "ksn", T.ksn[:, :], T.r16[:, :], T.km[:, :])
-        elif n == "h0":
-            scan("km r16", "ksn", T.ksn[:, :], T.r16[:, :], T.km[:, :])
+            tten(S2 + K("k%d" % x[0]) + "m16", K("km"), T.km[:, W], T.s2[:, :].indirect(T["k%d" % x[0]][:, Q]), T.m16[:, W], OP.mult)
+        elif n == "h" and q:
+            hold(K("km") + "mx", K("kh"), T.kh[:, W], T.mx[:, W], T.km[:, W])
+        elif n == "h":
+            scan(K("km") + "r16", K("ksn"), T.ksn[:, W], T.r16[:, W], T.km[:, W])
         elif n == "kb":
-            tten("ksn va1", "kb", T.kb[:, :], T.ksn[:, L], T.va[:, 22:44], OP.add)
-        elif n == "k2":
-            tten("kb va2", "ki", T.ki[:, :], T.kb[:, :], T.va[:, 44:66], OP.add)
-            ts("ki", "k2", T.k2[:, :], T.ki[:, :], 704.0, None, OP.add)
-        elif n == "k4":
-            tten("ksn va3", "ki", T.ki[:, :], T.ksn[:, L], T.va[:, 66:88], OP.add)
-            ts("ki", "k4", T.k4[:, :], T.ki[:, :], 704.0, None, OP.add)
+            tten(K("ksn") + K("va1"), K("kb"), T.kb[:, Q], T.ksn[:, L], VA(1), OP.add)
         elif n == "k6":
-            ts("ksn", "k6", T.k6[:, :], T.ksn[:, L], 0.25, 176.0, OP.mult, OP.add)
+            k = "kh" if q else "ksn"
+            ts(K(k) + "cg7", K(n), T.k6[:, Q], T[k][:, L], 0.25, cg[:, 7:8] if q else 176.0, OP.mult, OP.add)
         elif n[0:2] == "gi":
-            act("xh%d i6" % x[0], n, T.gi[:, x[0]:1408:4], plane(T.xh, x[0]).indirect(T.i6[:, :]))
+            act("xh%d i6A i6B" % x[0], n, T.gi[:, x[0]:1408:4], plane(T.xh, x[0]).indirect(T.i6[:, :]))
         elif n[0] == "z":
             a, m = PART[x[0]]
             for b in x[1:] or range(4):
                 v = slice(4 * a + b, 4 * a + 4 * m, 4)
-                tten("xh%d k6 gi%d" % (b, b), "z%d" % x[0], T.z[:, v], plane(T.xh, b).indirect(T.k6[:, a // 16:(a + m) // 16]), T.gi[:, v], OP.add)
+                tten("xh%d k6%s gi%d" % (b, "AB"[x[0]], b), "z%d" % x[0], T.z[:, v], plane(T.xh, b).indirect(T.k6[:, a // 16:(a + m) // 16]), T.gi[:, v], OP.add)
         elif n in ("q0", "q1"):
             a, m = PART[x[0]]
             op("v", "z%d" % x[0], "zq%d" % x[0], V.quantize_mx, T.zq[:, a:a + m], T.zs[:, a:a + m], T.z[:, 4 * a:4 * a + 4 * m])
@@ -428,7 +440,7 @@ def rank_program(g, core, T, topo):
                T["hs%d" % r][:, a:a + m], T.hb[:, 4 * a:4 * a + 4 * m])
             send_part(r, x[0])
         elif n == "en":
-            act("b6 k6", "en", T.en[:, :], T.b6[:, :].indirect(T.k6[:, :]))
+            act("b6 k6A k6B", "en", T.en[:, :], T.b6[:, :].indirect(T.k6[:, :]))
         elif n == "dd":
             tten("en", "dd", T.dd[:, :], T.en[:, 0:C:2], T.en[:, 1:C:2], OP.mult)
         elif n == "dn":
@@ -442,23 +454,28 @@ def rank_program(g, core, T, topo):
         elif n in ("u0", "u1"):
             times(q, "pw%d tl" % (1 - x[0]), "uw%d" % x[0], plane(T.uw, x[0]), plane(T.pw, 1 - x[0]).indirect(T.tl[:, :]))
         elif n == "n0":
-            tten("uw0 sn%d m16" % r, "km", T.km[:, :], T.uw[:, 0:C].indirect(sn[:, 0:22]), T.m16[:, :], OP.mult)
+            tten("uw0 sn%d m16" % r, K("km"), T.km[:, :], T.uw[:, 0:C].indirect(sn[:, 0:22]), T.m16[:, :], OP.mult)
         elif n == "n1" and r < 2:
             act("uw1 sn%d" % r, "t1", T.t1[:, :], T.uw[:, C:704].indirect(sn[:, 22:44]))
         elif n == "ns0":
-            scan("km r16", "ksn", T.ksn[:, :], T.r16[:, :], T.km[:, :])
-            ts("ksn", "tx", ns[:, 0:22], T.ksn[:, L], 176.0, None, OP.add)
+            ts(K("ksn"), "tx", ns[:, 0:22], T.ksn[:, L], 176.0, None, OP.add)
+        elif n == "nh" and r < 2:
+            hold("t1 mx", K("kh"), T.kh[:, :], T.mx[:, :], T.t1[:, :])
         elif n == "ns1" and r < 2:
-            hold("t1 mx", "kh", T.kh[:, :], T.mx[:, :], T.t1[:, :])
-            ts("kh cg2 tx", "sn%d" % (r + 1), ns[:, 22:44], T.kh[:, L], cg[:, 2:3], None, OP.add)
+            ts(K("kh") + "cg2", "sn%d" % (r + 1), ns[:, 22:44], T.kh[:, L], cg[:, 2:3], None, OP.add)
             send_list(r + 1)
-            own_lists(r + 1)
+        elif n == "sf":
+            cp("tx sn%d" % r, "sf", T.sf[:, :], sn[:, 0:44])
+        elif n == "sd":
+            tten("sf", "fb", T.fb[:, 44:88:2], T.sf[:, 22:44], T.sf[:, 0:22], OP.subtract)
+        elif n == "vq":
+            op("v", "vb", "vq", V.quantize_mx, T.vq[:, :], T.vs[:, :], T.vb[:, :])
         elif n[0] == "e" and x:
             a, m = PART[x[0]]
             for b in x[1:] or range(4):
                 k, ps = bank(x[0], b)
-                mm("eq dq%d%d" % (r, x[0]), k, ps, T.eq[:, 128 * b:128 * b + 128], T.es[:, 128 * b:128 * b + 128],
-                   T["dq%d" % r][:, a:a + m], T["ds%d" % r][:, a:a + m])
+                mm("eq dq%d%d" % (r - 1, x[0]), k, ps, T.eq[:, 128 * b:128 * b + 128], T.es[:, 128 * b:128 * b + 128],
+                   T["dq%d" % (r - 1)][:, a:a + m], T["ds%d" % (r - 1)][:, a:a + m])
         elif n[0] == "d" and len(x) == 2:
             a, m = PART[x[0]]
             k, ps = bank(x[0], x[1])
@@ -472,43 +489,45 @@ def rank_program(g, core, T, topo):
         elif n[0:2] == "qx":
             qx(r, x[0])
         elif n[0:2] == "fb":
-            repeat_lists(x[0])
+            repeat_lists(x[0], q)
         elif n == "r6":
-            pick_rows(1, 128, 128)
+            act("uq url", "urs1", T.urs[:, 128:256], T.us[:, :].indirect(T.url[:, 8:16]))
         elif n == "mx":
             act("m16", "mx", T.mx[:, :], T.m16[:, :], AF.Identity, scale=-BIG - KM, bias=KM)
         elif n == "kc":
-            act("jj", "cb", T.cb[:, :], T.jj[:, :], AF.Identity, bias=-176.0)
-        elif n == "m8":
+            act("cw0", "cb", T.cb[:, :], T.cw[:, 0:C], AF.Identity, scale=1.0 / 32, bias=-176.0)
+        elif n == "m8" and r == 0:
+            act("j16 cn", "tw", T.tw[:, 0:176], T.j16[:, 0:C:2], AF.Abs, bias=T.cn[:, 3:4])
+            for i in (1, 2, 3):
+                act("cf", "cg%d" % (i + 1), cg[:, i + 1:i + 2], columns[i][0], AF.Identity, scale=columns[i][1], bias=columns[i][2])
+            act("tw", "dd", T.dd[:, :], T.tw[:, 0:176], AF.Relu, scale=-1.0, bias=1.0)
             act("dd", "m8", T.m8[:, :], T.dd[:, :], AF.Identity, scale=-132.0, bias=4.0)
-        elif n == "r16":
-            op("v", "r16o", "r16", V.memset, T.r16[:, 0:C:16], 0.0)
-        elif n == "eq":
-            op("v", "eb", "eq", V.quantize_mx, T.eq[:, :], T.es[:, :], T.eb[:, :])
+        elif n[0] == "w" and r == 0:
+            v = slice(128 * x[0], 128 * x[0] + 128)
+            op("v", "eb", "eq", V.quantize_mx, T.eq[:, v], T.es[:, v], T.eb[:, 512 * x[0]:512 * x[0] + 512])
 
     def run(r, names):
         for name in names.split():
             step(r, name)
 
-    def pick_rows(i, a, n):
-        cp("uq url", "ur%d" % i, T.urq[:, a:a + n].bitcast(dt.uint32), T.uq[:, :].bitcast(dt.uint32).indirect(T.url[:, a // 16:(a + n) // 16]))
-        act("uq url", "urs%d" % i, T.urs[:, a:a + n], T.us[:, :].indirect(T.url[:, a // 16:(a + n) // 16]))
-
     send_list(0)
     op("v", "ub", "uq", V.quantize_mx, T.uq[:, :], T.us[:, :], T.ub[:, :])
-    iota("jj", T.jj[:, :], [[1, C]], 0, 0)
-    run(0, "qx0 s0")
-    pick_rows(0, 0, 128)
-    run(0, "qx1 s1")
-    score_list()
-    act("lm", "dd", T.dd[:, :], T.lm[:, 0:176], AF.Relu, scale=-1.0, bias=1.0)
-    run(0, "fb0 mx fb1 fb2")
-    act("jj", "cw", T.cw[:, 0:C], T.jj[:, :], scale=32.0)
-    act("jj", "cw", T.cw[:, C:704], T.jj[:, :], AF.Identity, scale=32.0, bias=4.0)
+    iota("cw0", T.cw[:, 0:C], [[32, C]], 0, 0)
+    tten("ge ga0", "ge", T.ge[:, :], T.ge[:, :], T.cq[:, 10:20], OP.add)
+    run(0, "sf")
+    for i in range(2):
+        cp("uq url", "ur%d" % i, T.urq[:, 128 * i:128 * i + 128].bitcast(dt.uint32), T.uq[:, :].bitcast(dt.uint32).indirect(T.url[:, 8 * i:8 * i + 8]))
+    act("uq url", "urs0", T.urs[:, 0:128], T.us[:, :].indirect(T.url[:, 0:8]))
+    run(0, "qx0 s0 qx1 s1 sd")
+    cp("ge", "gl", T.gl[:, :], T.ge[:, :])
+    run(0, "mx fb0.a fb1.a")
+    act("cw0", "cw", T.cw[:, C:704], T.cw[:, 0:C], AF.Identity, bias=4.0)
+    run(0, "fb2.a")
     dma("s", "d_w", "xp00 xp01 ub", "wq", T.wq[:, :].bitcast(dt.uint8), T.wc[:, :])
     dma("s", "d_wp", "", "wp", T.wp[:, :], T.ws[:, :])
     dma("s", "d_v", "", "vb", T.vb[:, :], T.v[:, :])
     iota("r16o", T.r16[:, :], [[0, C]], 1, 0)
+    op("g", "r16o", "r16", g.iota, T.r16[:, 0:C:16], [[0, 22]], 0, 0, allow_small_or_imprecise_dtypes=True)
     for r in (1, 2):
         iota("pad%d" % r, T["xp%d" % r][:, 0:64], [[0, 64]], 0, 0)
         iota("pad%d" % r, T["xp%d" % r][:, 1472:1536], [[0, 64]], 0, 0)
@@ -517,17 +536,13 @@ def rank_program(g, core, T, topo):
         op("g", "one", "eb", g.affine_select, T.eb[:, 512 * b:512 * b + 512], T.one[:, :], [[-1, 512]], OP.is_equal, 0.0, b, 4)
 
     for r in range(3):
-        run(r, (BITS if r else BITS0) + PATH + (PATH1 if r else PATH0) + SECOND + LAYER + "eq " * (r == 0) + TURNS)
-        if r == 2:
-            op("v", "vb", "vq", V.quantize_mx, T.vq[:, :], T.vs[:, :], T.vb[:, :])
-        run(r, NEWX if r < 2 else NEWX.replace("fb0 ", "").replace("fb1 ", ""))
-        if r < 2:
-            run(r + 1, NEXT)
+        run(r, (BITS if r else BITS0) + PATH + (PATH1 if r else PATH0) + SECOND + (LAYER if r < 2 else LAYER2) + TURNS)
+        run(r + 1, NEXT if r < 2 else LAST)
     for b in range(2):
         act("uw%d sn2" % b, "tw", plane(T.tw, b), plane(T.uw, b).indirect(T.sn2[:, 22 * b:22 * b + 22]), AF.Identity, bias=176.0)
     dma("s", "d_so", "tw", "so", T.so[:, :], T.tw[0:128:16, :])
     for h in range(2):
-        run(3, "x%d qx%d" % (h, h))
+        run(3, ("x0 x10 qx0", "x11 x12 x13 qx1")[h])
         a, n = XH[h]
         q = slice(16 + a, 16 + a + n)
         mm("vq xq%d" % h, "pa%d" % h, T.pa[:, 512 * h:512 * h + n], T.vq[:, :], T.vs[:, :], T.xq[:, q], T.xs[:, q])

@@ -6,6 +6,7 @@ MASK = [2, 4, 1]
 PART = [(0, 192), (192, 160)]
 XH = [(0, 224), (224, 128)]
 KM, BIG = 32768.0, 2097152.0
+UNIT = 2.0 ** -15
 ROWS = [1, 6]
 BF, F32, I32, U16, U8, E4 = "bfloat16", "float32", "int32", "uint16", "uint8", "float8_e4m3fn_x4"
 SCRATCH = {
@@ -13,25 +14,26 @@ SCRATCH = {
     "wq": ("sbuf", [128, 512], E4), "wp": ("sbuf", [128, 512], U8),
     "uq": ("sbuf", [128, 128], E4), "us": ("sbuf", [128, 128], U8), "vq": ("sbuf", [128, 128], E4), "vs": ("sbuf", [128, 128], U8),
     "urq": ("sbuf", [128, 384], E4), "urs": ("sbuf", [128, 384], U8),
-    "pc": ("sbuf", [128, 8], I32), "ci": ("sbuf", [128, 8], I32), "cf": ("sbuf", [128, 8], F32), "cg": ("sbuf", [128, 8], F32),
+    "pc": ("sbuf", [128, 8], I32), "ci": ("sbuf", [128, 8], I32), "cf": ("sbuf", [128, 8], F32), "cg": ("sbuf", [128, 12], F32),
     "cn": ("sbuf", [128, 4], F32),
     "j16": ("sbuf", [128, C], F32), "cw": ("sbuf", [128, 704], F32), "cb": ("sbuf", [128, C], BF),
-    "m16": ("sbuf", [128, C], BF), "r16": ("sbuf", [128, C], BF), "mx": ("sbuf", [128, C], BF), "m8": ("sbuf", [128, 176], BF),
+    "m16": ("sbuf", [128, C], BF), "r16": ("sbuf", [128, C], BF), "mx": ("sbuf", [128, C], BF), "my": ("sbuf", [128, C], BF),
+    "m2": ("sbuf", [128, C], BF),
     "cq": ("sbuf", [128, 24], F32), "cl": ("sbuf", [128, 24], F32), "ga": ("sbuf", [128, 10], I32), "gb": ("sbuf", [128, 10], F32),
     "ge": ("sbuf", [128, 10], F32), "gl": ("sbuf", [128, 10], U16), "url": ("sbuf", [128, 24], U16),
     "one": ("sbuf", [128, 512], BF), "eb": ("sbuf", [128, 2048], BF), "eq": ("sbuf", [128, 512], E4), "es": ("sbuf", [128, 512], U8),
     "xq": ("sbuf", [128, 384], E4), "xs": ("sbuf", [128, 384], U8), "xh": ("sbuf", [128, 1408], BF),
-    "b1": ("sbuf", [128, C], BF), "b3": ("sbuf", [128, C], BF), "b6": ("sbuf", [128, C], BF),
+    "b1": ("sbuf", [128, C], BF), "b6": ("sbuf", [128, C], BF),
     "tt": ("sbuf", [128, 736], F32), "fm": ("sbuf", [128, 320], F32), "fb": ("sbuf", [128, 308], F32),
     "fo": ("sbuf", [128, 308], F32), "fl": ("sbuf", [128, 132], U16), "sf": ("sbuf", [128, 44], F32),
     "la": ("sbuf", [128, C], F32), "lb": ("sbuf", [128, C], F32), "lm": ("sbuf", [128, C], F32), "ln": ("sbuf", [128, C], F32),
     "ha": ("sbuf", [128, 704], F32), "hc": ("sbuf", [128, 704], F32), "hd": ("sbuf", [128, C], F32),
     "i3": ("sbuf", [128, 22], U16), "i6": ("sbuf", [128, 22], U16), "vi": ("sbuf", [128, 22], I32), "vj": ("sbuf", [128, 22], I32),
-    "va": ("sbuf", [128, 88], I32), "y3": ("sbuf", [128, 22], F32),
+    "va": ("sbuf", [128, 110], I32), "jf": ("sbuf", [128, 132], F32),
     "pw": ("sbuf", [128, 704], BF), "s2": ("sbuf", [128, 1408], BF), "km": ("sbuf", [128, C], BF), "ksn": ("sbuf", [128, C], BF),
-    "ku": ("sbuf", [128, C], BF), "kh": ("sbuf", [128, C], F32), "ki": ("sbuf", [128, 22], F32), "kb": ("sbuf", [128, 22], F32),
+    "kh": ("sbuf", [128, C], F32), "ki": ("sbuf", [128, 22], F32), "kb": ("sbuf", [128, 22], F32),
     "k0": ("sbuf", [128, 22], U16), "k2": ("sbuf", [128, 22], U16), "k4": ("sbuf", [128, 22], U16), "k6": ("sbuf", [128, 22], U16),
-    "en": ("sbuf", [128, C], BF), "dd": ("sbuf", [128, 176], BF), "dn": ("sbuf", [128, 176], BF), "tf": ("sbuf", [128, 22], F32),
+    "en": ("sbuf", [128, C], BF), "dd": ("sbuf", [128, 22], F32), "dn": ("sbuf", [128, C], BF), "tf": ("sbuf", [128, 22], F32),
     "tg": ("sbuf", [128, 22], F32), "tl": ("sbuf", [128, 22], U16), "uw": ("sbuf", [128, 704], BF), "t1": ("sbuf", [128, C], BF),
     "tw": ("sbuf", [128, 704], F32),
     "gi": ("sbuf", [128, 1408], BF), "z": ("sbuf", [128, 1408], BF), "zq": ("sbuf", [128, C], E4), "zs": ("sbuf", [128, C], U8),
@@ -55,19 +57,22 @@ for _r in range(3):
     SEMAPHORES += [n + str(_r) for n in ("hl", "hc", "hp", "la", "ca", "cb")]
 CODES = [(0, 1), (2, 3)]
 SCALES = [2, 0]
-LISTS = 3
+LISTS = [(0, 1, 2, 3), (3,), (3,)]
 
-BITS = "s1 m1 m6 ts0 tr1 ts1 fm xh0.v fo xh1.v fl t2.a b1 t3.a "
-BITS0 = "m1 tr0 ts0 tr1 ts1 fm xh0.v fo xh1.v fl b1 kc "
-PATH = "ha la ha2 lb hc lm hc2 ln hd "
-PATH1 = "vi i3 hm xh2.a xh3.a b6 va0 va1 p0 k0 g0 hn h vj y3 kb va2 p2 i6 k2 va3 "
-PATH0 = "i3 vi pw0.v hm va0 pw1.v va1 p0 t1.v k0 t0.a t2.a hn t3.v vj y3 g0 va2 h i6 va3 r6 m6 xh2.a xh3.a kb w0 b6 p2 w1 k2 "
-SECOND = "g2B.a g2A gi0 gi1 w2 hA w3 p4A hB.a k4A p4B.a g4A k4B.a gi2 gi3 m8 hA g4B k6A hB z00 k6B en "
-LAYER = "z01 z02 z03 z10 q0 c00.a c01.a c02.a z11 z12 z13 q1 c03.v dd h0q dn c10.a c11.v tf c12.a c13.v tg h1q tl "
-LAYER2 = "z01 z02 z03 z10 q0 c00.a c01.a c02.a z11 z12 z13 q1 c03.v h0q c10.a dd c11.v c12.a c13.v h1q dn vq tf tg tl "
-TURNS = "u0.v u1.a n0 n1 h nh ns0 ns1 "
-NEXT = "sf sd e00 e01 e02 e10 e11 e03 e12 e13 fb0.a d00.v d01.a d02.v fb1.a d10.v d11.a d12.a d03.a d13.a pw0.a pw1.a fb2.a x0 x10 qx0 s0 t0.a t1.a x11 x12 x13 qx1 tr0 "
-LAST = "e00 e01 e02 e10 e11 e03 e12 e13 d00.v d01.a d02.a d10.v d11.v d12.a d03.a d13.a "
+BITS = "qx1 s1 m1 m6 t3.a xh1.a ts0 xh0.v tr1 ts1 b1 t2.a fm1 fm0 fo1 fo0 fl1 fl0 "
+BITS0 = "m1 tr0 ts0 tr1 ts1 xh0.v xh1.a b1 fm1 fm0 fo1 fo0 fl1 fl0 my mx "
+PATH = "la haA.a haB.a ha2A.a ha2B.a xh3.v lb hcA.a hcB.a hc2A.a hc2B.a xh2.v lmA lmB lnA lnB hdA.a hdB.a "
+PATH1 = "viA p0A viB va0A p0B k0A va0B i3A k0B hmA g0A i3B hmB g0B hA va1 hB hnA kbA hnB kbB p2A vj p2B k2A va2 k2B "
+PATH0 = ("j0 viA viB j1 va0A va4 va0B j2 i3A j3 i3B pw1.v j4 hmA hmB j5 pw0.a hnB j6 r6 m6 hnA j7 va1 vj h t2.a t3.a va2 va3 kb t1.v t0.a "
+         "p2A p2B k2A k2B i6 b6 ")
+SECOND = "g2A g2B.a i6 va3 hA hB.a p4A p4B.a k4A k4B.a gi0A gi1A g4A g4B.a hA hB.a gi2A gi3A gi0B gi1B gi2B gi3B k6A k6B.a z00 b6 en "
+SECOND0 = "g2A g2B.a m2a hA hB.a p4A p4B.a k4A k4B.a gi0A g4A g4B.a m2b hA hB.a gi1A gi2A gi3A gi0B gi1B k6A m2c k6B.a z00 z01 gi2B gi3B en "
+LAYER = "z02 z03 z10 q0 z11 c00.a c01.a z12 c03.a z13 dn q1 dd c02.v tf tg h0q tl c10.a c12.a c13.a c11.v u1.a u0.v h1q "
+TURNS = "n0 n1 h nh ns0 ns1 "
+NEXT = ("w0 w1 w2 w3 e00 e01 e03 e10 e11 e02 e12 e13 sf d00.v sd fb0.a d03.a d01.v d10.v d02.a d11.v d12.a d13.a "
+        "x00 pw1.a x01 fb1.a pw0.a x02 t0.a x03 fb2.a x10 t1.a qx0 s0 x11 x12 x13 tr0 ")
+LAST = "so e00 e01 e02 e03 e10 e11 e12 e13 vq d00.v d01.v d02.a d03.a d10.v d11.v d12.a d13.a "
+END = ("x00 x01 x02 x03 x10 qx0", "x11 x12 x13 qx1")
 
 
 def route(topo, core, dst):
@@ -99,9 +104,11 @@ def hand_on(g, core, T, topo):
             rid, pid = topo.addr(dst, core)
             e = topo.engines(core, dst)
             n_in = len(topo.engines(c, core))
-            if i == LISTS:
-                g.wait_ge(T.sem["hl%d" % r], n_in)
-                g.remote_dma(T["pl%d" % r][:, :], T["lh%d" % r][:, :], T.sem["la%d" % r], T.sem.ls, pid, rid, bits(e))
+            if i in LISTS[r]:
+                w = 44 // len(LISTS[r])
+                v = slice(w * LISTS[r].index(i), w * LISTS[r].index(i) + w)
+                g.wait_ge(T.sem["hl%d" % r], n_in // len(LISTS[r]))
+                g.remote_dma(T["pl%d" % r][:, v], T["lh%d" % r][:, v], T.sem["la%d" % r], T.sem.ls, pid, rid, bits(e))
                 sent += len(e)
             for h in range(2):
                 arr = T.sem[("ca%d", "cb%d")[h] % r]
@@ -208,14 +215,18 @@ def rank_program(g, core, T, topo):
     def iota(k, out, pattern, base, cm):
         op("g", "", k, g.iota, out, pattern, base, cm, allow_small_or_imprecise_dtypes=True)
 
+    def xp(r, h):
+        return "".join("xp%d%d%d " % (r, h, b) for b in range(4))
+
     dma("s", "d_se", "", "sei", T.sei[:, :], T.se[:, :])
     dma("a", "d_u", "", "ub", T.ub[:, :], T.u[:, :])
-    dma("s", "d_x", "", "xp00", T.xp0[:, 64:64 + 4 * XH[1][0]], T.x[:, 0:4 * XH[1][0]])
-    dma("a", "d_x2", "", "xp01", T.xp0[:, 64 + 4 * XH[1][0]:1472], T.x[:, 4 * XH[1][0]:1408])
+    dma("s", "d_x", "", xp(0, 0), T.xp0[:, 64:64 + 4 * XH[1][0]], T.x[:, 0:4 * XH[1][0]])
+    dma("s", "d_x2", "", xp(0, 1), T.xp0[:, 64 + 4 * XH[1][0]:1472], T.x[:, 4 * XH[1][0]:1408])
     op("g", "", "pc", g.iota, T.pc[:, 0:1], [[0, 1]], 0, 1)
     iota("cq", T.cq[:, :], [[16, 24]], 0, 0)
     iota("j16", T.j16[:, :], [[0, 22], [1, 16]], 0, 0)
-    iota("fbc", T.fb[:, 0:44:2], [[0, 22]], 2, 0)
+    iota("fbc", T.fb[:, 0:44:2], [[0, 22]], 1, 0)
+    iota("cw0", T.tw[:, 0:C], [[1, C]], 0, 0)
     op("v", "", "pad0", V.memset, T.xp0[:, 0:64], 0.0)
     op("v", "", "pad0", V.memset, T.xp0[:, 1472:1536], 0.0)
     ci, cf, cg = T.ci, T.cf, T.cg
@@ -231,17 +242,20 @@ def rank_program(g, core, T, topo):
     ts("cq cf", "cl", T.cl[:, :], T.cq[:, :], PR, None, OP.add)
     ts("cf", "cg0", cg[:, 0:1], PH, PP, 368.0, OP.not_equal, OP.mult)
     ts("cf", "cn", T.cn[:, :], cf[:, 0:4], -1.0, None, OP.mult)
-    columns = ((PR, -KM, 15.5 * KM), (PR, KM, 176 - 15 * KM), (PE, -2.0, 28.0), (PP, -2.0, 1.0), (PR, KM / 32, -15 * KM / 32),
-               (PR, KM, 704 - 15 * KM), (PR, KM / 4, 176 - 15 * KM / 4))
-    for i in (0, 4, 5, 6):
-        act("cf", "cg%d" % (i + 1), cg[:, i + 1:i + 2], columns[i][0], AF.Identity, scale=columns[i][1], bias=columns[i][2])
-    act("j16 cn", "lnA lnB", T.ln[:, :], T.j16[:, :], AF.Abs, bias=T.cn[:, 0:1])
+    columns = {1: (PR, 4.0, -60.0), 4: (PP, -2.0, 1.0), 5: (PR, 4.0, 704 - 60.0), 6: (PR, KM, 704 - 15 * KM),
+               7: (PR, KM / 4, 176 - 15 * KM / 4), 8: (PR, KM + 4, 704 - 60.0 - 15 * KM)}
+
+    for i in columns:
+        act("cf", "cg%d" % i, cg[:, i:i + 1], columns[i][0], AF.Identity, scale=columns[i][1], bias=columns[i][2])
+    act("j16 cn", "dn", T.dn[:, :], T.j16[:, :], AF.Square, bias=T.cn[:, 3:4])
     act("cl", "fbd", T.fb[:, 1:44:2], T.cl[:, 0:22], scale=4.0)
-    act("lnA lnB", "m16", T.m16[:, :], T.ln[:, :], AF.Relu, scale=-1.0, bias=1.0)
+    for i in range(2):
+        act("cw0", "cw", T.cw[:, C * i:C * i + C], T.tw[:, 0:C], AF.Identity, scale=32 * UNIT, bias=8 * UNIT * i)
     ts("cl", "ga", T.ga[:, :], T.cl[:, 0:10], 1.0 / 22, -0.477, OP.mult, OP.add)
     ts("cl cg0", "ge", T.ge[:, :], T.cl[:, 0:10], 16.0, cg[:, 0:1], OP.mult, OP.add)
     ts("ga", "gb", T.gb[:, :], T.ga[:, :], -351.0, -1.0, OP.mult, OP.add)
     ts("ga", "ga0", T.cq[:, 10:20], T.ga[:, :], 0.0, None, OP.is_equal)
+    ts("j16 cf", "m16", T.m16[:, :], T.j16[:, :], PR, None, OP.is_equal)
     cp("sei", "sn0", T.sn0[:, 0:44], T.sei[:, :])
     tten("gb ge", "ge", T.ge[:, :], T.ge[:, :], T.gb[:, :], OP.add)
 
@@ -251,13 +265,18 @@ def rank_program(g, core, T, topo):
         return T.cores[rank ^ MASK[r]]
 
     def send_list(r):
-        h = route(topo, core, partner(r))[LISTS]
-        rid, pid = topo.addr(h, core)
-        e = topo.engines(core, h)
+        hs, tr, w = route(topo, core, partner(r)), [], 44 // len(LISTS[r])
+        for i, k in enumerate(LISTS[r]):
+            rid, pid = topo.addr(hs[k], core)
+            e = topo.engines(core, hs[k])
+            n = len(e) // len(LISTS[r])
+            tr.append(RemoteDMATransfer(dst_ids=[DstId(rid=rid, pnc=pid)], dma_engine_mask=bits(e[n * i:n * i + n]), remote_sem=T.sem["hl%d" % r],
+                                        src=T["sn%d" % r][:, w * i:w * i + w], dst=T["lh%d" % r][:, w * i:w * i + w]))
+            sent[0] += n
         need("g", ["tx", "sn%d" % r], [])
-        g.remote_dma(T["lh%d" % r][:, :], T["sn%d" % r][:, 0:44], T.sem["hl%d" % r], T.sem.ls, pid, rid, bits(e))
-        sent[0] += len(e)
-        arrived("pl%d" % r, "la%d" % r, len(topo.engines(route(topo, partner(r), core)[LISTS], core)))
+        g.remote_dma_fused(tr, local_sem=T.sem.ls)
+        hp = route(topo, partner(r), core)
+        arrived("pl%d" % r, "la%d" % r, sum(len(topo.engines(hp[k], core)) for k in LISTS[r]))
 
     def send_part(r, h):
         hs = route(topo, core, partner(r))
@@ -267,7 +286,7 @@ def rank_program(g, core, T, topo):
             e = topo.engines(core, hs[k])
             n = len(e) // 2
             a, m = chunk(h, i)
-            tr.append(RemoteDMATransfer(dst_ids=[DstId(rid=rid, pnc=pid)], dma_engine_mask=bits(e[n * i:n * i + n]), remote_sem=T.sem["hc%d" % r],
+            tr.append(RemoteDMATransfer(dst_ids=[DstId(rid=rid, pnc=pid)], dma_engine_mask=bits(e[(i + h) % 2::2]), remote_sem=T.sem["hc%d" % r],
                                         src=T["hq%d" % r][:, a:a + m].bitcast(dt.uint8), dst=T["fq%d" % r][:, 0:m].bitcast(dt.uint8)))
             sent[0] += n
         need("g", ["hq%d%d" % (r, h)], [])
@@ -284,10 +303,7 @@ def rank_program(g, core, T, topo):
         if i == 0:
             times(q, "sf", "fb1", T.fb[:, 45:88:2], T.sf[:, 0:22])
             times(q, "sf", "fb1", T.fb[:, 133:176:2], T.sf[:, 0:22])
-            if q == "a":
-                act("fb", "fb1", T.fb[:, 132:176:2], T.fb[:, 44:88:2], AF.Identity, bias=352.0)
-            else:
-                ts("fb", "fb1", T.fb[:, 132:176:2], T.fb[:, 44:88:2], 352.0, None, OP.add)
+            act("fb", "fb1", T.fb[:, 132:176:2], T.fb[:, 44:88:2], AF.Identity, bias=352.0)
         elif i == 1:
             times(q, "fb fb1", "fb2", T.fb[:, 88:132], T.fb[:, 44:88])
             times(q, "fb1", "fb2", T.fb[:, 176:220], T.fb[:, 132:176])
@@ -305,14 +321,11 @@ def rank_program(g, core, T, topo):
         a, n = 16 + XH[h][0], XH[h][1]
         if r < 3:
             a, n = a - 16 * (1 - h), n + 16
-        op("v", "xp%d%d pad%d" % (r, h, r), "xq%d" % h, V.quantize_mx, T.xq[:, a:a + n], T.xs[:, a:a + n], T["xp%d" % r][:, 4 * a:4 * a + 4 * n])
+        op("v", xp(r, h) + "pad%d" % r, "xq%d" % h, V.quantize_mx, T.xq[:, a:a + n], T.xs[:, a:a + n], T["xp%d" % r][:, 4 * a:4 * a + 4 * n])
 
     def scores(h):
         a, n = XH[h][0], XH[h][1] + 16 + 16 * h
         mm("uq xq0" + " xq1" * h, "pb%d" % h, T.pb[:, 512 * h:512 * h + n], T.uq[:, :], T.us[:, :], T.xq[:, a:a + n], T.xs[:, a:a + n])
-
-    def F(l):
-        return T.fl[:, 22 * l:22 * l + 22]
 
     def rows_bank(i):
         return "pb%d" % (2 + i), T.pb[:, 1024 + 512 * i:1024 + 512 * i + C]
@@ -330,6 +343,9 @@ def rank_program(g, core, T, topo):
 
         def K(k):
             return "".join(k + p + " " for p in parts)
+
+        def F(l):
+            return T.fl[:, 22 * l + lo:22 * l + hi]
 
         def VA(i):
             return T.va[:, 22 * i + lo:22 * i + hi]
@@ -351,59 +367,78 @@ def rank_program(g, core, T, topo):
             h = x[0]
             a, m = XH[h][0], XH[h][1] + 32 * h
             op("v", "pb%d" % h, "tt", V.transpose, T.tt[:, C + a:C + a + m], T.pb[:, 512 * h:512 * h + m])
-        elif n == "fm":
-            ts("tt gl", "fm", T.fm[:, 1:320:2], T.tt[:, :].indirect(T.gl[:, :]), 0.0, None, OP.is_gt)
-        elif n == "fo":
-            scan("fm fbc fbd fb fb1 fb2 fb3", "fo", T.fo[:, :], T.fm[:, 0:308], T.fb[:, :])
-        elif n == "fl":
-            cp("fo", "fl", T.fl[:, :], T.fo[:, 45:308:2])
+        elif n in ("fm0", "fm1"):
+            a, b = ((6, 10), (0, 6))[x[0]]
+            ts("tt fm gl", n, T.fm[:, 32 * a + 1:32 * b:2], T.tt[:, :].indirect(T.gl[:, a:b]), 0.0, None, OP.is_gt)
+        elif n in ("fo0", "fo1"):
+            v = (slice(176, 308), slice(0, 176))[x[0]]
+            scan("fm1 fbc fbd fb fb1 fb2 fb3" + " fm0" * (1 - x[0]), n, T.fo[:, v], T.fm[:, v], T.fb[:, v])
+        elif n in ("fl0", "fl1"):
+            a = 66 * (1 - x[0])
+            cp("fo%d" % x[0], n, T.fl[:, a:a + 66], T.fo[:, 2 * a + 45:2 * a + 176:2])
         elif n[0:2] == "xh":
-            times(q, "xp%d0 xp%d1" % (r, r), n, plane(T.xh, x[0]), XP[:, 64 + x[0]:1472:4], 0.5)
+            times(q, "xp%d0%d xp%d1%d" % (r, x[0], r, x[0]), n, plane(T.xh, x[0]), XP[:, 64 + x[0]:1472:4], 0.5)
         elif n == "la":
-            ts("cw fl", "la", T.la[:, :], T.cw[:, :].indirect(F(2)), 1.0, None, OP.add)
+            ts("cw fl1", "la", T.la[:, :], T.cw[:, :].indirect(F(2)), 1.0, None, OP.add)
         elif n == "lb":
-            tten("la fl b1", "lb", T.lb[:, :], T.la[:, :].indirect(F(1)), T.b1[:, :], OP.add)
+            tten("la fl1 b1", "lb", T.lb[:, :], T.la[:, :].indirect(F(1)), T.b1[:, :], OP.add)
         elif n == "lm":
-            cp("lb fl", K("lm"), T.lm[:, W], T.lb[:, :].indirect(T.fl[:, Q]))
+            cp("lb fl1", K("lm"), T.lm[:, W], T.lb[:, :].indirect(T.fl[:, Q]))
         elif n in ("ln", "hn"):
-            hold(K("lm") + "mx", K("ln"), T.ln[:, W], T.mx[:, W], T.lm[:, W])
-        elif n == "i3":
-            ts(K("ln") + "cg5", K(n), T.i3[:, Q], T.ln[:, L], 1.0 / 32, cg[:, 5:6], OP.mult, OP.add)
+            hold(K("lm") + "my", K("ln"), T.ln[:, W], T.my[:, W], T.lm[:, W])
         elif n in ("vi", "vj"):
-            cp(K("ln"), K(n), T[n][:, Q], T.ln[:, L])
-        elif n == "y3":
-            ts(K("ln") + "cg1", K(n), T.y3[:, Q], T.ln[:, L], cg[:, 1:2], None, OP.is_ge)
-        elif n == "i6":
-            cp(K("va2"), K(n), T.i6[:, Q], VA(2))
+            ts(K("ln"), K(n), T[n][:, Q], T.ln[:, L], 1 / UNIT, None, OP.mult)
+        elif n in ("i3", "i6"):
+            i = 2 * (n == "i6")
+            cp(K("va%d" % i), K(n), T[n][:, Q], VA(i))
         elif n == "ha":
-            act("cw fl", "ha", T.ha[:, 0:C], T.cw[:, :].indirect(F(5)))
-        elif n == "ha2":
-            act("ha", "ha2", T.ha[:, C:704], T.ha[:, 0:C], AF.Identity, bias=8.0)
+            times(q, "cw fl0", K(n), T.ha[:, W], T.cw[:, :].indirect(F(5)))
+        elif n in ("ha2", "hc2"):
+            t, c = T[n[0:2]], (4 * UNIT if n == "ha2" else 2.0)
+            if q == "a":
+                act(K(n[0:2]), K(n), t[:, C + 16 * lo:C + 16 * hi], t[:, W], AF.Identity, bias=c)
+            else:
+                ts(K(n[0:2]), K(n), t[:, C + 16 * lo:C + 16 * hi], t[:, W], c, None, OP.add)
         elif n == "hc":
-            act("ha ha2 fl", "hc", T.hc[:, 0:C], T.ha[:, :].indirect(F(4)))
-        elif n == "hc2":
-            act("hc", "hc2", T.hc[:, C:704], T.hc[:, 0:C], AF.Identity, bias=KM / 2)
+            times(q, "haA haB ha2A ha2B fl0", K(n), T.hc[:, W], T.ha[:, :].indirect(F(4)))
         elif n == "hd":
-            act("hc hc2 fl", "hd", T.hd[:, :], T.hc[:, :].indirect(F(3)))
+            times(q, "hcA hcB hc2A hc2B fl0", K(n), T.hd[:, W], T.hc[:, :].indirect(F(3)))
         elif n == "hm":
-            act("hd " + K("i3"), K("lm"), T.lm[:, W], T.hd[:, :].indirect(T.i3[:, Q]))
+            act("hdA hdB " + K("i3"), K("lm"), T.lm[:, W], T.hd[:, :].indirect(T.i3[:, Q]))
         elif n[0:2] == "va":
-            k, sh, m = (("vi", 1, 1), ("vi", 1, 2), ("vj", 5, 511), ("vj", 2, 3))[x[0]]
+            k, sh, m = (("vi", 5, 511), ("vi", 3, 1), ("vj", 5, 511), ("vj", 2, 3), ("vi", 16, 1))[x[0]]
             ts(K(k), K(n), VA(x[0]), T[k][:, Q], sh, m, OP.logical_shift_right, OP.bitwise_and)
         elif n[0:2] == "pw":
-            times(q, "cb pl%d" % r, n, plane(T.pw, x[0]), T.cb[:, :].indirect(T["pl%d" % r][:, 22 * x[0]:22 * x[0] + 22]))
+            times(q, "cb pl%d" % r, n, plane(T.pw, x[0]), T.cb[:, :].indirect(T["pl%d" % r][:, 22 * x[0]:22 * x[0] + 22]), 4.0)
         elif n in ("t0", "t1", "t2", "t3"):
-            a, b = x[0] >> 1, x[0] & 1
-            times(q, "pw%d pl%d" % (1 - b, r), "s2%d" % x[0], T.s2[:, x[0]:1408:4], plane(T.pw, 1 - b).indirect(T["pl%d" % r][:, 22 * (1 - a):22 * (2 - a)]), 4.0)
+            a, b = x[0] & 1, x[0] >> 1
+            times(q, "pw%d pl%d" % (1 - b, r), "s2%d" % x[0], T.s2[:, x[0]:1408:4], plane(T.pw, 1 - b).indirect(T["pl%d" % r][:, 22 * (1 - a):22 * (2 - a)]))
+        elif n == "j0":
+            cp("pl0", "jf", T.jf[:, 0:44], T.pl0[:, :])
+        elif n == "j1":
+            tten("jf", "j1", T.jf[:, 44:66], T.jf[:, 0:22], T.jf[:, 22:44], OP.subtract)
+        elif n == "j2":
+            tten("j1 fm1", "j2", T.jf[:, 66:88], T.jf[:, 44:66], T.fm[:, 1:44:2], OP.mult)
+        elif n == "j3":
+            ts(K("va4"), "j3", T.jf[:, 88:110], VA(4), -352.0, 352.0, OP.mult, OP.add)
+        elif n == "j4":
+            tten("jf j3", "j4", T.jf[:, 110:132], T.jf[:, 22:44], T.jf[:, 88:110], OP.add)
+        elif n == "j5":
+            tten("j2 j4", K("ki"), T.ki[:, :], T.jf[:, 66:88], T.jf[:, 110:132], OP.add)
+        elif n == "j6":
+            cp(K("ki"), K("k0"), T.k0[:, :], T.ki[:, :])
+        elif n == "j7":
+            tten("pw0 pw1 m16 " + K("k0"), K("km"), T.km[:, :], T.pw[:, :].indirect(T.k0[:, :]), T.m16[:, :], OP.mult)
         elif n == "p0":
-            tten(K("va0") + "fo", K("ki"), T.ki[:, Q], VA(0), T.fo[:, 2 * lo + 1:2 * hi:2], OP.add)
+            tten(K("ln") + "fo1", K("ki"), T.ki[:, Q], T.ln[:, L], T.fo[:, 2 * lo + 1:2 * hi:2], OP.add)
         elif n == "p2":
-            tten(K("kb") + K("y3"), K("ki"), T.ki[:, Q], T.kb[:, Q], T.y3[:, Q], OP.add)
+            tten(K("kb") + K("ln"), K("ki"), T.ki[:, Q], T.kb[:, Q], T.ln[:, L], OP.add)
         elif n == "p4":
             k = "kh" if q else "ksn"
             tten(K(k) + K("va3"), K("ki"), T.ki[:, Q], T[k][:, L], VA(3), OP.add)
         elif n in ("k0", "k2", "k4"):
-            ts(K("ki") + "cg6", K(n), T[n][:, Q], T.ki[:, Q], cg[:, 6:7] if q else 704.0 * (x[0] > 0), None, OP.add)
+            i = {"k0": 1, "k2": 8 if q else 5, "k4": 6}[n]
+            ts(K("ki") + "cg%d" % i, K(n), T[n][:, Q], T.ki[:, Q], cg[:, i:i + 1] if q or i < 6 else 704.0, None, OP.add)
         elif n in ("g0", "g2", "g4") and q:
             act(S2 + K("k%d" % x[0]), K("km"), T.km[:, W], T.s2[:, :].indirect(T["k%d" % x[0]][:, Q]))
         elif n in ("g0", "g2", "g4"):
@@ -413,17 +448,18 @@ def rank_program(g, core, T, topo):
         elif n == "h":
             scan(K("km") + "r16", K("ksn"), T.ksn[:, W], T.r16[:, W], T.km[:, W])
         elif n == "kb":
-            tten(K("ksn") + K("va1"), K("kb"), T.kb[:, Q], T.ksn[:, L], VA(1), OP.add)
+            k = "kh" if q else "ksn"
+            tten(K(k) + K("va1"), K("kb"), T.kb[:, Q], T[k][:, L], VA(1), OP.add)
         elif n == "k6":
             k = "kh" if q else "ksn"
             ts(K(k) + "cg7", K(n), T.k6[:, Q], T[k][:, L], 0.25, cg[:, 7:8] if q else 176.0, OP.mult, OP.add)
         elif n[0:2] == "gi":
-            act("xh%d i6A i6B" % x[0], n, T.gi[:, x[0]:1408:4], plane(T.xh, x[0]).indirect(T.i6[:, :]))
+            act("xh%d " % x[0] + K("i6"), K(n), T.gi[:, 64 * lo + x[0]:64 * hi:4], plane(T.xh, x[0]).indirect(T.i6[:, Q]))
         elif n[0] == "z":
             a, m = PART[x[0]]
-            for b in x[1:] or range(4):
-                v = slice(4 * a + b, 4 * a + 4 * m, 4)
-                tten("xh%d k6%s gi%d" % (b, "AB"[x[0]], b), "z%d" % x[0], T.z[:, v], plane(T.xh, b).indirect(T.k6[:, a // 16:(a + m) // 16]), T.gi[:, v], OP.add)
+            b = x[1]
+            v = slice(4 * a + b, 4 * a + 4 * m, 4)
+            tten("xh%d k6%s gi%d%s" % (b, "AB"[x[0]], b, "AB"[x[0]]), "z%d" % x[0], T.z[:, v], plane(T.xh, b).indirect(T.k6[:, a // 16:(a + m) // 16]), T.gi[:, v], OP.add)
         elif n in ("q0", "q1"):
             a, m = PART[x[0]]
             op("v", "z%d" % x[0], "zq%d" % x[0], V.quantize_mx, T.zq[:, a:a + m], T.zs[:, a:a + m], T.z[:, 4 * a:4 * a + 4 * m])
@@ -441,51 +477,58 @@ def rank_program(g, core, T, topo):
             send_part(r, x[0])
         elif n == "en":
             act("b6 k6A k6B", "en", T.en[:, :], T.b6[:, :].indirect(T.k6[:, :]))
-        elif n == "dd":
-            tten("en", "dd", T.dd[:, :], T.en[:, 0:C:2], T.en[:, 1:C:2], OP.mult)
         elif n == "dn":
-            hold("dd m8", "dn", T.dn[:, :], T.m8[:, :], T.dd[:, :])
+            scan("en m2", "dn", T.dn[:, :], T.m2[:, :], T.en[:, :])
+        elif n == "dd":
+            tten("dn", "dd", T.dd[:, :], T.dn[:, L], T.dn[:, L], OP.mult)
         elif n == "tf":
-            ts("dn cg3 cg4", "tf", T.tf[:, :], T.dn[:, 7:176:8], cg[:, 3:4], cg[:, 4:5], OP.is_lt, OP.mult)
+            ts("dd cg3 cg4", "tf", T.tf[:, :], T.dd[:, :], cg[:, 3:4], cg[:, 4:5], OP.is_lt, OP.mult)
         elif n == "tg":
             tten("tf cl", "tg", T.tg[:, :], T.tf[:, :], T.cl[:, 0:22], OP.add)
         elif n == "tl":
             cp("tg", "tl", T.tl[:, :], T.tg[:, :])
         elif n in ("u0", "u1"):
             times(q, "pw%d tl" % (1 - x[0]), "uw%d" % x[0], plane(T.uw, x[0]), plane(T.pw, 1 - x[0]).indirect(T.tl[:, :]))
+        elif n == "n0" and q:
+            act("uw0 sn%d" % r, K("km"), T.km[:, :], T.uw[:, 0:C].indirect(sn[:, 0:22]))
         elif n == "n0":
             tten("uw0 sn%d m16" % r, K("km"), T.km[:, :], T.uw[:, 0:C].indirect(sn[:, 0:22]), T.m16[:, :], OP.mult)
         elif n == "n1" and r < 2:
             act("uw1 sn%d" % r, "t1", T.t1[:, :], T.uw[:, C:704].indirect(sn[:, 22:44]))
         elif n == "ns0":
-            ts(K("ksn"), "tx", ns[:, 0:22], T.ksn[:, L], 176.0, None, OP.add)
+            k = "kh" if q else "ksn"
+            ts(K(k) + "cg7", "tx", ns[:, 0:22], T[k][:, L], 0.25, cg[:, 7:8] if q else 176.0, OP.mult, OP.add)
         elif n == "nh" and r < 2:
-            hold("t1 mx", K("kh"), T.kh[:, :], T.mx[:, :], T.t1[:, :])
+            hold("t1 mx", K("ln"), T.ln[:, :], T.mx[:, :], T.t1[:, :])
         elif n == "ns1" and r < 2:
-            ts(K("kh") + "cg2", "sn%d" % (r + 1), ns[:, 22:44], T.kh[:, L], cg[:, 2:3], None, OP.add)
+            ts(K("ln") + "cg7", "sn%d" % (r + 1), ns[:, 22:44], T.ln[:, L], 0.25, cg[:, 7:8], OP.mult, OP.add)
             send_list(r + 1)
         elif n == "sf":
             cp("tx sn%d" % r, "sf", T.sf[:, :], sn[:, 0:44])
         elif n == "sd":
             tten("sf", "fb", T.fb[:, 44:88:2], T.sf[:, 22:44], T.sf[:, 0:22], OP.subtract)
+        elif n == "so":
+            for b in range(2):
+                act("uw%d sn2" % b, "tw cw0", plane(T.tw, b), plane(T.uw, b).indirect(T.sn2[:, 22 * b:22 * b + 22]), AF.Identity, scale=0.25, bias=176.0)
+            dma("s", "d_so", "tw", "so", T.so[:, :], T.tw[0:128:16, :])
         elif n == "vq":
             op("v", "vb", "vq", V.quantize_mx, T.vq[:, :], T.vs[:, :], T.vb[:, :])
-        elif n[0] == "e" and x:
+        elif n[0] == "e":
             a, m = PART[x[0]]
-            for b in x[1:] or range(4):
-                k, ps = bank(x[0], b)
-                mm("eq dq%d%d" % (r - 1, x[0]), k, ps, T.eq[:, 128 * b:128 * b + 128], T.es[:, 128 * b:128 * b + 128],
-                   T["dq%d" % (r - 1)][:, a:a + m], T["ds%d" % (r - 1)][:, a:a + m])
-        elif n[0] == "d" and len(x) == 2:
+            b = x[1]
+            k, ps = bank(x[0], b)
+            mm("eq dq%d%d" % (r - 1, x[0]), k, ps, T.eq[:, 128 * b:128 * b + 128], T.es[:, 128 * b:128 * b + 128],
+               T["dq%d" % (r - 1)][:, a:a + m], T["ds%d" % (r - 1)][:, a:a + m])
+        elif n[0] == "d":
             a, m = PART[x[0]]
             k, ps = bank(x[0], x[1])
             times(q, k, "dw%d%d" % (x[0], x[1]), T.dw[:, C * x[1] + a:C * x[1] + a + m], ps)
         elif n[0] == "x":
             a, m = XH[x[0]]
-            for b in x[1:] or range(4):
-                v = slice(64 + 4 * a + b, 64 + 4 * a + 4 * m, 4)
-                tten("tx xp%d%d dw0%d dw1%d" % (r - 1, x[0], b, b), "xp%d%d" % (r, x[0]), XP[:, v],
-                     plane(T.dw, b).indirect(sn[:, a // 16:(a + m) // 16]), T["xp%d" % (r - 1)][:, v], OP.add)
+            b = x[1]
+            v = slice(64 + 4 * a + b, 64 + 4 * a + 4 * m, 4)
+            tten("tx xp%d%d%d dw0%d dw1%d" % (r - 1, x[0], b, b, b), "xp%d%d%d" % (r, x[0], b), XP[:, v],
+                 plane(T.dw, b).indirect(sn[:, a // 16:(a + m) // 16]), T["xp%d" % (r - 1)][:, v], OP.add)
         elif n[0:2] == "qx":
             qx(r, x[0])
         elif n[0:2] == "fb":
@@ -494,15 +537,17 @@ def rank_program(g, core, T, topo):
             act("uq url", "urs1", T.urs[:, 128:256], T.us[:, :].indirect(T.url[:, 8:16]))
         elif n == "mx":
             act("m16", "mx", T.mx[:, :], T.m16[:, :], AF.Identity, scale=-BIG - KM, bias=KM)
+        elif n == "my":
+            ts("m16", "my", T.my[:, :], T.m16[:, :], -260.0, 4.0, OP.mult, OP.add)
+        elif n == "m2a":
+            ts("dn", "m2", T.m2[:, :], T.dn[:, :], 4.0, None, OP.min)
         elif n == "kc":
-            act("cw0", "cb", T.cb[:, :], T.cw[:, 0:C], AF.Identity, scale=1.0 / 32, bias=-176.0)
-        elif n == "m8" and r == 0:
-            act("j16 cn", "tw", T.tw[:, 0:176], T.j16[:, 0:C:2], AF.Abs, bias=T.cn[:, 3:4])
-            for i in (1, 2, 3):
-                act("cf", "cg%d" % (i + 1), cg[:, i + 1:i + 2], columns[i][0], AF.Identity, scale=columns[i][1], bias=columns[i][2])
-            act("tw", "dd", T.dd[:, :], T.tw[:, 0:176], AF.Relu, scale=-1.0, bias=1.0)
-            act("dd", "m8", T.m8[:, :], T.dd[:, :], AF.Identity, scale=-132.0, bias=4.0)
-        elif n[0] == "w" and r == 0:
+            act("cw0", "cb", T.cb[:, :], T.tw[:, 0:C], AF.Identity, bias=-176.0)
+        elif n == "m2b":
+            scan("m2 one", "dd", T.dd[:, 0:16], T.m2[:, 0:16], T.one[:, 0:16])
+        elif n == "m2c":
+            ts("dd", "cg3", cg[:, 3:4], T.dd[:, 15:16], T.dd[:, 15:16], 0.18, OP.mult, OP.mult)
+        elif n[0] == "w" and r == 1:
             v = slice(128 * x[0], 128 * x[0] + 128)
             op("v", "eb", "eq", V.quantize_mx, T.eq[:, v], T.es[:, v], T.eb[:, 512 * x[0]:512 * x[0] + 512])
 
@@ -512,7 +557,6 @@ def rank_program(g, core, T, topo):
 
     send_list(0)
     op("v", "ub", "uq", V.quantize_mx, T.uq[:, :], T.us[:, :], T.ub[:, :])
-    iota("cw0", T.cw[:, 0:C], [[32, C]], 0, 0)
     tten("ge ga0", "ge", T.ge[:, :], T.ge[:, :], T.cq[:, 10:20], OP.add)
     run(0, "sf")
     for i in range(2):
@@ -520,10 +564,8 @@ def rank_program(g, core, T, topo):
     act("uq url", "urs0", T.urs[:, 0:128], T.us[:, :].indirect(T.url[:, 0:8]))
     run(0, "qx0 s0 qx1 s1 sd")
     cp("ge", "gl", T.gl[:, :], T.ge[:, :])
-    run(0, "mx fb0.a fb1.a")
-    act("cw0", "cw", T.cw[:, C:704], T.cw[:, 0:C], AF.Identity, bias=4.0)
-    run(0, "fb2.a")
-    dma("s", "d_w", "xp00 xp01 ub", "wq", T.wq[:, :].bitcast(dt.uint8), T.wc[:, :])
+    run(0, "kc fb0.a fb1.a fb2.a")
+    dma("s", "d_w", xp(0, 0) + xp(0, 1) + "ub", "wq", T.wq[:, :].bitcast(dt.uint8), T.wc[:, :])
     dma("s", "d_wp", "", "wp", T.wp[:, :], T.ws[:, :])
     dma("s", "d_v", "", "vb", T.vb[:, :], T.v[:, :])
     iota("r16o", T.r16[:, :], [[0, C]], 1, 0)
@@ -536,21 +578,19 @@ def rank_program(g, core, T, topo):
         op("g", "one", "eb", g.affine_select, T.eb[:, 512 * b:512 * b + 512], T.one[:, :], [[-1, 512]], OP.is_equal, 0.0, b, 4)
 
     for r in range(3):
-        run(r, (BITS if r else BITS0) + PATH + (PATH1 if r else PATH0) + SECOND + (LAYER if r < 2 else LAYER2) + TURNS)
+        run(r, (BITS + PATH + PATH1 + SECOND + "z01 " if r else BITS0 + PATH + PATH0 + SECOND0) + LAYER + TURNS)
         run(r + 1, NEXT if r < 2 else LAST)
-    for b in range(2):
-        act("uw%d sn2" % b, "tw", plane(T.tw, b), plane(T.uw, b).indirect(T.sn2[:, 22 * b:22 * b + 22]), AF.Identity, bias=176.0)
-    dma("s", "d_so", "tw", "so", T.so[:, :], T.tw[0:128:16, :])
     for h in range(2):
-        run(3, ("x0 x10 qx0", "x11 x12 x13 qx1")[h])
+        run(3, END[h])
         a, n = XH[h]
         q = slice(16 + a, 16 + a + n)
         mm("vq xq%d" % h, "pa%d" % h, T.pa[:, 512 * h:512 * h + n], T.vq[:, :], T.vs[:, :], T.xq[:, q], T.xs[:, q])
         dma("s", "d_oc", "xq%d" % h, "oc%d" % h, T.oc[:, 4 * a:4 * a + 4 * n], T.xq[:, q].bitcast(dt.uint8))
+        if h:
+            for k in range(4):
+                dma("sa"[k % 2], "d_oc", "xq0 xq1", "osc%d" % k, T.osc[4 * k:4 * k + 4, :], T.xs[32 * k:32 * k + 4, 16:368])
         times("av"[h], "pa%d" % h, "yb%d" % h, T.yb[:, a:a + n], T.pa[:, 512 * h:512 * h + n])
-        dma("a", "d_y", "yb%d" % h, "y%d" % h, T.y[:, a:a + n], T.yb[:, a:a + n])
-    for k in range(4):
-        dma("s", "d_oc", "xq0 xq1", "osc%d" % k, T.osc[4 * k:4 * k + 4, :], T.xs[32 * k:32 * k + 4, 16:368])
+        dma("sa"[h], "d_y", "yb%d" % h, "y%d" % h, T.y[:, a:a + n], T.yb[:, a:a + n])
     total["ls"] = sent[0]
     for s in total:
         g.wait_ge(T.sem[s], total[s])

@@ -5,9 +5,10 @@ C = 352
 MASK = [2, 4, 1]
 PART = [(0, 192), (192, 160)]
 XH = [(0, 224), (224, 128)]
+HALF = PART[1][0] // 16
 KM, BIG = 32768.0, 2097152.0
-UNIT = 2.0 ** -15
-ROWS = [1, 6]
+ROWS = [1, 6, 3]
+BANKS = {"1": 6, "6": 7, "30": 0, "31": 1}
 BF, F32, I32, U16, U8, E4 = "bfloat16", "float32", "int32", "uint16", "uint8", "float8_e4m3fn_x4"
 SCRATCH = {
     "sei": ("sbuf", [128, 44], I32), "ub": ("sbuf", [128, 512], BF), "vb": ("sbuf", [128, 512], BF),
@@ -15,28 +16,29 @@ SCRATCH = {
     "uq": ("sbuf", [128, 128], E4), "us": ("sbuf", [128, 128], U8), "vq": ("sbuf", [128, 128], E4), "vs": ("sbuf", [128, 128], U8),
     "urq": ("sbuf", [128, 384], E4), "urs": ("sbuf", [128, 384], U8),
     "pc": ("sbuf", [128, 8], I32), "ci": ("sbuf", [128, 8], I32), "cf": ("sbuf", [128, 8], F32), "cg": ("sbuf", [128, 12], F32),
-    "cn": ("sbuf", [128, 4], F32),
-    "j16": ("sbuf", [128, C], F32), "cw": ("sbuf", [128, 704], F32), "cb": ("sbuf", [128, C], BF),
-    "m16": ("sbuf", [128, C], BF), "r16": ("sbuf", [128, C], BF), "mx": ("sbuf", [128, C], BF), "my": ("sbuf", [128, C], BF),
-    "m2": ("sbuf", [128, C], BF),
-    "cq": ("sbuf", [128, 24], F32), "cl": ("sbuf", [128, 24], F32), "ga": ("sbuf", [128, 10], I32), "gb": ("sbuf", [128, 10], F32),
-    "ge": ("sbuf", [128, 10], F32), "gl": ("sbuf", [128, 10], U16), "url": ("sbuf", [128, 24], U16),
+    "cn": ("sbuf", [128, 4], F32), "sq": ("sbuf", [128, C], BF),
+    "j16": ("sbuf", [128, C], F32), "cw": ("sbuf", [128, 3 * C], F32), "cb": ("sbuf", [128, C], BF),
+    "m16": ("sbuf", [128, C], BF), "r16": ("sbuf", [128, C], BF), "mx": ("sbuf", [128, C], BF), "m2": ("sbuf", [128, C], BF),
+    "cq": ("sbuf", [128, 24], F32), "cl": ("sbuf", [128, 24], F32), "ga": ("sbuf", [128, 10], I32), "gb": ("sbuf", [128, 40], F32),
+    "gl": ("sbuf", [128, 10], U16), "url": ("sbuf", [128, 24], U16),
     "one": ("sbuf", [128, 512], BF), "eb": ("sbuf", [128, 2048], BF), "eq": ("sbuf", [128, 512], E4), "es": ("sbuf", [128, 512], U8),
     "xq": ("sbuf", [128, 384], E4), "xs": ("sbuf", [128, 384], U8), "xh": ("sbuf", [128, 1408], BF),
-    "b1": ("sbuf", [128, C], BF), "b6": ("sbuf", [128, C], BF),
+    "b1": ("sbuf", [128, C], BF), "b6": ("sbuf", [128, C], BF), "b3": ("sbuf", [128, C], BF),
     "tt": ("sbuf", [128, 736], F32), "fm": ("sbuf", [128, 320], F32), "fb": ("sbuf", [128, 308], F32),
     "fo": ("sbuf", [128, 308], F32), "fl": ("sbuf", [128, 132], U16), "sf": ("sbuf", [128, 44], F32),
     "la": ("sbuf", [128, C], F32), "lb": ("sbuf", [128, C], F32), "lm": ("sbuf", [128, C], F32), "ln": ("sbuf", [128, C], F32),
-    "ha": ("sbuf", [128, 704], F32), "hc": ("sbuf", [128, 704], F32), "hd": ("sbuf", [128, C], F32),
+    "lw": ("sbuf", [128, 704], F32), "ha": ("sbuf", [128, 704], F32), "hc": ("sbuf", [128, C], F32), "hd": ("sbuf", [128, C], F32),
+    "hm": ("sbuf", [128, C], F32), "hn": ("sbuf", [128, C], F32),
     "i3": ("sbuf", [128, 22], U16), "i6": ("sbuf", [128, 22], U16), "vi": ("sbuf", [128, 22], I32), "vj": ("sbuf", [128, 22], I32),
-    "va": ("sbuf", [128, 110], I32), "jf": ("sbuf", [128, 132], F32),
-    "pw": ("sbuf", [128, 704], BF), "s2": ("sbuf", [128, 1408], BF), "km": ("sbuf", [128, C], BF), "ksn": ("sbuf", [128, C], BF),
-    "kh": ("sbuf", [128, C], F32), "ki": ("sbuf", [128, 22], F32), "kb": ("sbuf", [128, 22], F32),
+    "va": ("sbuf", [128, 44], I32), "jf": ("sbuf", [128, 132], F32),
+    "pw": ("sbuf", [128, 704], BF), "s2": ("sbuf", [128, 1408], BF), "km": ("sbuf", [128, 6 * C], BF), "ks": ("sbuf", [128, 6 * C], BF),
+    "kh": ("sbuf", [128, 5 * C], F32), "ki": ("sbuf", [128, 66], F32),
     "k0": ("sbuf", [128, 22], U16), "k2": ("sbuf", [128, 22], U16), "k4": ("sbuf", [128, 22], U16), "k6": ("sbuf", [128, 22], U16),
-    "en": ("sbuf", [128, C], BF), "dd": ("sbuf", [128, 22], F32), "dn": ("sbuf", [128, C], BF), "tf": ("sbuf", [128, 22], F32),
-    "tg": ("sbuf", [128, 22], F32), "tl": ("sbuf", [128, 22], U16), "uw": ("sbuf", [128, 704], BF), "t1": ("sbuf", [128, C], BF),
+    "en": ("sbuf", [128, C], BF), "dd": ("sbuf", [128, 40], F32), "dn": ("sbuf", [128, C], BF), "tf": ("sbuf", [128, 22], F32),
+    "tg": ("sbuf", [128, 22], F32), "tl": ("sbuf", [128, 22], U16), "uw": ("sbuf", [128, 704], BF),
     "tw": ("sbuf", [128, 704], F32),
     "gi": ("sbuf", [128, 1408], BF), "z": ("sbuf", [128, 1408], BF), "zq": ("sbuf", [128, C], E4), "zs": ("sbuf", [128, C], U8),
+    "gs": ("sbuf", [128, 640], BF), "gx": ("sbuf", [128, 512], BF), "alt": ("sbuf", [128, 640], BF),
     "hb": ("sbuf", [128, 1408], BF), "dw": ("sbuf", [128, 1408], BF), "yb": ("sbuf", [128, C], F32),
     "pa": ("psum", [128, 2048], F32), "pb": ("psum", [128, 2048], F32),
 }
@@ -48,7 +50,7 @@ for _r in range(3):
     SCRATCH["pl%d" % _r] = ("sbuf", [128, 44], U16)
     SCRATCH["hq%d" % _r] = ("sbuf", [128, C], E4)
     SCRATCH["hs%d" % _r] = ("sbuf", [128, C], U8)
-    SCRATCH["fq%d" % _r] = ("sbuf", [128, 112], E4)
+    SCRATCH["fq%d" % _r] = ("sbuf", [128, 128], E4)
     SCRATCH["fs%d" % _r] = ("sbuf", [128, 224], U8)
     SCRATCH["dq%d" % _r] = ("sbuf", [128, C], E4)
     SCRATCH["ds%d" % _r] = ("sbuf", [128, C], U8)
@@ -56,23 +58,30 @@ SEMAPHORES = ["sv", "sa", "sp", "sg", "ls"] + ["d_" + n for n in ("se", "x", "x2
 for _r in range(3):
     SEMAPHORES += [n + str(_r) for n in ("hl", "hc", "hp", "la", "ca", "cb")]
 CODES = [(0, 1), (2, 3)]
-SCALES = [2, 0]
-LISTS = [(0, 1, 2, 3), (3,), (3,)]
+SCALES = [3, 0]
+LISTS = [(0, 1, 2, 3), (2,), (2,)]
 
-BITS = "qx1 s1 m1 m6 t3.a xh1.a ts0 xh0.v tr1 ts1 b1 t2.a fm1 fm0 fo1 fo0 fl1 fl0 "
-BITS0 = "m1 tr0 ts0 tr1 ts1 xh0.v xh1.a b1 fm1 fm0 fo1 fo0 fl1 fl0 my mx "
-PATH = "la haA.a haB.a ha2A.a ha2B.a xh3.v lb hcA.a hcB.a hc2A.a hc2B.a xh2.v lmA lmB lnA lnB hdA.a hdB.a "
-PATH1 = "viA p0A viB va0A p0B k0A va0B i3A k0B hmA g0A i3B hmB g0B hA va1 hB hnA kbA hnB kbB p2A vj p2B k2A va2 k2B "
-PATH0 = ("j0 viA viB j1 va0A va4 va0B j2 i3A j3 i3B pw1.v j4 hmA hmB j5 pw0.a hnB j6 r6 m6 hnA j7 va1 vj h t2.a t3.a va2 va3 kb t1.v t0.a "
-         "p2A p2B k2A k2B i6 b6 ")
-SECOND = "g2A g2B.a i6 va3 hA hB.a p4A p4B.a k4A k4B.a gi0A gi1A g4A g4B.a hA hB.a gi2A gi3A gi0B gi1B gi2B gi3B k6A k6B.a z00 b6 en "
-SECOND0 = "g2A g2B.a m2a hA hB.a p4A p4B.a k4A k4B.a gi0A g4A g4B.a m2b hA hB.a gi1A gi2A gi3A gi0B gi1B k6A m2c k6B.a z00 z01 gi2B gi3B en "
-LAYER = "z02 z03 z10 q0 z11 c00.a c01.a z12 c03.a z13 dn q1 dd c02.v tf tg h0q tl c10.a c12.a c13.a c11.v u1.a u0.v h1q "
-TURNS = "n0 n1 h nh ns0 ns1 "
-NEXT = ("w0 w1 w2 w3 e00 e01 e03 e10 e11 e02 e12 e13 sf d00.v sd fb0.a d03.a d01.v d10.v d02.a d11.v d12.a d13.a "
-        "x00 pw1.a x01 fb1.a pw0.a x02 t0.a x03 fb2.a x10 t1.a qx0 s0 x11 x12 x13 tr0 ")
-LAST = "so e00 e01 e02 e03 e10 e11 e12 e13 vq d00.v d01.v d02.a d03.a d10.v d11.v d12.a d13.a "
-END = ("x00 x01 x02 x03 x10 qx0", "x11 x12 x13 qx1")
+START = ("Lse Lu Lx0 Lx1 Ipc Icq Ij fmz pad0 pad1 ci2 ci1 ci3 ci0 cf url1 url0 url2 cl Ifb Icw cg0 sn cn ga uq ge cg6 cg4 fbd cg7 sq r3 r1 gz gb "
+         "sf ur2 sd ge2 qx0 ge3 s0 m30 ur0 gl qx1 s1 Lw Ir Ione Ie Ipad Ialt m31 cw2 fb0.a cw1 fb1.a m1 b30 m16 r6 b31 cw0 b1 kc mx ")
+BITS0 = "tr0 ts0 tr1 ts1 fb2.v lw00 fm1 fm0 lw10 fo1 fo0 lw1 fl1 fl0 ur1 "
+PATH0 = ("laB.a ha laA.v ge1 lbB.a lbA.v j0 he ha2 cg5 lmA j1 j3 lmB j2 j4 lnA lnB hc pw0.a hd j5 pw1.v j6 vi i3 t1.v j7 "
+         "va1 xh0.v h0A h0B t3.a hm t2.a t0.a hnA m6 ")
+SECOND0 = ("p2A hnB p2B k2A xh12.v i6 k2B xh13.v vj g2A xh1.a g2B.a va3 m2a h2A h2B p4A xh02.v p4B k4A xh03.v k4B g4A gi02.v h4A gi01 gi0 "
+           "g4B.a h4B k6A m2b k6B gi03 gi13 gi11 zk3 zk1 b6 gi12 ")
+LAYER0 = "z00 z02 z03 z01 zs q0 z10 z12 en c00.a c01.a dn q1 c03.a m2c c02.v dd tf h0q tg c10.a c11.a c12.a c13.v tl u1.a h1q "
+TURNS0 = "u0.v n0 w1 n1.a h8B h6 h8A ns0 w0 ns1 w2 w3 "
+NEXT = ("sf e01 e00 sd fb0.a fb2.a d01.a d00.v e10 e11 e02 e12 e03 e13 d02.a d10.v d11.v d12.a d03.a d13.a pw0.a pw1.a t3.a t1.a "
+        "x0 x01 x2 x03 x11 qx0 s0 m30 x13 fb1.v qx1 b30 s1 m31 m6 m1 xh02.v ")
+BITS = "tr0 ts0 tr1 ts1 lw00 fm1 t0.a b31 t2.a b1 fm0 lw01 fo1 lw11 fo0 lw10 fl1 xh03.v fl0 "
+PATH = "laB.a ha laA.v ge1 lbB.a lbA.v he lmA p0 lmB k0 lnA ha2 lnB g0A vi i3 g0B h0A va1 xh01.v h0B "
+SECOND = ("p2A xh11.v p2B hc xh12.a hd hmA hmB k2A hnA g2A.a xh13.a k2B hnB g2B vj i6 h2A va3A va3B h2B p4A xh0.v p4B k4A k4B g4A b6 g4B "
+          "h4A h4B k6A k6B gi13 gi02 gi03 gi00 gi11 gi01 zk1 zk3 gi10 gi12 ")
+LAYER = "z02 z03 z01 z00 zs q0 z10 z12 en c00.a c01.a dn q1 c03.a c02.v dd tf h0q tg c10.a c11.a c12.a c13.v tl h1q u1.a "
+TURNS = "u0.v n0 n1.a h8B h8A h6 ns0 ns1 "
+LAST = ("e01 e00 e03 xc d01.v vq d03.v e11 e10 e12 e02 e13 d11.v d00.a d10.v d12.a d02.a d13.a xk1 xk3 so x01 x00 x02 x03 xs qx0 y0 oc0 "
+        "x10 x12 yc0.a qx1 y1 oc1 osc yc1.v")
+ROUND = NEXT + BITS + PATH + SECOND + LAYER + TURNS
+ORDER = [(0, START + BITS0 + PATH0 + SECOND0 + LAYER0 + TURNS0), (1, ROUND), (2, ROUND), (3, LAST)]
 
 
 def route(topo, core, dst):
@@ -204,6 +213,12 @@ def rank_program(g, core, T, topo):
         else:
             ts(r, w, out, in_, c, None, OP.mult)
 
+    def affine(q, r, w, out, in_, a, b):
+        if q == "a":
+            act(r, w, out, in_, AF.Identity, scale=a, bias=b)
+        else:
+            ts(r, w, out, in_, a, b, OP.mult, OP.add)
+
     def mm(r, w, out, wq, wsc, xq, xsc):
         op("p", r, w, P.matmul_mx, out, wq, wsc, xq, xsc, True, True)
 
@@ -218,48 +233,11 @@ def rank_program(g, core, T, topo):
     def xp(r, h):
         return "".join("xp%d%d%d " % (r, h, b) for b in range(4))
 
-    dma("s", "d_se", "", "sei", T.sei[:, :], T.se[:, :])
-    dma("a", "d_u", "", "ub", T.ub[:, :], T.u[:, :])
-    dma("s", "d_x", "", xp(0, 0), T.xp0[:, 64:64 + 4 * XH[1][0]], T.x[:, 0:4 * XH[1][0]])
-    dma("s", "d_x2", "", xp(0, 1), T.xp0[:, 64 + 4 * XH[1][0]:1472], T.x[:, 4 * XH[1][0]:1408])
-    op("g", "", "pc", g.iota, T.pc[:, 0:1], [[0, 1]], 0, 1)
-    iota("cq", T.cq[:, :], [[16, 24]], 0, 0)
-    iota("j16", T.j16[:, :], [[0, 22], [1, 16]], 0, 0)
-    iota("fbc", T.fb[:, 0:44:2], [[0, 22]], 1, 0)
-    iota("cw0", T.tw[:, 0:C], [[1, C]], 0, 0)
-    op("v", "", "pad0", V.memset, T.xp0[:, 0:64], 0.0)
-    op("v", "", "pad0", V.memset, T.xp0[:, 1472:1536], 0.0)
     ci, cf, cg = T.ci, T.cf, T.cg
-    ts("pc", "ci", ci[:, 0:1], T.pc[:, 0:1], 15, None, OP.bitwise_and)
-    ts("pc", "ci", ci[:, 1:2], T.pc[:, 0:1], 4, 1, OP.logical_shift_right, OP.bitwise_and)
-    ts("pc", "ci", ci[:, 2:3], T.pc[:, 0:1], 1, None, OP.bitwise_and)
-    ts("pc", "ci", ci[:, 3:4], T.pc[:, 0:1], 14, None, OP.bitwise_and)
-    for i, l in enumerate(ROWS):
-        ts("cq", "url", T.url[:, 8 * i:8 * i + 8], T.cq[:, 0:8], float(l), None, OP.add)
-    cp("ci", "cf", cf[:, 0:4], ci[:, 0:4])
-    op("v", "", "fm", V.memset, T.fm[:, 0:320:2], 0.0)
     PR, PH, PP, PE = (cf[:, i:i + 1] for i in range(4))
-    ts("cq cf", "cl", T.cl[:, :], T.cq[:, :], PR, None, OP.add)
-    ts("cf", "cg0", cg[:, 0:1], PH, PP, 368.0, OP.not_equal, OP.mult)
-    ts("cf", "cn", T.cn[:, :], cf[:, 0:4], -1.0, None, OP.mult)
-    columns = {1: (PR, 4.0, -60.0), 4: (PP, -2.0, 1.0), 5: (PR, 4.0, 704 - 60.0), 6: (PR, KM, 704 - 15 * KM),
-               7: (PR, KM / 4, 176 - 15 * KM / 4), 8: (PR, KM + 4, 704 - 60.0 - 15 * KM)}
-
-    for i in columns:
-        act("cf", "cg%d" % i, cg[:, i:i + 1], columns[i][0], AF.Identity, scale=columns[i][1], bias=columns[i][2])
-    act("j16 cn", "dn", T.dn[:, :], T.j16[:, :], AF.Square, bias=T.cn[:, 3:4])
-    act("cl", "fbd", T.fb[:, 1:44:2], T.cl[:, 0:22], scale=4.0)
-    for i in range(2):
-        act("cw0", "cw", T.cw[:, C * i:C * i + C], T.tw[:, 0:C], AF.Identity, scale=32 * UNIT, bias=8 * UNIT * i)
-    ts("cl", "ga", T.ga[:, :], T.cl[:, 0:10], 1.0 / 22, -0.477, OP.mult, OP.add)
-    ts("cl cg0", "ge", T.ge[:, :], T.cl[:, 0:10], 16.0, cg[:, 0:1], OP.mult, OP.add)
-    ts("ga", "gb", T.gb[:, :], T.ga[:, :], -351.0, -1.0, OP.mult, OP.add)
-    ts("ga", "ga0", T.cq[:, 10:20], T.ga[:, :], 0.0, None, OP.is_equal)
-    ts("j16 cf", "m16", T.m16[:, :], T.j16[:, :], PR, None, OP.is_equal)
-    cp("sei", "sn0", T.sn0[:, 0:44], T.sei[:, :])
-    tten("gb ge", "ge", T.ge[:, :], T.ge[:, :], T.gb[:, :], OP.add)
-
+    columns = {4: (PP, -2.0, 1.0), 5: (PR, KM / 4, -0.375 - 15 * KM / 4), 6: (PR, KM, 704 - 15 * KM), 7: (PR, KM / 4, 176 - 15 * KM / 4)}
     sent = [0]
+    held = {}
 
     def partner(r):
         return T.cores[rank ^ MASK[r]]
@@ -299,17 +277,6 @@ def rank_program(g, core, T, topo):
         hp = route(topo, partner(r), core)
         arrived("dq%d%d" % (r, h), ("ca%d", "cb%d")[h] % r, sum(len(topo.engines(hp[k], core)) for k in CODES[h] + (SCALES[h],)))
 
-    def repeat_lists(i, q):
-        if i == 0:
-            times(q, "sf", "fb1", T.fb[:, 45:88:2], T.sf[:, 0:22])
-            times(q, "sf", "fb1", T.fb[:, 133:176:2], T.sf[:, 0:22])
-            act("fb", "fb1", T.fb[:, 132:176:2], T.fb[:, 44:88:2], AF.Identity, bias=352.0)
-        elif i == 1:
-            times(q, "fb fb1", "fb2", T.fb[:, 88:132], T.fb[:, 44:88])
-            times(q, "fb1", "fb2", T.fb[:, 176:220], T.fb[:, 132:176])
-        else:
-            times(q, "fb1 fb2", "fb3", T.fb[:, 220:308], T.fb[:, 132:220])
-
     def bank(h, b):
         n = PART[h][1]
         return ("pb%d" if h else "pa%d") % b, (T.pb if h else T.pa)[:, 512 * b:512 * b + n]
@@ -317,28 +284,123 @@ def rank_program(g, core, T, topo):
     def plane(t, b):
         return t[:, C * b:C * b + C]
 
-    def qx(r, h):
-        a, n = 16 + XH[h][0], XH[h][1]
-        if r < 3:
-            a, n = a - 16 * (1 - h), n + 16
-        op("v", xp(r, h) + "pad%d" % r, "xq%d" % h, V.quantize_mx, T.xq[:, a:a + n], T.xs[:, a:a + n], T["xp%d" % r][:, 4 * a:4 * a + 4 * n])
-
-    def scores(h):
-        a, n = XH[h][0], XH[h][1] + 16 + 16 * h
-        mm("uq xq0" + " xq1" * h, "pb%d" % h, T.pb[:, 512 * h:512 * h + n], T.uq[:, :], T.us[:, :], T.xq[:, a:a + n], T.xs[:, a:a + n])
-
-    def rows_bank(i):
-        return "pb%d" % (2 + i), T.pb[:, 1024 + 512 * i:1024 + 512 * i + C]
-
     S2 = "s20 s21 s22 s23 "
+
+    def start(n, q, x):
+        if n == "Lse":
+            dma("s", "d_se", "", "sei", T.sei[:, :], T.se[:, :])
+        elif n == "Lu":
+            dma("a", "d_u", "", "ub", T.ub[:, :], T.u[:, :])
+        elif n[0:2] == "Lx":
+            a, m = XH[x[0]]
+            dma("s", ("d_x", "d_x2")[x[0]], "", xp(0, x[0]), T.xp0[:, 64 + 4 * a:64 + 4 * a + 4 * m], T.x[:, 4 * a:4 * a + 4 * m])
+        elif n == "Lw":
+            dma("s", "d_w", xp(0, 0) + xp(0, 1) + "ub", "wq", T.wq[:, :].bitcast(dt.uint8), T.wc[:, :])
+            dma("s", "d_wp", "", "wp", T.wp[:, :], T.ws[:, :])
+            dma("s", "d_v", "", "vb", T.vb[:, :], T.v[:, :])
+        elif n == "Ipc":
+            op("g", "", "pc", g.iota, T.pc[:, 0:1], [[0, 1]], 0, 1)
+        elif n == "Icq":
+            iota("cq", T.cq[:, :], [[16, 24]], 0, 0)
+        elif n == "Ij":
+            iota("j16", T.j16[:, :], [[0, 22], [1, 16]], 0, 0)
+        elif n == "Ifb":
+            iota("fbc", T.fb[:, 0:44:2], [[0, 22]], 1, 0)
+        elif n == "Ipad":
+            for r in (1, 2):
+                iota("pad%d" % r, T["xp%d" % r][:, 0:64], [[0, 64]], 0, 0)
+                iota("pad%d" % r, T["xp%d" % r][:, 1472:1536], [[0, 64]], 0, 0)
+        elif n == "Icw":
+            iota("iw", T.tw[:, 0:C], [[1, C]], 0, 0)
+        elif n == "Ir":
+            iota("r16o", T.r16[:, :], [[0, C]], 1, 0)
+            op("g", "r16o", "r16", g.iota, T.r16[:, 0:C:16], [[0, 22]], 0, 0, allow_small_or_imprecise_dtypes=True)
+        elif n == "Ione":
+            iota("one", T.one[:, :], [[0, 512]], 1, 0)
+        elif n == "Ialt":
+            iota("alt", T.alt[:, :], [[0, 320], [1, 2]], 0, 0)
+        elif n == "Ie":
+            for b in range(4):
+                op("g", "one", "eb%d" % b, g.affine_select, T.eb[:, 512 * b:512 * b + 512], T.one[:, :], [[-1, 512]], OP.is_equal, 0.0, b, 4)
+        elif n[0:3] == "pad":
+            op("v", "", "pad0", V.memset, T.xp0[:, 1472 * x[0]:1472 * x[0] + 64], 0.0)
+        elif n == "ci1":
+            ts("pc", n, ci[:, 1:2], T.pc[:, 0:1], 4, 1, OP.logical_shift_right, OP.bitwise_and)
+        elif n[0:2] == "ci":
+            ts("pc", n, ci[:, x[0]:x[0] + 1], T.pc[:, 0:1], (15, 0, 1, 14)[x[0]], None, OP.bitwise_and)
+        elif n[0:3] == "url":
+            ts("cq", n, T.url[:, 8 * x[0]:8 * x[0] + 8], T.cq[:, 0:8], float(ROWS[x[0]]), None, OP.add)
+        elif n == "cf":
+            cp("ci0 ci1 ci2 ci3", "cf", cf[:, 0:4], ci[:, 0:4])
+        elif n == "fmz":
+            op("v", "", "fm", V.memset, T.fm[:, 0:320:2], 0.0)
+        elif n == "cl":
+            ts("cq cf", "cl", T.cl[:, :], T.cq[:, :], PR, None, OP.add)
+        elif n == "cg0":
+            ts("cf", "cg0", cg[:, 0:1], PH, PP, 368.0, OP.not_equal, OP.mult)
+        elif n[0:2] == "cg":
+            affine("a", "cf", n, cg[:, x[0]:x[0] + 1], *columns[x[0]])
+        elif n == "cn":
+            ts("cf", "cn", T.cn[:, :], cf[:, 0:4], -1.0, None, OP.mult)
+        elif n == "sq":
+            act("j16 cn", "sq", T.sq[:, :], T.j16[:, :], AF.Square, bias=T.cn[:, 3:4])
+        elif n == "fbd":
+            times("a", "cl", "fbd", T.fb[:, 1:44:2], T.cl[:, 0:22], 4.0)
+        elif n[0:2] == "cw":
+            affine("a", "iw", n, plane(T.cw, x[0]), T.tw[:, 0:C], 4.0, (0.0, 2.0, 1.0)[x[0]])
+        elif n == "ga":
+            ts("cl", "ga", T.ga[:, :], T.cl[:, 0:10], 1.0 / 22, -0.477, OP.mult, OP.add)
+        elif n == "ge":
+            ts("cl cg0", "ge", T.gb[:, 10:20], T.cl[:, 0:10], 16.0, cg[:, 0:1], OP.mult, OP.add)
+        elif n == "gb":
+            ts("ga", "gb", T.gb[:, 0:10], T.ga[:, :], -351.0, -1.0, OP.mult, OP.add)
+        elif n == "gz":
+            ts("ga", "gz", T.gb[:, 20:30], T.ga[:, :], 0.0, None, OP.is_equal)
+        elif n == "ge2":
+            tten("gb ge", "ge2", T.gb[:, 30:40], T.gb[:, 10:20], T.gb[:, 0:10], OP.add)
+        elif n == "ge3":
+            tten("ge2 gz", "ge", T.gb[:, 10:20], T.gb[:, 30:40], T.gb[:, 20:30], OP.add)
+        elif n == "gl":
+            cp("ge", "gl", T.gl[:, :], T.gb[:, 10:20])
+        elif n == "m16":
+            ts("j16 cf", "m16", T.m16[:, :], T.j16[:, :], PR, None, OP.is_equal)
+        elif n == "mx":
+            affine("a", "m16", "mx", T.mx[:, :], T.m16[:, :], -BIG - KM, KM)
+        elif n == "m2a":
+            ts("sq", "m2", T.m2[:, :], T.sq[:, :], 4.0, None, OP.min)
+        elif n == "m2b":
+            scan("m2 one", n, T.dd[:, 24:40], T.m2[:, 0:16], T.one[:, 0:16])
+        elif n == "m2c":
+            ts("m2b", "cg3", cg[:, 3:4], T.dd[:, 39:40], T.dd[:, 39:40], 0.18, OP.mult, OP.mult)
+        elif n == "kc":
+            affine("a", "iw", "cb", T.cb[:, :], T.tw[:, 0:C], 1.0, -176.0)
+        elif n == "sn":
+            cp("sei", "sn0 tx", T.sn0[:, 0:44], T.sei[:, :])
+            send_list(0)
+        elif n in ("uq", "vq"):
+            op("v", n[0] + "b", n, V.quantize_mx, T[n][:, :], T[n[0] + "s"][:, :], T[n[0] + "b"][:, :])
+        elif n in ("ur0", "ur1", "ur2"):
+            i = x[0]
+            cp("uq url%d" % i, n, T.urq[:, 128 * i:128 * i + 128].bitcast(dt.uint32), T.uq[:, :].bitcast(dt.uint32).indirect(T.url[:, 8 * i:8 * i + 8]))
+        elif n in ("r1", "r6", "r3"):
+            i = ROWS.index(x[0])
+            act("uq url%d" % i, "urs%d" % i, T.urs[:, 128 * i:128 * i + 128], T.us[:, :].indirect(T.url[:, 8 * i:8 * i + 8]))
+        elif n[0] == "w":
+            v = slice(128 * x[0], 128 * x[0] + 128)
+            op("v", "eb%d" % x[0], "eq%d" % x[0], V.quantize_mx, T.eq[:, v], T.es[:, v], T.eb[:, 512 * x[0]:512 * x[0] + 512])
+        else:
+            return False
+        return True
 
     def step(r, name):
         n, q = (name.split(".") + [None])[0:2]
         parts = n[-1] if n[-1] in "AB" else "AB"
         n = n.rstrip("AB")
         x = [int(ch) for ch in n if ch.isdigit()]
+        if start(n, q, x):
+            return
         sn, ns, XP = T["sn%d" % r], T["sn%d" % min(r + 1, 3)], T["xp%d" % r]
-        lo, hi = (0 if "A" in parts else PART[1][0] // 16), (C // 16 if "B" in parts else PART[1][0] // 16)
+        lo, hi = (0 if "A" in parts else HALF), (C // 16 if "B" in parts else HALF)
         Q, W, L = slice(lo, hi), slice(16 * lo, 16 * hi), slice(16 * lo + 15, 16 * hi, 16)
 
         def K(k):
@@ -348,28 +410,53 @@ def rank_program(g, core, T, topo):
             return T.fl[:, 22 * l + lo:22 * l + hi]
 
         def VA(i):
-            return T.va[:, 22 * i + lo:22 * i + hi]
+            return T.va[:, 11 * (i - 1) + lo:11 * (i - 1) + hi]
+
+        def KI(i):
+            return T.ki[:, 11 * i + lo:11 * i + hi]
+
+        def at(t, i, v):
+            return t[:, 176 * i + v.start:176 * i + v.stop:v.step or 1]
+
+        def gather(i, k, win):
+            for p in parts:
+                held[(r, i, p)] = q == "a"
+            if q == "a":
+                act(k, K("km%d" % i), at(T.km, i, W), win)
+            else:
+                tten(k + " m16", K("km%d" % i), at(T.km, i, W), win, T.m16[:, W], OP.mult)
+
+        def listed(i):
+            (h,) = {held[(r, i, p)] for p in parts}
+            return K("ks%d" % i), at(T.kh if h else T.ks, i, L), h
+
+        def cols():
+            return (XH[x[0]] if len(x) == 2 else (0, C)) + (x[-1], x[0:1] if len(x) == 2 else [0, 1])
 
         if n in ("s0", "s1"):
-            scores(x[0])
-        elif n in ("m1", "m6"):
-            i = ROWS.index(x[0])
-            k, o = rows_bank(i)
-            mm("ur%d urs%d xq0 xq1" % (i, i), k, o, T.urq[:, 128 * i:128 * i + 128], T.urs[:, 128 * i:128 * i + 128], T.xq[:, 16:368], T.xs[:, 16:368])
-        elif n in ("b1", "b6"):
-            k, o = rows_bank(ROWS.index(x[0]))
-            act(k, n, T[n][:, :], o, AF.Sign, bias=-2.0 ** -93)
+            h = x[0]
+            a, m = XH[h][0], XH[h][1] + 16 + 16 * h
+            mm("uq xq0" + " xq1" * h, "pb%d" % h, T.pb[:, 512 * h:512 * h + m], T.uq[:, :], T.us[:, :], T.xq[:, a:a + m], T.xs[:, a:a + m])
+        elif n[0] in "mb" and n[1:] in BANKS:
+            i, j = ROWS.index(x[0]), BANKS[n[1:]]
+            a, m = XH[x[1]] if len(x) == 2 else (0, C)
+            k, o = "p%s%d" % ("ab"[j // 4], j % 4), (T.pa, T.pb)[j // 4][:, 512 * (j % 4):512 * (j % 4) + m]
+            if n[0] == "m":
+                mm("ur%d urs%d " % (i, i) + ("xq%d" % x[1] if len(x) == 2 else "xq0 xq1"), k, o, T.urq[:, 128 * i:128 * i + 128],
+                   T.urs[:, 128 * i:128 * i + 128], T.xq[:, 16 + a:16 + a + m], T.xs[:, 16 + a:16 + a + m])
+            else:
+                act(k, n, T[n[0:2]][:, a:a + m], o, AF.Sign, bias=-2.0 ** -93)
         elif n in ("tr0", "tr1"):
             h = x[0]
             a, m = XH[h]
-            op("v", "pb%d" % h, "tt", V.transpose, T.tt[:, a:a + m], T.pb[:, 512 * h + 16:512 * h + 16 + m])
+            op("v", "pb%d" % h, n, V.transpose, T.tt[:, a:a + m], T.pb[:, 512 * h + 16:512 * h + 16 + m])
         elif n in ("ts0", "ts1"):
             h = x[0]
             a, m = XH[h][0], XH[h][1] + 32 * h
-            op("v", "pb%d" % h, "tt", V.transpose, T.tt[:, C + a:C + a + m], T.pb[:, 512 * h:512 * h + m])
+            op("v", "pb%d" % h, n, V.transpose, T.tt[:, C + a:C + a + m], T.pb[:, 512 * h:512 * h + m])
         elif n in ("fm0", "fm1"):
             a, b = ((6, 10), (0, 6))[x[0]]
-            ts("tt fm gl", n, T.fm[:, 32 * a + 1:32 * b:2], T.tt[:, :].indirect(T.gl[:, a:b]), 0.0, None, OP.is_gt)
+            ts("tr0 tr1 ts0 ts1 fm gl", n, T.fm[:, 32 * a + 1:32 * b:2], T.tt[:, :].indirect(T.gl[:, a:b]), 0.0, None, OP.is_gt)
         elif n in ("fo0", "fo1"):
             v = (slice(176, 308), slice(0, 176))[x[0]]
             scan("fm1 fbc fbd fb fb1 fb2 fb3" + " fm0" * (1 - x[0]), n, T.fo[:, v], T.fm[:, v], T.fb[:, v])
@@ -377,37 +464,42 @@ def rank_program(g, core, T, topo):
             a = 66 * (1 - x[0])
             cp("fo%d" % x[0], n, T.fl[:, a:a + 66], T.fo[:, 2 * a + 45:2 * a + 176:2])
         elif n[0:2] == "xh":
-            times(q, "xp%d0%d xp%d1%d" % (r, x[0], r, x[0]), n, plane(T.xh, x[0]), XP[:, 64 + x[0]:1472:4], 0.5)
+            a, m, b, hs = cols()
+            times(q, "".join("xp%d%d%d " % (r, h, b) for h in hs), "".join("xh%d%d " % (h, b) for h in hs),
+                  T.xh[:, C * b + a:C * b + a + m], XP[:, 64 + 4 * a + b:64 + 4 * a + 4 * m:4], 0.5)
+        elif n[0:2] == "lw":
+            a, m, b, hs = cols()
+            op("v", "cw1 cw2 " + "".join("b3%d " % h for h in hs), "".join("lw%d%d " % (h, b) for h in hs), V.tensor_tensor_scan,
+               T.lw[:, C * b + a:C * b + a + m], T.cw[:, C * (2 - b) + a:C * (2 - b) + a + m], T.b3[:, a:a + m], 0.0, OP.max, OP.add)
         elif n == "la":
-            ts("cw fl1", "la", T.la[:, :], T.cw[:, :].indirect(F(2)), 1.0, None, OP.add)
+            times(q, "lw00 lw01 lw10 lw11 fl1", K(n), T.la[:, W], T.lw[:, :].indirect(F(2)))
         elif n == "lb":
-            tten("la fl1 b1", "lb", T.lb[:, :], T.la[:, :].indirect(F(1)), T.b1[:, :], OP.add)
+            times(q, "laA laB fl1", K(n), T.lb[:, W], T.la[:, :].indirect(F(1)))
         elif n == "lm":
-            cp("lb fl1", K("lm"), T.lm[:, W], T.lb[:, :].indirect(T.fl[:, Q]))
+            cp("lbA lbB fl1", K(n), T.lm[:, W], T.lb[:, :].indirect(F(0)))
         elif n in ("ln", "hn"):
-            hold(K("lm") + "my", K("ln"), T.ln[:, W], T.my[:, W], T.lm[:, W])
+            hold(K(n[0] + "m") + "mx", K(n), T[n][:, W], T.mx[:, W], T[n[0] + "m"][:, W])
         elif n in ("vi", "vj"):
-            ts(K("ln"), K(n), T[n][:, Q], T.ln[:, L], 1 / UNIT, None, OP.mult)
+            k = "ln" if n == "vi" else "hn"
+            cp(K(k), K(n), T[n][:, Q], T[k][:, L])
         elif n in ("i3", "i6"):
-            i = 2 * (n == "i6")
-            cp(K("va%d" % i), K(n), T[n][:, Q], VA(i))
+            k = "ln" if n == "i3" else "hn"
+            ts(K(k) + "cg5", K(n), T[n][:, Q], T[k][:, L], 0.25, cg[:, 5:6], OP.mult, OP.add)
         elif n == "ha":
-            times(q, "cw fl0", K(n), T.ha[:, W], T.cw[:, :].indirect(F(5)))
-        elif n in ("ha2", "hc2"):
-            t, c = T[n[0:2]], (4 * UNIT if n == "ha2" else 2.0)
-            if q == "a":
-                act(K(n[0:2]), K(n), t[:, C + 16 * lo:C + 16 * hi], t[:, W], AF.Identity, bias=c)
-            else:
-                ts(K(n[0:2]), K(n), t[:, C + 16 * lo:C + 16 * hi], t[:, W], c, None, OP.add)
+            act("cw0 cw1 fl0", n, T.ha[:, 0:C], T.cw[:, 0:704].indirect(F(5)))
+        elif n == "ha2":
+            affine("a", "ha", n, T.ha[:, C:704], T.ha[:, 0:C], 1.0, 1.0)
         elif n == "hc":
-            times(q, "haA haB ha2A ha2B fl0", K(n), T.hc[:, W], T.ha[:, :].indirect(F(4)))
+            act("ha ha2 fl0", n, T.hc[:, :], T.ha[:, :].indirect(F(4)))
         elif n == "hd":
-            times(q, "hcA hcB hc2A hc2B fl0", K(n), T.hd[:, W], T.hc[:, :].indirect(F(3)))
+            act("hc fl0", n, T.hd[:, :], T.hc[:, :].indirect(F(3)))
         elif n == "hm":
-            act("hdA hdB " + K("i3"), K("lm"), T.lm[:, W], T.hd[:, :].indirect(T.i3[:, Q]))
+            act("hd " + K("i3"), K(n), T.hm[:, W], T.hd[:, :].indirect(T.i3[:, Q]))
         elif n[0:2] == "va":
-            k, sh, m = (("vi", 5, 511), ("vi", 3, 1), ("vj", 5, 511), ("vj", 2, 3), ("vi", 16, 1))[x[0]]
-            ts(K(k), K(n), VA(x[0]), T[k][:, Q], sh, m, OP.logical_shift_right, OP.bitwise_and)
+            k = "vi" if x[0] == 1 else "vj"
+            ts(K(k), K(n), VA(x[0]), T[k][:, Q], 3, None, OP.bitwise_and)
+        elif n == "ge1":
+            gather(10, "b1 fl1", T.b1[:, :].indirect(F(0)))
         elif n[0:2] == "pw":
             times(q, "cb pl%d" % r, n, plane(T.pw, x[0]), T.cb[:, :].indirect(T["pl%d" % r][:, 22 * x[0]:22 * x[0] + 22]), 4.0)
         elif n in ("t0", "t1", "t2", "t3"):
@@ -420,49 +512,59 @@ def rank_program(g, core, T, topo):
         elif n == "j2":
             tten("j1 fm1", "j2", T.jf[:, 66:88], T.jf[:, 44:66], T.fm[:, 1:44:2], OP.mult)
         elif n == "j3":
-            ts(K("va4"), "j3", T.jf[:, 88:110], VA(4), -352.0, 352.0, OP.mult, OP.add)
+            k, v, h = listed(10)
+            ts(k, "j3", T.jf[:, 88:110], v, -176.0, 176.0, OP.mult, OP.add)
         elif n == "j4":
             tten("jf j3", "j4", T.jf[:, 110:132], T.jf[:, 22:44], T.jf[:, 88:110], OP.add)
         elif n == "j5":
-            tten("j2 j4", K("ki"), T.ki[:, :], T.jf[:, 66:88], T.jf[:, 110:132], OP.add)
+            tten("j2 j4", K("ki0"), KI(0), T.jf[:, 66:88], T.jf[:, 110:132], OP.add)
         elif n == "j6":
-            cp(K("ki"), K("k0"), T.k0[:, :], T.ki[:, :])
+            cp(K("ki0"), K("k0"), T.k0[:, :], KI(0))
         elif n == "j7":
-            tten("pw0 pw1 m16 " + K("k0"), K("km"), T.km[:, :], T.pw[:, :].indirect(T.k0[:, :]), T.m16[:, :], OP.mult)
+            gather(0, "pw0 pw1 " + K("k0"), T.pw[:, :].indirect(T.k0[:, Q]))
         elif n == "p0":
-            tten(K("ln") + "fo1", K("ki"), T.ki[:, Q], T.ln[:, L], T.fo[:, 2 * lo + 1:2 * hi:2], OP.add)
-        elif n == "p2":
-            tten(K("kb") + K("ln"), K("ki"), T.ki[:, Q], T.kb[:, Q], T.ln[:, L], OP.add)
-        elif n == "p4":
-            k = "kh" if q else "ksn"
-            tten(K(k) + K("va3"), K("ki"), T.ki[:, Q], T[k][:, L], VA(3), OP.add)
-        elif n in ("k0", "k2", "k4"):
-            i = {"k0": 1, "k2": 8 if q else 5, "k4": 6}[n]
-            ts(K("ki") + "cg%d" % i, K(n), T[n][:, Q], T.ki[:, Q], cg[:, i:i + 1] if q or i < 6 else 704.0, None, OP.add)
-        elif n in ("g0", "g2", "g4") and q:
-            act(S2 + K("k%d" % x[0]), K("km"), T.km[:, W], T.s2[:, :].indirect(T["k%d" % x[0]][:, Q]))
+            k, v, h = listed(10)
+            tten(k + "fo1", K("ki0"), KI(0), v, T.fo[:, 2 * lo + 1:2 * hi:2], OP.add)
+        elif n in ("p2", "p4"):
+            k, v, h = listed(x[0] - 2)
+            tten(k + K("va%d" % (x[0] - 1)), K("ki%d" % x[0]), KI(x[0]), v, VA(x[0] - 1), OP.add)
+        elif n == "k0":
+            ts(K("ki0"), K(n), T.k0[:, Q], KI(0), 1.0, None, OP.add)
+        elif n in ("k2", "k4"):
+            ts(K("ki%d" % x[0]) + "cg6", K(n), T[n][:, Q], KI(x[0]), cg[:, 6:7] if listed(x[0] - 2)[2] else 704.0, None, OP.add)
         elif n in ("g0", "g2", "g4"):
-            tten(S2 + K("k%d" % x[0]) + "m16", K("km"), T.km[:, W], T.s2[:, :].indirect(T["k%d" % x[0]][:, Q]), T.m16[:, W], OP.mult)
-        elif n == "h" and q:
-            hold(K("km") + "mx", K("kh"), T.kh[:, W], T.mx[:, W], T.km[:, W])
-        elif n == "h":
-            scan(K("km") + "r16", K("ksn"), T.ksn[:, W], T.r16[:, W], T.km[:, W])
-        elif n == "kb":
-            k = "kh" if q else "ksn"
-            tten(K(k) + K("va1"), K("kb"), T.kb[:, Q], T[k][:, L], VA(1), OP.add)
+            gather(x[0], S2 + K("k%d" % x[0]), T.s2[:, :].indirect(T["k%d" % x[0]][:, Q]))
+        elif n in ("h0", "h2", "h4", "h6", "h8", "he"):
+            i = x[0] if x else 10
+            if i == 8 and r == 2:
+                return
+            if listed(i)[2]:
+                hold(K("km%d" % i) + "mx", K("ks%d" % i), at(T.kh, i, W), T.mx[:, W], at(T.km, i, W))
+            else:
+                scan(K("km%d" % i) + "r16", K("ks%d" % i), at(T.ks, i, W), T.r16[:, W], at(T.km, i, W))
         elif n == "k6":
-            k = "kh" if q else "ksn"
-            ts(K(k) + "cg7", K(n), T.k6[:, Q], T[k][:, L], 0.25, cg[:, 7:8] if q else 176.0, OP.mult, OP.add)
+            k, v, h = listed(4)
+            ts(k + "cg7", K(n), T.k6[:, Q], v, 0.25, cg[:, 7:8] if h else 176.0, OP.mult, OP.add)
         elif n[0:2] == "gi":
-            act("xh%d " % x[0] + K("i6"), K(n), T.gi[:, 64 * lo + x[0]:64 * hi:4], plane(T.xh, x[0]).indirect(T.i6[:, Q]))
+            a, m = PART[x[0]] if len(x) == 2 else (0, C)
+            b = x[-1]
+            out = T.gs[:, b - 1:4 * m:4] if n in ("gi11", "gi13") else T.gi[:, 4 * a + b:4 * a + 4 * m:4]
+            times(q or "a", "xh0%d xh1%d i6A i6B" % (b, b), n if len(x) == 2 else "gi0%d gi1%d" % (b, b), out,
+                  plane(T.xh, b).indirect(T.i6[:, a // 16:(a + m) // 16]))
+        elif n[0:2] == "zk":
+            a, m = PART[1]
+            act("xh0%d xh1%d k6B" % (x[0], x[0]), n, T.gs[:, x[0]:4 * m:4], plane(T.xh, x[0]).indirect(T.k6[:, a // 16:(a + m) // 16]))
+        elif n == "zs":
+            a, m = PART[1]
+            scan("alt gi11 gi13 zk1 zk3", "zs z10 z11 z12 z13", T.z[:, 4 * a:4 * a + 4 * m], T.alt[:, 0:4 * m], T.gs[:, 0:4 * m])
         elif n[0] == "z":
             a, m = PART[x[0]]
             b = x[1]
             v = slice(4 * a + b, 4 * a + 4 * m, 4)
-            tten("xh%d k6%s gi%d%s" % (b, "AB"[x[0]], b, "AB"[x[0]]), "z%d" % x[0], T.z[:, v], plane(T.xh, b).indirect(T.k6[:, a // 16:(a + m) // 16]), T.gi[:, v], OP.add)
+            tten("xh0%d xh1%d gi%d%d k6%s" % (b, b, x[0], b, ("A", "B zs")[x[0]]), n, T.z[:, v], plane(T.xh, b).indirect(T.k6[:, a // 16:(a + m) // 16]), T.gi[:, v], OP.add)
         elif n in ("q0", "q1"):
             a, m = PART[x[0]]
-            op("v", "z%d" % x[0], "zq%d" % x[0], V.quantize_mx, T.zq[:, a:a + m], T.zs[:, a:a + m], T.z[:, 4 * a:4 * a + 4 * m])
+            op("v", " ".join("z%d%d" % (x[0], b) for b in range(4)), "zq%d" % x[0], V.quantize_mx, T.zq[:, a:a + m], T.zs[:, a:a + m], T.z[:, 4 * a:4 * a + 4 * m])
             for b in range(4):
                 k, o = bank(x[0], b)
                 mm("wq wp zq%d" % x[0], k, o, T.wq[:, 128 * b:128 * b + 128], T.wp[:, 128 * b:128 * b + 128], T.zq[:, a:a + m], T.zs[:, a:a + m])
@@ -480,117 +582,93 @@ def rank_program(g, core, T, topo):
         elif n == "dn":
             scan("en m2", "dn", T.dn[:, :], T.m2[:, :], T.en[:, :])
         elif n == "dd":
-            tten("dn", "dd", T.dd[:, :], T.dn[:, L], T.dn[:, L], OP.mult)
+            tten("dn", "dd", T.dd[:, 0:22], T.dn[:, L], T.dn[:, L], OP.mult)
         elif n == "tf":
-            ts("dd cg3 cg4", "tf", T.tf[:, :], T.dd[:, :], cg[:, 3:4], cg[:, 4:5], OP.is_lt, OP.mult)
+            ts("dd cg3 cg4", "tf", T.tf[:, :], T.dd[:, 0:22], cg[:, 3:4], cg[:, 4:5], OP.is_lt, OP.mult)
         elif n == "tg":
             tten("tf cl", "tg", T.tg[:, :], T.tf[:, :], T.cl[:, 0:22], OP.add)
         elif n == "tl":
             cp("tg", "tl", T.tl[:, :], T.tg[:, :])
         elif n in ("u0", "u1"):
             times(q, "pw%d tl" % (1 - x[0]), "uw%d" % x[0], plane(T.uw, x[0]), plane(T.pw, 1 - x[0]).indirect(T.tl[:, :]))
-        elif n == "n0" and q:
-            act("uw0 sn%d" % r, K("km"), T.km[:, :], T.uw[:, 0:C].indirect(sn[:, 0:22]))
-        elif n == "n0":
-            tten("uw0 sn%d m16" % r, K("km"), T.km[:, :], T.uw[:, 0:C].indirect(sn[:, 0:22]), T.m16[:, :], OP.mult)
-        elif n == "n1" and r < 2:
-            act("uw1 sn%d" % r, "t1", T.t1[:, :], T.uw[:, C:704].indirect(sn[:, 22:44]))
-        elif n == "ns0":
-            k = "kh" if q else "ksn"
-            ts(K(k) + "cg7", "tx", ns[:, 0:22], T[k][:, L], 0.25, cg[:, 7:8] if q else 176.0, OP.mult, OP.add)
-        elif n == "nh" and r < 2:
-            hold("t1 mx", K("ln"), T.ln[:, :], T.mx[:, :], T.t1[:, :])
-        elif n == "ns1" and r < 2:
-            ts(K("ln") + "cg7", "sn%d" % (r + 1), ns[:, 22:44], T.ln[:, L], 0.25, cg[:, 7:8], OP.mult, OP.add)
-            send_list(r + 1)
+        elif n in ("n0", "n1"):
+            b = x[0]
+            if b == 0 or r < 2:
+                gather(6 + 2 * b, "uw%d tx sn%d" % (b, r), plane(T.uw, b).indirect(sn[:, 22 * b + lo:22 * b + hi]))
+        elif n in ("ns0", "ns1"):
+            b = x[0]
+            if b == 0 or r < 2:
+                k, v, h = listed(6 + 2 * b)
+                ts(k + "cg7", ("tx", "sn%d" % (r + 1))[b], ns[:, 22 * b:22 * b + 22], v, 0.25, cg[:, 7:8] if h else 176.0, OP.mult, OP.add)
+            if b == 1 and r < 2:
+                send_list(r + 1)
         elif n == "sf":
             cp("tx sn%d" % r, "sf", T.sf[:, :], sn[:, 0:44])
         elif n == "sd":
             tten("sf", "fb", T.fb[:, 44:88:2], T.sf[:, 22:44], T.sf[:, 0:22], OP.subtract)
+        elif n == "fb0":
+            times(q, "sf", "fb1", T.fb[:, 45:88:2], T.sf[:, 0:22])
+            times(q, "sf", "fb1", T.fb[:, 133:176:2], T.sf[:, 0:22])
+            affine(q, "fb", "fb1", T.fb[:, 132:176:2], T.fb[:, 44:88:2], 1.0, 352.0)
+        elif n == "fb1":
+            times(q, "fb fb1", "fb2", T.fb[:, 88:132], T.fb[:, 44:88])
+            times(q, "fb fb1", "fb2", T.fb[:, 176:220], T.fb[:, 44:88])
+        elif n == "fb2":
+            times(q, "fb1", "fb3", T.fb[:, 220:264], T.fb[:, 132:176])
+            times(q, "fb1", "fb3", T.fb[:, 264:308], T.fb[:, 132:176])
         elif n == "so":
             for b in range(2):
-                act("uw%d sn2" % b, "tw cw0", plane(T.tw, b), plane(T.uw, b).indirect(T.sn2[:, 22 * b:22 * b + 22]), AF.Identity, scale=0.25, bias=176.0)
+                act("uw%d sn2" % b, "tw iw", plane(T.tw, b), plane(T.uw, b).indirect(T.sn2[:, 22 * b:22 * b + 22]), AF.Identity, scale=0.25, bias=176.0)
             dma("s", "d_so", "tw", "so", T.so[:, :], T.tw[0:128:16, :])
-        elif n == "vq":
-            op("v", "vb", "vq", V.quantize_mx, T.vq[:, :], T.vs[:, :], T.vb[:, :])
         elif n[0] == "e":
             a, m = PART[x[0]]
             b = x[1]
             k, ps = bank(x[0], b)
-            mm("eq dq%d%d" % (r - 1, x[0]), k, ps, T.eq[:, 128 * b:128 * b + 128], T.es[:, 128 * b:128 * b + 128],
+            mm("eq%d dq%d%d" % (b, r - 1, x[0]), k, ps, T.eq[:, 128 * b:128 * b + 128], T.es[:, 128 * b:128 * b + 128],
                T["dq%d" % (r - 1)][:, a:a + m], T["ds%d" % (r - 1)][:, a:a + m])
         elif n[0] == "d":
             a, m = PART[x[0]]
             k, ps = bank(x[0], x[1])
             times(q, k, "dw%d%d" % (x[0], x[1]), T.dw[:, C * x[1] + a:C * x[1] + a + m], ps)
+        elif n == "xc":
+            a, m = XH[1]
+            cp(xp(r - 1, 1), n, T.gx[:, 1:4 * m:2], T["xp%d" % (r - 1)][:, 65 + 4 * a:64 + 4 * a + 4 * m:2])
+        elif n[0:2] == "xk":
+            a, m = XH[1]
+            act("tx dw0%d dw1%d" % (x[0], x[0]), n, T.gx[:, x[0] - 1:4 * m:4], plane(T.dw, x[0]).indirect(sn[:, a // 16:(a + m) // 16]))
+        elif n == "xs":
+            a, m = XH[1]
+            scan("alt xc xk1 xk3", xp(r, 1) + "xs", XP[:, 64 + 4 * a:64 + 4 * a + 4 * m], T.alt[:, 0:4 * m], T.gx[:, :])
         elif n[0] == "x":
-            a, m = XH[x[0]]
-            b = x[1]
+            a, m, b, hs = cols()
             v = slice(64 + 4 * a + b, 64 + 4 * a + 4 * m, 4)
-            tten("tx xp%d%d%d dw0%d dw1%d" % (r - 1, x[0], b, b, b), "xp%d%d%d" % (r, x[0], b), XP[:, v],
-                 plane(T.dw, b).indirect(sn[:, a // 16:(a + m) // 16]), T["xp%d" % (r - 1)][:, v], OP.add)
+            tten("tx dw0%d dw1%d " % (b, b) + "xs " * (r == 3 and 1 in hs) + "".join("xp%d%d%d " % (r - 1, h, b) for h in hs), "".join("xp%d%d%d " % (r, h, b) for h in hs),
+                 XP[:, v], plane(T.dw, b).indirect(sn[:, a // 16:(a + m) // 16]), T["xp%d" % (r - 1)][:, v], OP.add)
         elif n[0:2] == "qx":
-            qx(r, x[0])
-        elif n[0:2] == "fb":
-            repeat_lists(x[0], q)
-        elif n == "r6":
-            act("uq url", "urs1", T.urs[:, 128:256], T.us[:, :].indirect(T.url[:, 8:16]))
-        elif n == "mx":
-            act("m16", "mx", T.mx[:, :], T.m16[:, :], AF.Identity, scale=-BIG - KM, bias=KM)
-        elif n == "my":
-            ts("m16", "my", T.my[:, :], T.m16[:, :], -260.0, 4.0, OP.mult, OP.add)
-        elif n == "m2a":
-            ts("dn", "m2", T.m2[:, :], T.dn[:, :], 4.0, None, OP.min)
-        elif n == "kc":
-            act("cw0", "cb", T.cb[:, :], T.tw[:, 0:C], AF.Identity, bias=-176.0)
-        elif n == "m2b":
-            scan("m2 one", "dd", T.dd[:, 0:16], T.m2[:, 0:16], T.one[:, 0:16])
-        elif n == "m2c":
-            ts("dd", "cg3", cg[:, 3:4], T.dd[:, 15:16], T.dd[:, 15:16], 0.18, OP.mult, OP.mult)
-        elif n[0] == "w" and r == 1:
-            v = slice(128 * x[0], 128 * x[0] + 128)
-            op("v", "eb", "eq", V.quantize_mx, T.eq[:, v], T.es[:, v], T.eb[:, 512 * x[0]:512 * x[0] + 512])
-
-    def run(r, names):
-        for name in names.split():
-            step(r, name)
-
-    send_list(0)
-    op("v", "ub", "uq", V.quantize_mx, T.uq[:, :], T.us[:, :], T.ub[:, :])
-    tten("ge ga0", "ge", T.ge[:, :], T.ge[:, :], T.cq[:, 10:20], OP.add)
-    run(0, "sf")
-    for i in range(2):
-        cp("uq url", "ur%d" % i, T.urq[:, 128 * i:128 * i + 128].bitcast(dt.uint32), T.uq[:, :].bitcast(dt.uint32).indirect(T.url[:, 8 * i:8 * i + 8]))
-    act("uq url", "urs0", T.urs[:, 0:128], T.us[:, :].indirect(T.url[:, 0:8]))
-    run(0, "qx0 s0 qx1 s1 sd")
-    cp("ge", "gl", T.gl[:, :], T.ge[:, :])
-    run(0, "kc fb0.a fb1.a fb2.a")
-    dma("s", "d_w", xp(0, 0) + xp(0, 1) + "ub", "wq", T.wq[:, :].bitcast(dt.uint8), T.wc[:, :])
-    dma("s", "d_wp", "", "wp", T.wp[:, :], T.ws[:, :])
-    dma("s", "d_v", "", "vb", T.vb[:, :], T.v[:, :])
-    iota("r16o", T.r16[:, :], [[0, C]], 1, 0)
-    op("g", "r16o", "r16", g.iota, T.r16[:, 0:C:16], [[0, 22]], 0, 0, allow_small_or_imprecise_dtypes=True)
-    for r in (1, 2):
-        iota("pad%d" % r, T["xp%d" % r][:, 0:64], [[0, 64]], 0, 0)
-        iota("pad%d" % r, T["xp%d" % r][:, 1472:1536], [[0, 64]], 0, 0)
-    iota("one", T.one[:, :], [[0, 512]], 1, 0)
-    for b in range(4):
-        op("g", "one", "eb", g.affine_select, T.eb[:, 512 * b:512 * b + 512], T.one[:, :], [[-1, 512]], OP.is_equal, 0.0, b, 4)
-
-    for r in range(3):
-        run(r, (BITS + PATH + PATH1 + SECOND + "z01 " if r else BITS0 + PATH + PATH0 + SECOND0) + LAYER + TURNS)
-        run(r + 1, NEXT if r < 2 else LAST)
-    for h in range(2):
-        run(3, END[h])
-        a, n = XH[h]
-        q = slice(16 + a, 16 + a + n)
-        mm("vq xq%d" % h, "pa%d" % h, T.pa[:, 512 * h:512 * h + n], T.vq[:, :], T.vs[:, :], T.xq[:, q], T.xs[:, q])
-        dma("s", "d_oc", "xq%d" % h, "oc%d" % h, T.oc[:, 4 * a:4 * a + 4 * n], T.xq[:, q].bitcast(dt.uint8))
-        if h:
+            h = x[0]
+            a, m = 16 + XH[h][0], XH[h][1]
+            if r < 3:
+                a, m = a - 16 * (1 - h), m + 16
+            op("v", xp(r, h) + "pad%d" % r, "xq%d" % h, V.quantize_mx, T.xq[:, a:a + m], T.xs[:, a:a + m], XP[:, 4 * a:4 * a + 4 * m])
+        elif n in ("y0", "y1"):
+            a, m = XH[x[0]]
+            v = slice(16 + a, 16 + a + m)
+            mm("vq xq%d" % x[0], "pa%d" % x[0], T.pa[:, 512 * x[0]:512 * x[0] + m], T.vq[:, :], T.vs[:, :], T.xq[:, v], T.xs[:, v])
+        elif n in ("oc0", "oc1"):
+            a, m = XH[x[0]]
+            dma("s", "d_oc", "xq%d" % x[0], n, T.oc[:, 4 * a:4 * a + 4 * m], T.xq[:, 16 + a:16 + a + m].bitcast(dt.uint8))
+        elif n == "osc":
             for k in range(4):
                 dma("sa"[k % 2], "d_oc", "xq0 xq1", "osc%d" % k, T.osc[4 * k:4 * k + 4, :], T.xs[32 * k:32 * k + 4, 16:368])
-        times("av"[h], "pa%d" % h, "yb%d" % h, T.yb[:, a:a + n], T.pa[:, 512 * h:512 * h + n])
-        dma("sa"[h], "d_y", "yb%d" % h, "y%d" % h, T.y[:, a:a + n], T.yb[:, a:a + n])
+        elif n in ("yc0", "yc1"):
+            h = x[0]
+            a, m = XH[h]
+            times(q, "pa%d" % h, "yb%d" % h, T.yb[:, a:a + m], T.pa[:, 512 * h:512 * h + m])
+            dma("sa"[h], "d_y", "yb%d" % h, "y%d" % h, T.y[:, a:a + m], T.yb[:, a:a + m])
+
+    for r, names in ORDER:
+        for name in names.split():
+            step(r, name)
     total["ls"] = sent[0]
     for s in total:
         g.wait_ge(T.sem[s], total[s])

from concourse.bass import DstId, RemoteDMATransfer
from concourse.mybir import dt, AluOpType as OP, ActivationFunctionType as AF

C = 352
MASK = [2, 4, 1]
PART = [(0, 192), (192, 160)]
XH = [(0, 224), (224, 128)]
HALF = PART[1][0] // 16
KM, BIG = 32768.0, 2097152.0
ROWS = [1, 6, 3]
BANKS = {"1": 6, "6": 7, "30": 0, "31": 1}
BF, F32, I32, U16, U8, E4 = "bfloat16", "float32", "int32", "uint16", "uint8", "float8_e4m3fn_x4"
SCRATCH = {
    "sei": ("sbuf", [128, 44], I32), "ub": ("sbuf", [128, 512], BF), "vb": ("sbuf", [128, 512], BF),
    "wq": ("sbuf", [128, 512], E4), "wp": ("sbuf", [128, 512], U8),
    "uq": ("sbuf", [128, 128], E4), "us": ("sbuf", [128, 128], U8), "vq": ("sbuf", [128, 128], E4), "vs": ("sbuf", [128, 128], U8),
    "urq": ("sbuf", [128, 384], E4), "urs": ("sbuf", [128, 384], U8),
    "pc": ("sbuf", [128, 8], I32), "ci": ("sbuf", [128, 8], I32), "cf": ("sbuf", [128, 8], F32), "cg": ("sbuf", [128, 12], F32),
    "cn": ("sbuf", [128, 4], F32), "sq": ("sbuf", [128, C], BF),
    "j16": ("sbuf", [128, C], F32), "cw": ("sbuf", [128, 3 * C], F32), "cb": ("sbuf", [128, C], BF),
    "m16": ("sbuf", [128, C], BF), "r16": ("sbuf", [128, C], BF), "mx": ("sbuf", [128, C], BF), "m2": ("sbuf", [128, C], BF),
    "cq": ("sbuf", [128, 24], F32), "cl": ("sbuf", [128, 24], F32), "ga": ("sbuf", [128, 10], I32), "gb": ("sbuf", [128, 40], F32),
    "gl": ("sbuf", [128, 10], U16), "url": ("sbuf", [128, 24], U16),
    "one": ("sbuf", [128, 512], BF), "eb": ("sbuf", [128, 2048], BF), "eq": ("sbuf", [128, 512], E4), "es": ("sbuf", [128, 512], U8),
    "xq": ("sbuf", [128, 384], E4), "xs": ("sbuf", [128, 384], U8), "xh": ("sbuf", [128, 1408], BF),
    "b1": ("sbuf", [128, C], BF), "b6": ("sbuf", [128, C], BF), "b3": ("sbuf", [128, C], BF),
    "tt": ("sbuf", [128, 736], F32), "fm": ("sbuf", [128, 320], F32), "fb": ("sbuf", [128, 308], F32),
    "fo": ("sbuf", [128, 308], F32), "fl": ("sbuf", [128, 132], U16), "sf": ("sbuf", [128, 44], F32),
    "la": ("sbuf", [128, C], F32), "lb": ("sbuf", [128, C], F32), "lm": ("sbuf", [128, C], F32), "ln": ("sbuf", [128, C], F32),
    "lw": ("sbuf", [128, 704], F32), "ha": ("sbuf", [128, 704], F32), "hc": ("sbuf", [128, C], F32), "hd": ("sbuf", [128, C], F32),
    "hm": ("sbuf", [128, C], F32), "hn": ("sbuf", [128, C], F32),
    "i3": ("sbuf", [128, 22], U16), "i6": ("sbuf", [128, 22], U16), "vi": ("sbuf", [128, 22], I32), "vj": ("sbuf", [128, 22], I32),
    "va": ("sbuf", [128, 44], I32), "jf": ("sbuf", [128, 132], F32),
    "pw": ("sbuf", [128, 704], BF), "s2": ("sbuf", [128, 1408], BF), "km": ("sbuf", [128, 6 * C], BF), "ks": ("sbuf", [128, 6 * C], BF),
    "kh": ("sbuf", [128, 5 * C], F32), "ki": ("sbuf", [128, 66], F32),
    "k0": ("sbuf", [128, 22], U16), "k2": ("sbuf", [128, 22], U16), "k4": ("sbuf", [128, 22], U16), "k6": ("sbuf", [128, 22], U16),
    "en": ("sbuf", [128, C], BF), "dd": ("sbuf", [128, 40], F32), "dn": ("sbuf", [128, C], BF), "tf": ("sbuf", [128, 22], F32),
    "tg": ("sbuf", [128, 22], F32), "tl": ("sbuf", [128, 22], U16), "uw": ("sbuf", [128, 704], BF),
    "tw": ("sbuf", [128, 704], F32),
    "gi": ("sbuf", [128, 1408], BF), "z": ("sbuf", [128, 1408], BF), "zq": ("sbuf", [128, C], E4), "zs": ("sbuf", [128, C], U8),
    "gs": ("sbuf", [128, 640], BF), "gx": ("sbuf", [128, 512], BF), "alt": ("sbuf", [128, 640], BF),
    "hb": ("sbuf", [128, 1408], BF), "dw": ("sbuf", [128, 1408], BF), "yb": ("sbuf", [128, C], F32),
    "pa": ("psum", [128, 2048], F32), "pb": ("psum", [128, 2048], F32),
}
for _r in range(4):
    SCRATCH["xp%d" % _r] = ("sbuf", [128, 1536], BF)
    SCRATCH["sn%d" % _r] = ("sbuf", [128, 48], U16)
for _r in range(3):
    SCRATCH["lh%d" % _r] = ("sbuf", [128, 44], U16)
    SCRATCH["pl%d" % _r] = ("sbuf", [128, 44], U16)
    SCRATCH["hq%d" % _r] = ("sbuf", [128, C], E4)
    SCRATCH["hs%d" % _r] = ("sbuf", [128, C], U8)
    SCRATCH["fq%d" % _r] = ("sbuf", [128, 128], E4)
    SCRATCH["fs%d" % _r] = ("sbuf", [128, 224], U8)
    SCRATCH["dq%d" % _r] = ("sbuf", [128, C], E4)
    SCRATCH["ds%d" % _r] = ("sbuf", [128, C], U8)
SEMAPHORES = ["sv", "sa", "sp", "sg", "ls"] + ["d_" + n for n in ("se", "x", "x2", "u", "w", "wp", "v", "y", "oc", "so")]
for _r in range(3):
    SEMAPHORES += [n + str(_r) for n in ("hl", "hc", "hp", "la", "ca", "cb")]
CODES = [(0, 1), (2, 3)]
SCALES = [3, 0]
LISTS = [(0, 1, 2, 3), (2,), (2,)]

START = ("Lse Lu Lx0 Lx1 Ipc Icq Ij fmz pad0 pad1 ci2 ci1 ci3 ci0 cf url1 url0 url2 cl Ifb Icw cg0 sn cn ga uq ge cg6 cg4 fbd cg7 sq r3 r1 gz gb "
         "sf ur2 sd ge2 qx0 ge3 s0 m30 ur0 gl qx1 s1 Lw Ir Ione Ie Ipad Ialt m31 cw2 fb0.a cw1 fb1.a m1 b30 m16 r6 b31 cw0 b1 kc mx ")
BITS0 = "tr0 ts0 tr1 ts1 fb2.v lw00 fm1 fm0 lw10 fo1 fo0 lw1 fl1 fl0 ur1 "
PATH0 = ("laB.a ha laA.v ge1 lbB.a lbA.v j0 he ha2 cg5 lmA j1 j3 lmB j2 j4 lnA lnB hc pw0.a hd j5 pw1.v j6 vi i3 t1.v j7 "
         "va1 xh0.v h0A h0B t3.a hm t2.a t0.a hnA m6 ")
SECOND0 = ("p2A hnB p2B k2A xh12.v i6 k2B xh13.v vj g2A xh1.a g2B.a va3 m2a h2A h2B p4A xh02.v p4B k4A xh03.v k4B g4A gi02.v h4A gi01 gi0 "
           "g4B.a h4B k6A m2b k6B gi03 gi13 gi11 zk3 zk1 b6 gi12 ")
LAYER0 = "z00 z02 z03 z01 zs q0 z10 z12 en c00.a c01.a dn q1 c03.a m2c c02.v dd tf h0q tg c10.a c11.a c12.a c13.v tl u1.a h1q "
TURNS0 = "u0.v n0 w1 n1.a h8B h6 h8A ns0 w0 ns1 w2 w3 "
NEXT = ("sf e01 e00 sd fb0.a fb2.a d01.a d00.v e10 e11 e02 e12 e03 e13 d02.a d10.v d11.v d12.a d03.a d13.a pw0.a pw1.a t3.a t1.a "
        "x0 x01 x2 x03 x11 qx0 s0 m30 x13 fb1.v qx1 b30 s1 m31 m6 m1 xh02.v ")
BITS = "tr0 ts0 tr1 ts1 lw00 fm1 t0.a b31 t2.a b1 fm0 lw01 fo1 lw11 fo0 lw10 fl1 xh03.v fl0 "
PATH = "laB.a ha laA.v ge1 lbB.a lbA.v he lmA p0 lmB k0 lnA ha2 lnB g0A vi i3 g0B h0A va1 xh01.v h0B "
SECOND = ("p2A xh11.v p2B hc xh12.a hd hmA hmB k2A hnA g2A.a xh13.a k2B hnB g2B vj i6 h2A va3A va3B h2B p4A xh0.v p4B k4A k4B g4A b6 g4B "
          "h4A h4B k6A k6B gi13 gi02 gi03 gi00 gi11 gi01 zk1 zk3 gi10 gi12 ")
LAYER = "z02 z03 z01 z00 zs q0 z10 z12 en c00.a c01.a dn q1 c03.a c02.v dd tf h0q tg c10.a c11.a c12.a c13.v tl h1q u1.a "
TURNS = "u0.v n0 n1.a h8B h8A h6 ns0 ns1 "
LAST = ("e01 e00 e03 xc d01.v vq d03.v e11 e10 e12 e02 e13 d11.v d00.a d10.v d12.a d02.a d13.a xk1 xk3 so x01 x00 x02 x03 xs qx0 y0 oc0 "
        "x10 x12 yc0.a qx1 y1 oc1 osc yc1.v")
ROUND = NEXT + BITS + PATH + SECOND + LAYER + TURNS
ORDER = [(0, START + BITS0 + PATH0 + SECOND0 + LAYER0 + TURNS0), (1, ROUND), (2, ROUND), (3, LAST)]


def route(topo, core, dst):
    ok = [h for h in topo.cores_of(core) if h != core and topo.may_write(h, dst)]
    near = [h for h in ok if topo.die(h) == topo.die(core)]
    far = [h for h in ok if topo.die(h) != topo.die(core)]
    return [near[0], far[0], near[1], far[1]]


def chunk(h, i):
    a, n = PART[h]
    return a + n // 2 * i, n // 2


def bits(e):
    return sum(1 << i for i in e)


def hand_on(g, core, T, topo):
    mine = [c for c in T.cores if c in topo.cores_of(core)]
    sent = 0
    for r in range(3):
        for c in mine:
            dst = T.cores[T.rank_of(c) ^ MASK[r]]
            hs = route(topo, c, dst)
            if core not in hs:
                continue
            i = hs.index(core)
            rid, pid = topo.addr(dst, core)
            e = topo.engines(core, dst)
            n_in = len(topo.engines(c, core))
            if i in LISTS[r]:
                w = 44 // len(LISTS[r])
                v = slice(w * LISTS[r].index(i), w * LISTS[r].index(i) + w)
                g.wait_ge(T.sem["hl%d" % r], n_in // len(LISTS[r]))
                g.remote_dma(T["pl%d" % r][:, v], T["lh%d" % r][:, v], T.sem["la%d" % r], T.sem.ls, pid, rid, bits(e))
                sent += len(e)
            for h in range(2):
                arr = T.sem[("ca%d", "cb%d")[h] % r]
                if i in CODES[h]:
                    a, n = chunk(h, CODES[h].index(i))
                    g.wait_ge(T.sem["hc%d" % r], n_in // 2)
                    g.remote_dma(T["dq%d" % r][:, a:a + n].bitcast(dt.uint8), T["fq%d" % r][:, 0:n].bitcast(dt.uint8), arr, T.sem.ls, pid, rid, bits(e))
                    sent += len(e)
                if i == SCALES[h]:
                    a, n = PART[h]
                    g.wait_ge(T.sem["hp%d" % r], n_in)
                    g.remote_dma(T["ds%d" % r][:, a:a + n], T["fs%d" % r][:, 0:n], arr, T.sem.ls, pid, rid, bits(e))
                    sent += len(e)
    if sent:
        g.wait_ge(T.sem.ls, sent)


def rank_program(g, core, T, topo):
    rank = T.rank_of(core)
    if rank is None:
        hand_on(g, core, T, topo)
        return
    eng = {"v": g.vector, "a": g.scalar, "p": g.tensor, "g": g, "s": g.sync}
    sem_of = {"v": "sv", "a": "sa", "p": "sp", "g": "sg"}
    total, seen = {}, {}
    last, readers = {}, {}

    def need(q, r, w):
        d = {}
        for k in r:
            t = last.get(k)
            if t is not None:
                d[t[0]] = max(d.get(t[0], 0), t[1])
        for k in w:
            for t in readers.get(k, []) + ([last[k]] if k in last else []):
                if t[2] != q or t[0][0:2] == "d_":
                    d[t[0]] = max(d.get(t[0], 0), t[1])
        for s in d:
            if seen.get((q, s), 0) < d[s]:
                eng[q].wait_ge(T.sem[s], d[s])
                seen[(q, s)] = d[s]

    def mark(t, r, w):
        for k in r:
            readers[k] = [x for x in readers.get(k, []) if x[0] != t[0]] + [t]
        for k in w:
            last[k] = t
            readers[k] = []

    def op(q, r, w, f, *args, **kw):
        r, w = r.split(), w.split()
        need(q, r, w)
        s = sem_of[q]
        f(*args, **kw).then_inc(T.sem[s], 1)
        total[s] = total.get(s, 0) + 1
        mark((s, total[s], q), r, w)

    def dma(q, sem, r, w, out, in_):
        r, w = r.split(), w.split()
        need(q, r, w)
        eng[q].dma_start(out, in_).then_inc(T.sem[sem], 16)
        total[sem] = total.get(sem, 0) + 16
        mark((sem, total[sem], q), r, w)

    V, A, P = g.vector, g.scalar, g.tensor

    def ts(r, w, out, in0, s1, s2, o0, o1=None):
        if o1 is None:
            op("v", r, w, V.tensor_scalar, out, in0, s1, s2, o0)
        else:
            op("v", r, w, V.tensor_scalar, out, in0, s1, s2, o0, o1)

    def tten(r, w, out, a, b, o):
        op("v", r, w, V.tensor_tensor, out, a, b, o)

    def cp(r, w, out, in_):
        op("v", r, w, V.tensor_copy, out, in_)

    def scan(r, w, out, d0, d1):
        op("v", r, w, V.tensor_tensor_scan, out, d0, d1, 0.0, OP.mult, OP.add)

    def hold(r, w, out, d0, d1):
        op("v", r, w, V.tensor_tensor_scan, out, d0, d1, 0.0, OP.add, OP.max)

    def act(r, w, out, in_, func=AF.Copy, **kw):
        op("a", r, w, A.activation, out, in_, func, **kw)

    def times(q, r, w, out, in_, c=None):
        if q == "a":
            act(r, w, out, in_, **({} if c is None else {"scale": c}))
        elif c is None:
            cp(r, w, out, in_)
        else:
            ts(r, w, out, in_, c, None, OP.mult)

    def affine(q, r, w, out, in_, a, b):
        if q == "a":
            act(r, w, out, in_, AF.Identity, scale=a, bias=b)
        else:
            ts(r, w, out, in_, a, b, OP.mult, OP.add)

    def mm(r, w, out, wq, wsc, xq, xsc):
        op("p", r, w, P.matmul_mx, out, wq, wsc, xq, xsc, True, True)

    def arrived(key, sem, n):
        total[sem] = n
        last[key] = (sem, n, "r")
        readers[key] = []

    def iota(k, out, pattern, base, cm):
        op("g", "", k, g.iota, out, pattern, base, cm, allow_small_or_imprecise_dtypes=True)

    def xp(r, h):
        return "".join("xp%d%d%d " % (r, h, b) for b in range(4))

    ci, cf, cg = T.ci, T.cf, T.cg
    PR, PH, PP, PE = (cf[:, i:i + 1] for i in range(4))
    columns = {4: (PP, -2.0, 1.0), 5: (PR, KM / 4, -0.375 - 15 * KM / 4), 6: (PR, KM, 704 - 15 * KM), 7: (PR, KM / 4, 176 - 15 * KM / 4)}
    sent = [0]
    held = {}

    def partner(r):
        return T.cores[rank ^ MASK[r]]

    def send_list(r):
        hs, tr, w = route(topo, core, partner(r)), [], 44 // len(LISTS[r])
        for i, k in enumerate(LISTS[r]):
            rid, pid = topo.addr(hs[k], core)
            e = topo.engines(core, hs[k])
            n = len(e) // len(LISTS[r])
            tr.append(RemoteDMATransfer(dst_ids=[DstId(rid=rid, pnc=pid)], dma_engine_mask=bits(e[n * i:n * i + n]), remote_sem=T.sem["hl%d" % r],
                                        src=T["sn%d" % r][:, w * i:w * i + w], dst=T["lh%d" % r][:, w * i:w * i + w]))
            sent[0] += n
        need("g", ["tx", "sn%d" % r], [])
        g.remote_dma_fused(tr, local_sem=T.sem.ls)
        hp = route(topo, partner(r), core)
        arrived("pl%d" % r, "la%d" % r, sum(len(topo.engines(hp[k], core)) for k in LISTS[r]))

    def send_part(r, h):
        hs = route(topo, core, partner(r))
        tr = []
        for i, k in enumerate(CODES[h]):
            rid, pid = topo.addr(hs[k], core)
            e = topo.engines(core, hs[k])
            n = len(e) // 2
            a, m = chunk(h, i)
            tr.append(RemoteDMATransfer(dst_ids=[DstId(rid=rid, pnc=pid)], dma_engine_mask=bits(e[(i + h) % 2::2]), remote_sem=T.sem["hc%d" % r],
                                        src=T["hq%d" % r][:, a:a + m].bitcast(dt.uint8), dst=T["fq%d" % r][:, 0:m].bitcast(dt.uint8)))
            sent[0] += n
        need("g", ["hq%d%d" % (r, h)], [])
        g.remote_dma_fused(tr, local_sem=T.sem.ls)
        rid, pid = topo.addr(hs[SCALES[h]], core)
        e = topo.engines(core, hs[SCALES[h]])
        a, m = PART[h]
        g.remote_dma(T["fs%d" % r][:, 0:m], T["hs%d" % r][:, a:a + m], T.sem["hp%d" % r], T.sem.ls, pid, rid, bits(e))
        sent[0] += len(e)
        hp = route(topo, partner(r), core)
        arrived("dq%d%d" % (r, h), ("ca%d", "cb%d")[h] % r, sum(len(topo.engines(hp[k], core)) for k in CODES[h] + (SCALES[h],)))

    def bank(h, b):
        n = PART[h][1]
        return ("pb%d" if h else "pa%d") % b, (T.pb if h else T.pa)[:, 512 * b:512 * b + n]

    def plane(t, b):
        return t[:, C * b:C * b + C]

    S2 = "s20 s21 s22 s23 "

    def start(n, q, x):
        if n == "Lse":
            dma("s", "d_se", "", "sei", T.sei[:, :], T.se[:, :])
        elif n == "Lu":
            dma("a", "d_u", "", "ub", T.ub[:, :], T.u[:, :])
        elif n[0:2] == "Lx":
            a, m = XH[x[0]]
            dma("s", ("d_x", "d_x2")[x[0]], "", xp(0, x[0]), T.xp0[:, 64 + 4 * a:64 + 4 * a + 4 * m], T.x[:, 4 * a:4 * a + 4 * m])
        elif n == "Lw":
            dma("s", "d_w", xp(0, 0) + xp(0, 1) + "ub", "wq", T.wq[:, :].bitcast(dt.uint8), T.wc[:, :])
            dma("s", "d_wp", "", "wp", T.wp[:, :], T.ws[:, :])
            dma("s", "d_v", "", "vb", T.vb[:, :], T.v[:, :])
        elif n == "Ipc":
            op("g", "", "pc", g.iota, T.pc[:, 0:1], [[0, 1]], 0, 1)
        elif n == "Icq":
            iota("cq", T.cq[:, :], [[16, 24]], 0, 0)
        elif n == "Ij":
            iota("j16", T.j16[:, :], [[0, 22], [1, 16]], 0, 0)
        elif n == "Ifb":
            iota("fbc", T.fb[:, 0:44:2], [[0, 22]], 1, 0)
        elif n == "Ipad":
            for r in (1, 2):
                iota("pad%d" % r, T["xp%d" % r][:, 0:64], [[0, 64]], 0, 0)
                iota("pad%d" % r, T["xp%d" % r][:, 1472:1536], [[0, 64]], 0, 0)
        elif n == "Icw":
            iota("iw", T.tw[:, 0:C], [[1, C]], 0, 0)
        elif n == "Ir":
            iota("r16o", T.r16[:, :], [[0, C]], 1, 0)
            op("g", "r16o", "r16", g.iota, T.r16[:, 0:C:16], [[0, 22]], 0, 0, allow_small_or_imprecise_dtypes=True)
        elif n == "Ione":
            iota("one", T.one[:, :], [[0, 512]], 1, 0)
        elif n == "Ialt":
            iota("alt", T.alt[:, :], [[0, 320], [1, 2]], 0, 0)
        elif n == "Ie":
            for b in range(4):
                op("g", "one", "eb%d" % b, g.affine_select, T.eb[:, 512 * b:512 * b + 512], T.one[:, :], [[-1, 512]], OP.is_equal, 0.0, b, 4)
        elif n[0:3] == "pad":
            op("v", "", "pad0", V.memset, T.xp0[:, 1472 * x[0]:1472 * x[0] + 64], 0.0)
        elif n == "ci1":
            ts("pc", n, ci[:, 1:2], T.pc[:, 0:1], 4, 1, OP.logical_shift_right, OP.bitwise_and)
        elif n[0:2] == "ci":
            ts("pc", n, ci[:, x[0]:x[0] + 1], T.pc[:, 0:1], (15, 0, 1, 14)[x[0]], None, OP.bitwise_and)
        elif n[0:3] == "url":
            ts("cq", n, T.url[:, 8 * x[0]:8 * x[0] + 8], T.cq[:, 0:8], float(ROWS[x[0]]), None, OP.add)
        elif n == "cf":
            cp("ci0 ci1 ci2 ci3", "cf", cf[:, 0:4], ci[:, 0:4])
        elif n == "fmz":
            op("v", "", "fm", V.memset, T.fm[:, 0:320:2], 0.0)
        elif n == "cl":
            ts("cq cf", "cl", T.cl[:, :], T.cq[:, :], PR, None, OP.add)
        elif n == "cg0":
            ts("cf", "cg0", cg[:, 0:1], PH, PP, 368.0, OP.not_equal, OP.mult)
        elif n[0:2] == "cg":
            affine("a", "cf", n, cg[:, x[0]:x[0] + 1], *columns[x[0]])
        elif n == "cn":
            ts("cf", "cn", T.cn[:, :], cf[:, 0:4], -1.0, None, OP.mult)
        elif n == "sq":
            act("j16 cn", "sq", T.sq[:, :], T.j16[:, :], AF.Square, bias=T.cn[:, 3:4])
        elif n == "fbd":
            times("a", "cl", "fbd", T.fb[:, 1:44:2], T.cl[:, 0:22], 4.0)
        elif n[0:2] == "cw":
            affine("a", "iw", n, plane(T.cw, x[0]), T.tw[:, 0:C], 4.0, (0.0, 2.0, 1.0)[x[0]])
        elif n == "ga":
            ts("cl", "ga", T.ga[:, :], T.cl[:, 0:10], 1.0 / 22, -0.477, OP.mult, OP.add)
        elif n == "ge":
            ts("cl cg0", "ge", T.gb[:, 10:20], T.cl[:, 0:10], 16.0, cg[:, 0:1], OP.mult, OP.add)
        elif n == "gb":
            ts("ga", "gb", T.gb[:, 0:10], T.ga[:, :], -351.0, -1.0, OP.mult, OP.add)
        elif n == "gz":
            ts("ga", "gz", T.gb[:, 20:30], T.ga[:, :], 0.0, None, OP.is_equal)
        elif n == "ge2":
            tten("gb ge", "ge2", T.gb[:, 30:40], T.gb[:, 10:20], T.gb[:, 0:10], OP.add)
        elif n == "ge3":
            tten("ge2 gz", "ge", T.gb[:, 10:20], T.gb[:, 30:40], T.gb[:, 20:30], OP.add)
        elif n == "gl":
            cp("ge", "gl", T.gl[:, :], T.gb[:, 10:20])
        elif n == "m16":
            ts("j16 cf", "m16", T.m16[:, :], T.j16[:, :], PR, None, OP.is_equal)
        elif n == "mx":
            affine("a", "m16", "mx", T.mx[:, :], T.m16[:, :], -BIG - KM, KM)
        elif n == "m2a":
            ts("sq", "m2", T.m2[:, :], T.sq[:, :], 4.0, None, OP.min)
        elif n == "m2b":
            scan("m2 one", n, T.dd[:, 24:40], T.m2[:, 0:16], T.one[:, 0:16])
        elif n == "m2c":
            ts("m2b", "cg3", cg[:, 3:4], T.dd[:, 39:40], T.dd[:, 39:40], 0.18, OP.mult, OP.mult)
        elif n == "kc":
            affine("a", "iw", "cb", T.cb[:, :], T.tw[:, 0:C], 1.0, -176.0)
        elif n == "sn":
            cp("sei", "sn0 tx", T.sn0[:, 0:44], T.sei[:, :])
            send_list(0)
        elif n in ("uq", "vq"):
            op("v", n[0] + "b", n, V.quantize_mx, T[n][:, :], T[n[0] + "s"][:, :], T[n[0] + "b"][:, :])
        elif n in ("ur0", "ur1", "ur2"):
            i = x[0]
            cp("uq url%d" % i, n, T.urq[:, 128 * i:128 * i + 128].bitcast(dt.uint32), T.uq[:, :].bitcast(dt.uint32).indirect(T.url[:, 8 * i:8 * i + 8]))
        elif n in ("r1", "r6", "r3"):
            i = ROWS.index(x[0])
            act("uq url%d" % i, "urs%d" % i, T.urs[:, 128 * i:128 * i + 128], T.us[:, :].indirect(T.url[:, 8 * i:8 * i + 8]))
        elif n[0] == "w":
            v = slice(128 * x[0], 128 * x[0] + 128)
            op("v", "eb%d" % x[0], "eq%d" % x[0], V.quantize_mx, T.eq[:, v], T.es[:, v], T.eb[:, 512 * x[0]:512 * x[0] + 512])
        else:
            return False
        return True

    def step(r, name):
        n, q = (name.split(".") + [None])[0:2]
        parts = n[-1] if n[-1] in "AB" else "AB"
        n = n.rstrip("AB")
        x = [int(ch) for ch in n if ch.isdigit()]
        if start(n, q, x):
            return
        sn, ns, XP = T["sn%d" % r], T["sn%d" % min(r + 1, 3)], T["xp%d" % r]
        lo, hi = (0 if "A" in parts else HALF), (C // 16 if "B" in parts else HALF)
        Q, W, L = slice(lo, hi), slice(16 * lo, 16 * hi), slice(16 * lo + 15, 16 * hi, 16)

        def K(k):
            return "".join(k + p + " " for p in parts)

        def F(l):
            return T.fl[:, 22 * l + lo:22 * l + hi]

        def VA(i):
            return T.va[:, 11 * (i - 1) + lo:11 * (i - 1) + hi]

        def KI(i):
            return T.ki[:, 11 * i + lo:11 * i + hi]

        def at(t, i, v):
            return t[:, 176 * i + v.start:176 * i + v.stop:v.step or 1]

        def gather(i, k, win):
            for p in parts:
                held[(r, i, p)] = q == "a"
            if q == "a":
                act(k, K("km%d" % i), at(T.km, i, W), win)
            else:
                tten(k + " m16", K("km%d" % i), at(T.km, i, W), win, T.m16[:, W], OP.mult)

        def listed(i):
            (h,) = {held[(r, i, p)] for p in parts}
            return K("ks%d" % i), at(T.kh if h else T.ks, i, L), h

        def cols():
            return (XH[x[0]] if len(x) == 2 else (0, C)) + (x[-1], x[0:1] if len(x) == 2 else [0, 1])

        if n in ("s0", "s1"):
            h = x[0]
            a, m = XH[h][0], XH[h][1] + 16 + 16 * h
            mm("uq xq0" + " xq1" * h, "pb%d" % h, T.pb[:, 512 * h:512 * h + m], T.uq[:, :], T.us[:, :], T.xq[:, a:a + m], T.xs[:, a:a + m])
        elif n[0] in "mb" and n[1:] in BANKS:
            i, j = ROWS.index(x[0]), BANKS[n[1:]]
            a, m = XH[x[1]] if len(x) == 2 else (0, C)
            k, o = "p%s%d" % ("ab"[j // 4], j % 4), (T.pa, T.pb)[j // 4][:, 512 * (j % 4):512 * (j % 4) + m]
            if n[0] == "m":
                mm("ur%d urs%d " % (i, i) + ("xq%d" % x[1] if len(x) == 2 else "xq0 xq1"), k, o, T.urq[:, 128 * i:128 * i + 128],
                   T.urs[:, 128 * i:128 * i + 128], T.xq[:, 16 + a:16 + a + m], T.xs[:, 16 + a:16 + a + m])
            else:
                act(k, n, T[n[0:2]][:, a:a + m], o, AF.Sign, bias=-2.0 ** -93)
        elif n in ("tr0", "tr1"):
            h = x[0]
            a, m = XH[h]
            op("v", "pb%d" % h, n, V.transpose, T.tt[:, a:a + m], T.pb[:, 512 * h + 16:512 * h + 16 + m])
        elif n in ("ts0", "ts1"):
            h = x[0]
            a, m = XH[h][0], XH[h][1] + 32 * h
            op("v", "pb%d" % h, n, V.transpose, T.tt[:, C + a:C + a + m], T.pb[:, 512 * h:512 * h + m])
        elif n in ("fm0", "fm1"):
            a, b = ((6, 10), (0, 6))[x[0]]
            ts("tr0 tr1 ts0 ts1 fm gl", n, T.fm[:, 32 * a + 1:32 * b:2], T.tt[:, :].indirect(T.gl[:, a:b]), 0.0, None, OP.is_gt)
        elif n in ("fo0", "fo1"):
            v = (slice(176, 308), slice(0, 176))[x[0]]
            scan("fm1 fbc fbd fb fb1 fb2 fb3" + " fm0" * (1 - x[0]), n, T.fo[:, v], T.fm[:, v], T.fb[:, v])
        elif n in ("fl0", "fl1"):
            a = 66 * (1 - x[0])
            cp("fo%d" % x[0], n, T.fl[:, a:a + 66], T.fo[:, 2 * a + 45:2 * a + 176:2])
        elif n[0:2] == "xh":
            a, m, b, hs = cols()
            times(q, "".join("xp%d%d%d " % (r, h, b) for h in hs), "".join("xh%d%d " % (h, b) for h in hs),
                  T.xh[:, C * b + a:C * b + a + m], XP[:, 64 + 4 * a + b:64 + 4 * a + 4 * m:4], 0.5)
        elif n[0:2] == "lw":
            a, m, b, hs = cols()
            op("v", "cw1 cw2 " + "".join("b3%d " % h for h in hs), "".join("lw%d%d " % (h, b) for h in hs), V.tensor_tensor_scan,
               T.lw[:, C * b + a:C * b + a + m], T.cw[:, C * (2 - b) + a:C * (2 - b) + a + m], T.b3[:, a:a + m], 0.0, OP.max, OP.add)
        elif n == "la":
            times(q, "lw00 lw01 lw10 lw11 fl1", K(n), T.la[:, W], T.lw[:, :].indirect(F(2)))
        elif n == "lb":
            times(q, "laA laB fl1", K(n), T.lb[:, W], T.la[:, :].indirect(F(1)))
        elif n == "lm":
            cp("lbA lbB fl1", K(n), T.lm[:, W], T.lb[:, :].indirect(F(0)))
        elif n in ("ln", "hn"):
            hold(K(n[0] + "m") + "mx", K(n), T[n][:, W], T.mx[:, W], T[n[0] + "m"][:, W])
        elif n in ("vi", "vj"):
            k = "ln" if n == "vi" else "hn"
            cp(K(k), K(n), T[n][:, Q], T[k][:, L])
        elif n in ("i3", "i6"):
            k = "ln" if n == "i3" else "hn"
            ts(K(k) + "cg5", K(n), T[n][:, Q], T[k][:, L], 0.25, cg[:, 5:6], OP.mult, OP.add)
        elif n == "ha":
            act("cw0 cw1 fl0", n, T.ha[:, 0:C], T.cw[:, 0:704].indirect(F(5)))
        elif n == "ha2":
            affine("a", "ha", n, T.ha[:, C:704], T.ha[:, 0:C], 1.0, 1.0)
        elif n == "hc":
            act("ha ha2 fl0", n, T.hc[:, :], T.ha[:, :].indirect(F(4)))
        elif n == "hd":
            act("hc fl0", n, T.hd[:, :], T.hc[:, :].indirect(F(3)))
        elif n == "hm":
            act("hd " + K("i3"), K(n), T.hm[:, W], T.hd[:, :].indirect(T.i3[:, Q]))
        elif n[0:2] == "va":
            k = "vi" if x[0] == 1 else "vj"
            ts(K(k), K(n), VA(x[0]), T[k][:, Q], 3, None, OP.bitwise_and)
        elif n == "ge1":
            gather(10, "b1 fl1", T.b1[:, :].indirect(F(0)))
        elif n[0:2] == "pw":
            times(q, "cb pl%d" % r, n, plane(T.pw, x[0]), T.cb[:, :].indirect(T["pl%d" % r][:, 22 * x[0]:22 * x[0] + 22]), 4.0)
        elif n in ("t0", "t1", "t2", "t3"):
            a, b = x[0] & 1, x[0] >> 1
            times(q, "pw%d pl%d" % (1 - b, r), "s2%d" % x[0], T.s2[:, x[0]:1408:4], plane(T.pw, 1 - b).indirect(T["pl%d" % r][:, 22 * (1 - a):22 * (2 - a)]))
        elif n == "j0":
            cp("pl0", "jf", T.jf[:, 0:44], T.pl0[:, :])
        elif n == "j1":
            tten("jf", "j1", T.jf[:, 44:66], T.jf[:, 0:22], T.jf[:, 22:44], OP.subtract)
        elif n == "j2":
            tten("j1 fm1", "j2", T.jf[:, 66:88], T.jf[:, 44:66], T.fm[:, 1:44:2], OP.mult)
        elif n == "j3":
            k, v, h = listed(10)
            ts(k, "j3", T.jf[:, 88:110], v, -176.0, 176.0, OP.mult, OP.add)
        elif n == "j4":
            tten("jf j3", "j4", T.jf[:, 110:132], T.jf[:, 22:44], T.jf[:, 88:110], OP.add)
        elif n == "j5":
            tten("j2 j4", K("ki0"), KI(0), T.jf[:, 66:88], T.jf[:, 110:132], OP.add)
        elif n == "j6":
            cp(K("ki0"), K("k0"), T.k0[:, :], KI(0))
        elif n == "j7":
            gather(0, "pw0 pw1 " + K("k0"), T.pw[:, :].indirect(T.k0[:, Q]))
        elif n == "p0":
            k, v, h = listed(10)
            tten(k + "fo1", K("ki0"), KI(0), v, T.fo[:, 2 * lo + 1:2 * hi:2], OP.add)
        elif n in ("p2", "p4"):
            k, v, h = listed(x[0] - 2)
            tten(k + K("va%d" % (x[0] - 1)), K("ki%d" % x[0]), KI(x[0]), v, VA(x[0] - 1), OP.add)
        elif n == "k0":
            ts(K("ki0"), K(n), T.k0[:, Q], KI(0), 1.0, None, OP.add)
        elif n in ("k2", "k4"):
            ts(K("ki%d" % x[0]) + "cg6", K(n), T[n][:, Q], KI(x[0]), cg[:, 6:7] if listed(x[0] - 2)[2] else 704.0, None, OP.add)
        elif n in ("g0", "g2", "g4"):
            gather(x[0], S2 + K("k%d" % x[0]), T.s2[:, :].indirect(T["k%d" % x[0]][:, Q]))
        elif n in ("h0", "h2", "h4", "h6", "h8", "he"):
            i = x[0] if x else 10
            if i == 8 and r == 2:
                return
            if listed(i)[2]:
                hold(K("km%d" % i) + "mx", K("ks%d" % i), at(T.kh, i, W), T.mx[:, W], at(T.km, i, W))
            else:
                scan(K("km%d" % i) + "r16", K("ks%d" % i), at(T.ks, i, W), T.r16[:, W], at(T.km, i, W))
        elif n == "k6":
            k, v, h = listed(4)
            ts(k + "cg7", K(n), T.k6[:, Q], v, 0.25, cg[:, 7:8] if h else 176.0, OP.mult, OP.add)
        elif n[0:2] == "gi":
            a, m = PART[x[0]] if len(x) == 2 else (0, C)
            b = x[-1]
            out = T.gs[:, b - 1:4 * m:4] if n in ("gi11", "gi13") else T.gi[:, 4 * a + b:4 * a + 4 * m:4]
            times(q or "a", "xh0%d xh1%d i6A i6B" % (b, b), n if len(x) == 2 else "gi0%d gi1%d" % (b, b), out,
                  plane(T.xh, b).indirect(T.i6[:, a // 16:(a + m) // 16]))
        elif n[0:2] == "zk":
            a, m = PART[1]
            act("xh0%d xh1%d k6B" % (x[0], x[0]), n, T.gs[:, x[0]:4 * m:4], plane(T.xh, x[0]).indirect(T.k6[:, a // 16:(a + m) // 16]))
        elif n == "zs":
            a, m = PART[1]
            scan("alt gi11 gi13 zk1 zk3", "zs z10 z11 z12 z13", T.z[:, 4 * a:4 * a + 4 * m], T.alt[:, 0:4 * m], T.gs[:, 0:4 * m])
        elif n[0] == "z":
            a, m = PART[x[0]]
            b = x[1]
            v = slice(4 * a + b, 4 * a + 4 * m, 4)
            tten("xh0%d xh1%d gi%d%d k6%s" % (b, b, x[0], b, ("A", "B zs")[x[0]]), n, T.z[:, v], plane(T.xh, b).indirect(T.k6[:, a // 16:(a + m) // 16]), T.gi[:, v], OP.add)
        elif n in ("q0", "q1"):
            a, m = PART[x[0]]
            op("v", " ".join("z%d%d" % (x[0], b) for b in range(4)), "zq%d" % x[0], V.quantize_mx, T.zq[:, a:a + m], T.zs[:, a:a + m], T.z[:, 4 * a:4 * a + 4 * m])
            for b in range(4):
                k, o = bank(x[0], b)
                mm("wq wp zq%d" % x[0], k, o, T.wq[:, 128 * b:128 * b + 128], T.wp[:, 128 * b:128 * b + 128], T.zq[:, a:a + m], T.zs[:, a:a + m])
        elif n[0] == "c":
            a, m = PART[x[0]]
            k, i = bank(x[0], x[1])
            times(q, k, "hb%d%d" % (x[0], x[1]), T.hb[:, 4 * a + x[1]:4 * a + 4 * m:4], i, 0.03125)
        elif n in ("h0q", "h1q"):
            a, m = PART[x[0]]
            op("v", " ".join("hb%d%d" % (x[0], b) for b in range(4)), "hq%d%d" % (r, x[0]), V.quantize_mx, T["hq%d" % r][:, a:a + m],
               T["hs%d" % r][:, a:a + m], T.hb[:, 4 * a:4 * a + 4 * m])
            send_part(r, x[0])
        elif n == "en":
            act("b6 k6A k6B", "en", T.en[:, :], T.b6[:, :].indirect(T.k6[:, :]))
        elif n == "dn":
            scan("en m2", "dn", T.dn[:, :], T.m2[:, :], T.en[:, :])
        elif n == "dd":
            tten("dn", "dd", T.dd[:, 0:22], T.dn[:, L], T.dn[:, L], OP.mult)
        elif n == "tf":
            ts("dd cg3 cg4", "tf", T.tf[:, :], T.dd[:, 0:22], cg[:, 3:4], cg[:, 4:5], OP.is_lt, OP.mult)
        elif n == "tg":
            tten("tf cl", "tg", T.tg[:, :], T.tf[:, :], T.cl[:, 0:22], OP.add)
        elif n == "tl":
            cp("tg", "tl", T.tl[:, :], T.tg[:, :])
        elif n in ("u0", "u1"):
            times(q, "pw%d tl" % (1 - x[0]), "uw%d" % x[0], plane(T.uw, x[0]), plane(T.pw, 1 - x[0]).indirect(T.tl[:, :]))
        elif n in ("n0", "n1"):
            b = x[0]
            if b == 0 or r < 2:
                gather(6 + 2 * b, "uw%d tx sn%d" % (b, r), plane(T.uw, b).indirect(sn[:, 22 * b + lo:22 * b + hi]))
        elif n in ("ns0", "ns1"):
            b = x[0]
            if b == 0 or r < 2:
                k, v, h = listed(6 + 2 * b)
                ts(k + "cg7", ("tx", "sn%d" % (r + 1))[b], ns[:, 22 * b:22 * b + 22], v, 0.25, cg[:, 7:8] if h else 176.0, OP.mult, OP.add)
            if b == 1 and r < 2:
                send_list(r + 1)
        elif n == "sf":
            cp("tx sn%d" % r, "sf", T.sf[:, :], sn[:, 0:44])
        elif n == "sd":
            tten("sf", "fb", T.fb[:, 44:88:2], T.sf[:, 22:44], T.sf[:, 0:22], OP.subtract)
        elif n == "fb0":
            times(q, "sf", "fb1", T.fb[:, 45:88:2], T.sf[:, 0:22])
            times(q, "sf", "fb1", T.fb[:, 133:176:2], T.sf[:, 0:22])
            affine(q, "fb", "fb1", T.fb[:, 132:176:2], T.fb[:, 44:88:2], 1.0, 352.0)
        elif n == "fb1":
            times(q, "fb fb1", "fb2", T.fb[:, 88:132], T.fb[:, 44:88])
            times(q, "fb fb1", "fb2", T.fb[:, 176:220], T.fb[:, 44:88])
        elif n == "fb2":
            times(q, "fb1", "fb3", T.fb[:, 220:264], T.fb[:, 132:176])
            times(q, "fb1", "fb3", T.fb[:, 264:308], T.fb[:, 132:176])
        elif n == "so":
            for b in range(2):
                act("uw%d sn2" % b, "tw iw", plane(T.tw, b), plane(T.uw, b).indirect(T.sn2[:, 22 * b:22 * b + 22]), AF.Identity, scale=0.25, bias=176.0)
            dma("s", "d_so", "tw", "so", T.so[:, :], T.tw[0:128:16, :])
        elif n[0] == "e":
            a, m = PART[x[0]]
            b = x[1]
            k, ps = bank(x[0], b)
            mm("eq%d dq%d%d" % (b, r - 1, x[0]), k, ps, T.eq[:, 128 * b:128 * b + 128], T.es[:, 128 * b:128 * b + 128],
               T["dq%d" % (r - 1)][:, a:a + m], T["ds%d" % (r - 1)][:, a:a + m])
        elif n[0] == "d":
            a, m = PART[x[0]]
            k, ps = bank(x[0], x[1])
            times(q, k, "dw%d%d" % (x[0], x[1]), T.dw[:, C * x[1] + a:C * x[1] + a + m], ps)
        elif n == "xc":
            a, m = XH[1]
            cp(xp(r - 1, 1), n, T.gx[:, 1:4 * m:2], T["xp%d" % (r - 1)][:, 65 + 4 * a:64 + 4 * a + 4 * m:2])
        elif n[0:2] == "xk":
            a, m = XH[1]
            act("tx dw0%d dw1%d" % (x[0], x[0]), n, T.gx[:, x[0] - 1:4 * m:4], plane(T.dw, x[0]).indirect(sn[:, a // 16:(a + m) // 16]))
        elif n == "xs":
            a, m = XH[1]
            scan("alt xc xk1 xk3", xp(r, 1) + "xs", XP[:, 64 + 4 * a:64 + 4 * a + 4 * m], T.alt[:, 0:4 * m], T.gx[:, :])
        elif n[0] == "x":
            a, m, b, hs = cols()
            v = slice(64 + 4 * a + b, 64 + 4 * a + 4 * m, 4)
            tten("tx dw0%d dw1%d " % (b, b) + "xs " * (r == 3 and 1 in hs) + "".join("xp%d%d%d " % (r - 1, h, b) for h in hs), "".join("xp%d%d%d " % (r, h, b) for h in hs),
                 XP[:, v], plane(T.dw, b).indirect(sn[:, a // 16:(a + m) // 16]), T["xp%d" % (r - 1)][:, v], OP.add)
        elif n[0:2] == "qx":
            h = x[0]
            a, m = 16 + XH[h][0], XH[h][1]
            if r < 3:
                a, m = a - 16 * (1 - h), m + 16
            op("v", xp(r, h) + "pad%d" % r, "xq%d" % h, V.quantize_mx, T.xq[:, a:a + m], T.xs[:, a:a + m], XP[:, 4 * a:4 * a + 4 * m])
        elif n in ("y0", "y1"):
            a, m = XH[x[0]]
            v = slice(16 + a, 16 + a + m)
            mm("vq xq%d" % x[0], "pa%d" % x[0], T.pa[:, 512 * x[0]:512 * x[0] + m], T.vq[:, :], T.vs[:, :], T.xq[:, v], T.xs[:, v])
        elif n in ("oc0", "oc1"):
            a, m = XH[x[0]]
            dma("s", "d_oc", "xq%d" % x[0], n, T.oc[:, 4 * a:4 * a + 4 * m], T.xq[:, 16 + a:16 + a + m].bitcast(dt.uint8))
        elif n == "osc":
            for k in range(4):
                dma("sa"[k % 2], "d_oc", "xq0 xq1", "osc%d" % k, T.osc[4 * k:4 * k + 4, :], T.xs[32 * k:32 * k + 4, 16:368])
        elif n in ("yc0", "yc1"):
            h = x[0]
            a, m = XH[h]
            times(q, "pa%d" % h, "yb%d" % h, T.yb[:, a:a + m], T.pa[:, 512 * h:512 * h + m])
            dma("sa"[h], "d_y", "yb%d" % h, "y%d" % h, T.y[:, a:a + m], T.yb[:, a:a + m])

    for r, names in ORDER:
        for name in names.split():
            step(r, name)
    total["ls"] = sent[0]
    for s in total:
        g.wait_ge(T.sem[s], total[s])
